import numpy as np
import ml_dtypes


def mxq(x, axis, fmt="e4m3"):
    dtype, down = {"e4m3": (ml_dtypes.float8_e4m3fn, 7), "e5m2": (ml_dtypes.float8_e5m2, 14)}[fmt]
    v = np.moveaxis(np.asarray(x, np.float32).astype(ml_dtypes.bfloat16).astype(np.float64), axis, -1)
    blocks = v.reshape(v.shape[:-1] + (-1, 32))
    amax = np.abs(blocks).max(-1, keepdims=True)
    byte = np.maximum(np.where(amax > 0, np.frexp(amax)[1] - 1 + 127, 0) - down, 1)
    scale = np.exp2(byte - 127.0)
    codes = (blocks / scale).astype(np.float32).astype(dtype).astype(np.float64)
    return np.moveaxis((codes * scale).reshape(v.shape), -1, axis)


WIDE = False


def mx_kscale(k):
    if not WIDE:
        return np.ones(k)
    levels = np.array([10, -10, 5, -5, 0])
    if k % 512:
        return np.exp2(np.random.permutation(np.resize(levels, k // 32))).repeat(32)
    a = np.empty((k // 512, 16))
    for p in range(k // 512):
        a[p, :8] = np.random.permutation(np.resize(levels, 8))
        for g in range(8):
            far = levels[np.abs(levels - a[p, g]) >= 10]
            a[p, g + 8] = far[np.random.randint(len(far))]
    return np.exp2(a.ravel()).repeat(32)


def f64(x):
    return np.asarray(x).astype(np.float64)


def striped(idx):
    return np.tile(idx.reshape(-1, 16).T, (8, 1)).astype(np.uint16)


def unstriped(offs):
    return offs[:16].T.reshape(-1).astype(np.int64)


E2M1 = np.array([0.0, 0.5, 1.0, 1.5, 2.0, 3.0, 4.0, 6.0, -0.0, -0.5, -1.0, -1.5, -2.0, -3.0, -4.0, -6.0])


def pack_weight(w, fmt):
    k, n = w.shape
    w = f64(np.asarray(w, np.float32).astype(ml_dtypes.bfloat16)).reshape(k // 32, 32, n)
    amax = np.abs(w).max(1)
    if fmt == "e4m3":
        byte = np.frexp(amax)[1] - 1 + 127 - 7
    else:
        mant, ex = np.frexp(amax / 6.0)
        byte = np.where(mant > 0.5, ex, ex - 1) + 127
    byte = np.clip(np.where(amax > 0, byte, 1), 1, 254)
    scaled = (w * np.exp2(127.0 - byte)[:, None, :]).reshape(k, n).astype(np.float32)
    by_word = np.ascontiguousarray(scaled.reshape(k // 512, 128, 4, n).transpose(0, 1, 3, 2))
    if fmt == "e4m3":
        words = by_word.astype(ml_dtypes.float8_e4m3fn).view(np.uint8)
    else:
        c = by_word.astype(ml_dtypes.float4_e2m1fn).view(np.uint8) & 0xF
        words = (c[..., 0::2] | (c[..., 1::2] << 4)).reshape(k // 512, 128, 2 * n)
    return np.ascontiguousarray(words), np.ascontiguousarray(byte.astype(np.uint8).reshape(k // 512, 16, n))


def unpack_weight(words, scales, fmt):
    g, _, n = scales.shape
    words = np.ascontiguousarray(words).reshape(g, 128, n, -1)
    if fmt == "e4m3":
        vals = words.view(ml_dtypes.float8_e4m3fn).astype(np.float64)
    else:
        nib = np.empty((g, 128, n, 4), np.uint8)
        nib[..., 0::2] = words & 0xF
        nib[..., 1::2] = words >> 4
        vals = E2M1[nib]
    vals = vals * np.repeat(np.exp2(scales.astype(np.float64) - 127.0), 8, axis=1)[..., None]
    return vals.transpose(0, 1, 3, 2).reshape(g * 512, n)


def gelu(v):
    return 0.5 * v * (1.0 + np.tanh(np.sqrt(2.0 / np.pi) * (v + 0.044715 * v**3)))


K, T, S, H, N = 512, 4096, 1024, 1024, 768

def setup_inputs():
    n = np.random.standard_normal
    s = mx_kscale(K)[:, None]
    u = mx_kscale(H)[:, None]
    tab_words, tab_scales = pack_weight(n((K, T)) * s, "e4m3")
    w2_words, w2_scales = pack_weight(n((K, H)) / np.sqrt(K) / s, "e2m1")
    w4_words, w4_scales = pack_weight(n((H, N)) / np.sqrt(H) / u, "e4m3")
    return {
        "tab_words": tab_words, "tab_scales": tab_scales,
        "offs": striped(np.random.permutation(T)[:S]),
        "w1": (n((K, H)) / np.sqrt(K) / s * u.T).astype(np.float32),
        "w2_words": w2_words, "w2_scales": w2_scales,
        "w3": (n((K, H)) / np.sqrt(K) / s).astype(np.float32),
        "w4_words": w4_words, "w4_scales": w4_scales,
        "offs2": striped(np.random.permutation(S)),
        "wgo": np.exp(0.3 * n((128, S))).astype(np.float32),
        "x0": n((N, S)).astype(np.float32),
    }

def reference(tab_words, tab_scales, offs, w1, w2_words, w2_scales, w3, w4_words, w4_scales, offs2, wgo, x0):
    v = unpack_weight(tab_words, tab_scales, "e4m3")[:, unstriped(offs)]
    a = mxq(f64(w1), 0, "e4m3").T @ v
    b = unpack_weight(w2_words, w2_scales, "e2m1").T @ v
    c = mxq(f64(w3), 0, "e4m3").T @ v
    h = a * b * c
    y = unpack_weight(w4_words, w4_scales, "e4m3").T @ mxq(h, 0, "e4m3")
    page = np.zeros((N, S))
    page[:, unstriped(offs2)] = np.tile(f64(wgo), (N // 128, 1)) * y
    x = f64(x0)
    return x + x * page

@@ -1,0 +1,266 @@
+from contextlib import ExitStack
+
+import concourse.mybir as mybir
+
+K, T, S, H, N = 512, 4096, 1024, 1024, 768
+FLOPS = 2 * (3 * K * H * S + H * N * S)
+
+F32 = mybir.dt.float32
+BF16 = mybir.dt.bfloat16
+U32 = mybir.dt.uint32
+I32 = mybir.dt.int32
+U16 = mybir.dt.uint16
+U8 = mybir.dt.uint8
+FP8X4 = mybir.dt.float8_e4m3fn_x4
+FP4X4 = mybir.dt.float4_e2m1fn_x4
+MULT = mybir.AluOpType.mult
+ADD = mybir.AluOpType.add
+COPY = mybir.ActivationFunctionType.Copy
+
+P = 128
+PACK = 4
+PASS = P * PACK
+PASSES = H // PASS
+HALF = S // 2
+CHUNK = 128
+CHUNKS = HALF // CHUNK
+NT = N // P
+
+
+def tile_list_marker_triple_interaction_kernel(
+    tc, tab_words, tab_scales, offs, w1, w2_words, w2_scales, w3, w4_words, w4_scales, offs2, wgo, x0, out
+):
+    nc = tc.nc
+    with ExitStack() as ctx:
+        held = ctx.enter_context(tc.tile_pool(name="held", bufs=1))
+        work = ctx.enter_context(tc.tile_pool(name="work", bufs=1))
+        shared = ctx.enter_context(tc.tile_pool(name="shared", bufs=1))
+        psum = ctx.enter_context(tc.psum_pool(name="psum", bufs=1))
+
+        def load_scale_rows(queue, plane, rows):
+            for q in range(4):
+                queue.dma_start(
+                    out=plane[32 * q : 32 * q + 4].bitcast(I32),
+                    in_=rows[:, 4 * q : 4 * q + 4, :].rearrange("a r c -> r a c").bitcast(I32),
+                )
+
+        idx = held.tile([P, S // 16], U16, name="idx")
+        idx2 = held.tile([P, S // 16], U16, name="idx2")
+        nc.sync.dma_start(idx[:], offs)
+        nc.sync.dma_start(idx2[:], offs2)
+        REGION = PACK * PASS * 4
+        regions = ctx.enter_context(tc.tile_pool(name="regions", bufs=1))
+
+        tab_plane = shared.tile([P, 1, T], U8, name="tab_plane", tag="plane", align_bytes=64, offset=6 * S * 4)
+        w2_plane_raw = held.tile([P, 1, H], U8, name="w2_plane_raw", align_bytes=64)
+        nc.vector.memset(tab_plane[:].bitcast(I32), 0)
+        nc.gpsimd.memset(w2_plane_raw[:].bitcast(I32), 0)
+
+        w2_raw = regions.tile([P, H], U16, name="w2_raw", align_bytes=64, offset=3 * REGION)
+        nc.sync.dma_start(out=w2_raw[:].bitcast(I32), in_=w2_words[0].bitcast(I32))
+        load_scale_rows(nc.sync, w2_plane_raw, w2_scales)
+        load_scale_rows(nc.sync, tab_plane, tab_scales)
+        tab = held.tile([P, T], U32, name="tab", align_bytes=64)
+        nc.sync.dma_start(out=tab[:].bitcast(I32), in_=tab_words[0].rearrange("p t i -> p (t i)").bitcast(I32))
+
+        raw = {}
+
+        def load_weight(name, w, a, region):
+            raw[name, a] = regions.tile([P, PACK, PASS], F32, name="raw_%d" % region, align_bytes=64, offset=region * REGION)
+            nc.sync.dma_start(
+                out=raw[name, a][:], in_=w[:, a * PASS : (a + 1) * PASS].rearrange("(p i) c -> p i c", i=PACK)
+            )
+
+        load_weight("w1", w1, 0, 0)
+        load_weight("w3", w3, 0, 1)
+        load_weight("w1", w1, 1, 2)
+
+        w2 = held.tile([P, H], U16, name="w2", align_bytes=64)
+        w2_plane = held.tile([P, H], U8, name="w2_plane", align_bytes=64)
+        nc.vector.tensor_copy(
+            out=w2[:].rearrange("p (a t m) -> p a t m", a=PASSES, t=PACK),
+            in_=w2_raw[:].rearrange("p (a m t) -> p a t m", a=PASSES, t=PACK),
+        )
+        nc.vector.tensor_copy(
+            out=w2_plane[:].rearrange("p (a t m) -> p a t m", a=PASSES, t=PACK),
+            in_=w2_plane_raw[:, 0, :].rearrange("p (a m t) -> p a t m", a=PASSES, t=PACK),
+        )
+
+        load_weight("w3", w3, 1, 3)
+        v = held.tile([P, S], U32, name="v", align_bytes=64)
+        v_plane = held.tile([P, S], U8, name="v_plane", align_bytes=64)
+        nc.vector.tensor_copy(out=v_plane[:], in_=tab_plane[:, 0, :].indirect(idx[:]))
+        nc.vector.tensor_copy(out=v[:], in_=tab[:].indirect(idx[:]))
+
+        w4_plane = shared.tile([P, PASSES, N], U8, name="w4_plane", align_bytes=64, offset=6 * S * 4)
+        nc.gpsimd.memset(w4_plane[:].bitcast(I32), 0)
+        load_scale_rows(nc.sync, w4_plane, w4_scales)
+        codes, planes = {}, {}
+
+        def quantise_weight(name, a, shares):
+            grouped = work.tile([P, PACK, P, PACK], BF16, name="grouped", tag="grouped", bufs=2, align_bytes=64)
+            src = raw[name, a][:].rearrange("p i (m t) -> p m t i", t=PACK)
+            dst = grouped[:].rearrange("p t m i -> p m t i")
+            for engine, m0, m1 in shares:
+                if engine == "v":
+                    nc.vector.tensor_copy(out=dst[:, m0:m1], in_=src[:, m0:m1])
+                elif engine == "s":
+                    nc.scalar.copy(out=dst[:, m0:m1], in_=src[:, m0:m1])
+                else:
+                    nc.gpsimd.tensor_scalar(dst[:, m0:m1], src[:, m0:m1], 1.0, 0.0, MULT, ADD)
+            codes[name, a] = held.tile([P, PASS], U32, name="codes_%s_%d" % (name, a), align_bytes=64)
+            planes[name, a] = held.tile([P, PASS], U8, name="plane_%s_%d" % (name, a), align_bytes=64)
+            nc.vector.quantize_mx(
+                out=codes[name, a][:].bitcast(FP8X4),
+                scales=planes[name, a][:],
+                in_=grouped[:].rearrange("p t m i -> p (t m i)"),
+            )
+
+        def project(name, a, j0, tag, bufs):
+            bank = psum.tile([P, PACK, CHUNK], F32, name="bank_" + tag, tag=tag, bufs=bufs)
+            for t in range(PACK):
+                if name == "w2":
+                    c0 = a * PASS + t * P
+                    lhsT, lhsT_scale = w2[:, c0 : c0 + P].bitcast(FP4X4), w2_plane[:, c0 : c0 + P]
+                else:
+                    lhsT = codes[name, a][:, t * P : (t + 1) * P].bitcast(FP8X4)
+                    lhsT_scale = planes[name, a][:, t * P : (t + 1) * P]
+                nc.tensor.matmul_mx(
+                    out=bank[:, t, :], lhsT=lhsT, lhsT_scale=lhsT_scale,
+                    rhs=v[:, j0 : j0 + CHUNK].bitcast(FP8X4), rhs_scale=v_plane[:, j0 : j0 + CHUNK],
+                    start=True, stop=True,
+                )
+            return bank[:].rearrange("p t j -> p j t")
+
+        def evacuate(bank, tag, bufs):
+            sb = work.tile([P, CHUNK, PACK], F32, name=tag, tag=tag, bufs=bufs)
+            nc.scalar.copy(out=sb[:], in_=bank)
+            return sb
+
+        hb, ab = {}, {}
+        PAGE_BYTES = S * 4
+        for half in range(2):
+            for a in range(PASSES):
+                if (half, a) == (1, 1):
+                    hb[half, a] = shared.tile([P, HALF, PACK], BF16, name="hb_last", offset=5 * PAGE_BYTES - PAGE_BYTES // 2, align_bytes=64)
+                elif (half, a) == (0, 0):
+                    hb[half, a] = regions.tile([P, HALF, PACK], BF16, name="hb_first", offset=4 * REGION, align_bytes=64)
+                else:
+                    hb[half, a] = held.tile([P, HALF, PACK], BF16, name="hb_%d_%d" % (half, a), align_bytes=64)
+
+        def first_product(a, q, engine):
+            j0 = q * CHUNK
+            if engine == "v":
+                a_sb = evacuate(project("w1", a, j0, "ay", 3), "av", 4)
+                b = project("w2", a, j0, "bc", 3)
+                ab[a, q] = work.tile([P, CHUNK, PACK], F32, name="abv", tag="abv", bufs=8)
+                nc.vector.tensor_tensor(ab[a, q][:], b, a_sb[:], MULT)
+            else:
+                a_sb = evacuate(project("w1", a, j0, "g", 2), "ag", 5)
+                b_sb = evacuate(project("w2", a, j0, "g", 2), "bg", 5)
+                ab[a, q] = work.tile([P, CHUNK, PACK], F32, name="abg", tag="abg", bufs=4)
+                nc.gpsimd.tensor_tensor(ab[a, q][:], b_sb[:], a_sb[:], MULT)
+
+        def second_product(a, q, engine):
+            j0 = q * CHUNK
+            dst = hb[q // CHUNKS, a][:, (q % CHUNKS) * CHUNK : (q % CHUNKS + 1) * CHUNK, :]
+            if engine == "v":
+                nc.vector.tensor_tensor(dst, project("w3", a, j0, "bc", 3), ab[a, q][:], MULT)
+            else:
+                c_sb = evacuate(project("w3", a, j0, "g", 2), "cg", 5)
+                nc.gpsimd.tensor_tensor(dst, c_sb[:], ab[a, q][:], MULT)
+
+        hq, hs = {}, {}
+
+        def quantise_h(half, a):
+            if half == 0:
+                where = (PAGE_BYTES, 3 * PAGE_BYTES - PAGE_BYTES // 4)[a]
+                hq[half, a] = shared.tile([P, HALF], U32, name="hq_%d_%d" % (half, a), align_bytes=64, offset=where)
+            else:
+                hq[half, a] = held.tile([P, HALF], U32, name="hq_%d_%d" % (half, a), align_bytes=64)
+            hs[half, a] = held.tile([P, HALF], U8, name="hs_%d_%d" % (half, a), align_bytes=64)
+            nc.vector.quantize_mx(
+                out=hq[half, a][:].bitcast(FP8X4), scales=hs[half, a][:],
+                in_=hb[half, a][:].rearrange("p j t -> p (j t)"),
+            )
+
+        yw = {}
+
+        def scores(half, n, engine):
+            bank = psum.tile([P, HALF], F32, name="bank_ay", tag="ay", bufs=3)
+            cols = slice(n * P, (n + 1) * P)
+            for a in reversed(range(PASSES)):
+                nc.tensor.matmul_mx(
+                    out=bank[:], lhsT=w4[:, a, cols].bitcast(FP8X4), lhsT_scale=w4_plane[:, a, cols],
+                    rhs=hq[half, a][:].bitcast(FP8X4), rhs_scale=hs[half, a][:],
+                    start=(a == PASSES - 1), stop=(a == 0),
+                )
+            yw[half, n] = work.tile([P, HALF], F32, name="yw", tag="yw", bufs=8)
+            g = gain[:, half * HALF : (half + 1) * HALF]
+            if engine == "v":
+                nc.vector.tensor_tensor(yw[half, n][:], bank[:], g, MULT)
+            else:
+                y_sb = work.tile([P, HALF], F32, name="y_sb", tag="y_sb", bufs=3)
+                nc.scalar.copy(out=y_sb[:], in_=bank[:])
+                nc.gpsimd.tensor_tensor(yw[half, n][:], y_sb[:], g, MULT)
+
+        page = {}
+
+        def place(half, n):
+            if half == 0:
+                page[n] = shared.tile([P, S], F32, name="page_%d" % n, offset=n * PAGE_BYTES, align_bytes=64)
+            cols = slice(half * HALF // 16, (half + 1) * HALF // 16)
+            nc.vector.tensor_copy(out=page[n][:].indirect(idx2[:, cols]), in_=yw[half, n][:])
+
+        J0 = ["vvvv","vvvv","vvvv","vvvv"]
+        J1 = ["gggg","gggg","gggg","gggg"]
+        quantise_weight("w1", 0, [("v", 0, P)])
+        for q in range(CHUNKS):
+            first_product(0, q, J0[0][q])
+        w4 = regions.tile([P, PASSES, N], U32, name="w4", align_bytes=64, offset=0)
+        nc.sync.dma_start(out=w4[:].bitcast(I32), in_=w4_words.rearrange("a p e i -> p a (e i)").bitcast(I32))
+        quantise_weight("w3", 0, [("g", 0, 64), ("s", 64, P)])
+        gain = regions.tile([P, S], F32, name="gain", align_bytes=64, offset=REGION)
+        nc.sync.dma_start(out=gain[:], in_=wgo)
+        quantise_weight("w1", 1, [("g", 0, 64), ("s", 64, P)])
+        quantise_weight("w3", 1, [("g", 0, 64), ("s", 64, P)])
+        for q in range(CHUNKS):
+            second_product(0, q, J0[1][q])
+        for q in range(CHUNKS):
+            first_product(1, q, J0[2][q])
+        quantise_h(0, 0)
+        for q in range(CHUNKS):
+            second_product(1, q, J0[3][q])
+        quantise_h(0, 1)
+
+        x = {}
+        for n in range(NT):
+            x[n] = regions.tile([P, S], F32, name="x_%d" % n, align_bytes=64, offset=(3 + n) * PAGE_BYTES)
+            nc.sync.dma_start(out=x[n][:], in_=x0[n * P : (n + 1) * P, :])
+
+        for n in range(NT):
+            scores(0, n, "vvvvvv"[n])
+        for a in range(PASSES):
+            for q in range(CHUNKS, 2 * CHUNKS):
+                first_product(a, q, J1[2 * a][q - CHUNKS])
+                second_product(a, q, J1[2 * a + 1][q - CHUNKS])
+            quantise_h(1, a)
+        for n in range(NT):
+            place(0, n)
+        for n in range(NT):
+            scores(1, n, "gggggg"[n])
+        for n in range(NT):
+            place(1, n)
+        for n in range(NT):
+            res = work.tile([P, S], F32, name="res", tag="res", bufs=3)
+            xn = x[n][:]
+            rows = slice(n * P, (n + 1) * P)
+            if "gggggv"[n] == "v":
+                for u in range(2):
+                    cols = slice(u * HALF, (u + 1) * HALF)
+                    nc.vector.scalar_tensor_tensor(res[:, cols], page[n][:, cols], 1.0, xn[:, cols], ADD, MULT)
+                    nc.sync.dma_start(out=out[rows, cols], in_=res[:, cols])
+            else:
+                nc.scalar.activation(res[:], page[n][:], COPY, bias=1.0, scale=1.0)
+                nc.gpsimd.tensor_tensor(res[:], res[:], xn, MULT)
+                nc.sync.dma_start(out=out[rows, :], in_=res[:])

@@ -35,6 +35,7 @@ def tile_list_marker_triple_interaction_kernel(
         held = ctx.enter_context(tc.tile_pool(name="held", bufs=1))
         work = ctx.enter_context(tc.tile_pool(name="work", bufs=1))
         shared = ctx.enter_context(tc.tile_pool(name="shared", bufs=1))
+        late = ctx.enter_context(tc.tile_pool(name="late", bufs=1))
         psum = ctx.enter_context(tc.psum_pool(name="psum", bufs=1))
 
         def load_scale_rows(queue, plane, rows):
@@ -59,9 +60,13 @@ def tile_list_marker_triple_interaction_kernel(
         w2_raw = regions.tile([P, H], U16, name="w2_raw", align_bytes=64, offset=3 * REGION)
         nc.sync.dma_start(out=w2_raw[:].bitcast(I32), in_=w2_words[0].bitcast(I32))
         load_scale_rows(nc.sync, w2_plane_raw, w2_scales)
-        load_scale_rows(nc.sync, tab_plane, tab_scales)
         tab = held.tile([P, T], U32, name="tab", align_bytes=64)
-        nc.sync.dma_start(out=tab[:].bitcast(I32), in_=tab_words[0].rearrange("p t i -> p (t i)").bitcast(I32))
+        tab_rows = tab_words[0].rearrange("p t i -> p (t i)").bitcast(I32)
+        for u in range(2):
+            cols = slice(u * T // 2, (u + 1) * T // 2)
+            nc.sync.dma_start(out=tab[:, cols].bitcast(I32), in_=tab_rows[:, cols])
+            if u == 0:
+                load_scale_rows(nc.sync, tab_plane, tab_scales)
 
         raw = {}
 
@@ -98,7 +103,7 @@ def tile_list_marker_triple_interaction_kernel(
         codes, planes = {}, {}
 
         def quantise_weight(name, a, shares):
-            grouped = work.tile([P, PACK, P, PACK], BF16, name="grouped", tag="grouped", bufs=2, align_bytes=64)
+            grouped = regions.tile([P, PACK, P, PACK], BF16, name="grouped", tag="grouped", bufs=2, align_bytes=64, offset=9 * S * 4)
             src = raw[name, a][:].rearrange("p i (m t) -> p m t i", t=PACK)
             dst = grouped[:].rearrange("p t m i -> p m t i")
             for engine, m0, m1 in shares:
@@ -132,8 +137,11 @@ def tile_list_marker_triple_interaction_kernel(
                 )
             return bank[:].rearrange("p t j -> p j t")
 
-        def evacuate(bank, tag, bufs):
-            sb = work.tile([P, CHUNK, PACK], F32, name=tag, tag=tag, bufs=bufs)
+        def evacuate(bank, tag, bufs, offset=None):
+            if offset is None:
+                sb = work.tile([P, CHUNK, PACK], F32, name=tag, tag=tag, bufs=bufs)
+            else:
+                sb = regions.tile([P, CHUNK, PACK], F32, name=tag, tag=tag, bufs=bufs, align_bytes=64, offset=offset)
             nc.scalar.copy(out=sb[:], in_=bank)
             return sb
 
@@ -142,24 +150,34 @@ def tile_list_marker_triple_interaction_kernel(
         for half in range(2):
             for a in range(PASSES):
                 if (half, a) == (1, 1):
-                    hb[half, a] = shared.tile([P, HALF, PACK], BF16, name="hb_last", offset=5 * PAGE_BYTES - PAGE_BYTES // 2, align_bytes=64)
+                    hb[half, a] = shared.tile([P, HALF, PACK], BF16, name="hb_last", offset=5 * PAGE_BYTES, align_bytes=64)
                 elif (half, a) == (0, 0):
                     hb[half, a] = regions.tile([P, HALF, PACK], BF16, name="hb_first", offset=4 * REGION, align_bytes=64)
                 else:
                     hb[half, a] = held.tile([P, HALF, PACK], BF16, name="hb_%d_%d" % (half, a), align_bytes=64)
 
+        b_sb = {}
+
+        def project_b(a, q):
+            if q < CHUNKS:
+                b_sb[a, q] = evacuate(project("w2", a, q * CHUNK, "ay", 3), "b0", 8)
+            else:
+                b_sb[a, q] = evacuate(project("w2", a, q * CHUNK, "g", 2), "bg", 2, 3 * REGION)
+
         def first_product(a, q, engine):
             j0 = q * CHUNK
-            if engine == "v":
-                a_sb = evacuate(project("w1", a, j0, "ay", 3), "av", 4)
-                b = project("w2", a, j0, "bc", 3)
+            if q < CHUNKS:
                 ab[a, q] = work.tile([P, CHUNK, PACK], F32, name="abv", tag="abv", bufs=8)
-                nc.vector.tensor_tensor(ab[a, q][:], b, a_sb[:], MULT)
             else:
-                a_sb = evacuate(project("w1", a, j0, "g", 2), "ag", 5)
-                b_sb = evacuate(project("w2", a, j0, "g", 2), "bg", 5)
-                ab[a, q] = work.tile([P, CHUNK, PACK], F32, name="abg", tag="abg", bufs=4)
-                nc.gpsimd.tensor_tensor(ab[a, q][:], b_sb[:], a_sb[:], MULT)
+                ab[a, q] = work.tile([P, CHUNK, PACK], F32, name="abg", tag="abg", bufs=3)
+            if engine == "v":
+                nc.vector.tensor_tensor(ab[a, q][:], project("w1", a, j0, "bc", 3), b_sb[a, q][:], MULT)
+            else:
+                if q < CHUNKS:
+                    a_sb = evacuate(project("w1", a, j0, "bc", 3), "jg", 2)
+                else:
+                    a_sb = evacuate(project("w1", a, j0, "g", 2), "ag", 2, 3 * REGION + REGION // 2)
+                nc.gpsimd.tensor_tensor(ab[a, q][:], a_sb[:], b_sb[a, q][:], MULT)
 
         def second_product(a, q, engine):
             j0 = q * CHUNK
@@ -167,17 +185,16 @@ def tile_list_marker_triple_interaction_kernel(
             if engine == "v":
                 nc.vector.tensor_tensor(dst, project("w3", a, j0, "bc", 3), ab[a, q][:], MULT)
             else:
-                c_sb = evacuate(project("w3", a, j0, "g", 2), "cg", 5)
+                if q < CHUNKS:
+                    c_sb = evacuate(project("w3", a, j0, "bc", 3), "jg", 2)
+                else:
+                    c_sb = evacuate(project("w3", a, j0, "g", 2), "cg", 2)
                 nc.gpsimd.tensor_tensor(dst, c_sb[:], ab[a, q][:], MULT)
 
         hq, hs = {}, {}
 
         def quantise_h(half, a):
-            if half == 0:
-                where = (PAGE_BYTES, 3 * PAGE_BYTES - PAGE_BYTES // 4)[a]
-                hq[half, a] = shared.tile([P, HALF], U32, name="hq_%d_%d" % (half, a), align_bytes=64, offset=where)
-            else:
-                hq[half, a] = held.tile([P, HALF], U32, name="hq_%d_%d" % (half, a), align_bytes=64)
+            hq[half, a] = held.tile([P, HALF], U32, name="hq_%d_%d" % (half, a), align_bytes=64)
             hs[half, a] = held.tile([P, HALF], U8, name="hs_%d_%d" % (half, a), align_bytes=64)
             nc.vector.quantize_mx(
                 out=hq[half, a][:].bitcast(FP8X4), scales=hs[half, a][:],
@@ -187,7 +204,8 @@ def tile_list_marker_triple_interaction_kernel(
         yw = {}
 
         def scores(half, n, engine):
-            bank = psum.tile([P, HALF], F32, name="bank_ay", tag="ay", bufs=3)
+            tag = "ay" if n < NT // 2 else "bc"
+            bank = psum.tile([P, HALF], F32, name="bank_" + tag, tag=tag, bufs=3)
             cols = slice(n * P, (n + 1) * P)
             for a in reversed(range(PASSES)):
                 nc.tensor.matmul_mx(
@@ -200,7 +218,7 @@ def tile_list_marker_triple_interaction_kernel(
             if engine == "v":
                 nc.vector.tensor_tensor(yw[half, n][:], bank[:], g, MULT)
             else:
-                y_sb = work.tile([P, HALF], F32, name="y_sb", tag="y_sb", bufs=3)
+                y_sb = late.tile([P, HALF], F32, name="y_sb_%d_%d" % (half, n), offset=(n - 1) * HALF * 4)
                 nc.scalar.copy(out=y_sb[:], in_=bank[:])
                 nc.gpsimd.tensor_tensor(yw[half, n][:], y_sb[:], g, MULT)
 
@@ -212,55 +230,106 @@ def tile_list_marker_triple_interaction_kernel(
             cols = slice(half * HALF // 16, (half + 1) * HALF // 16)
             nc.vector.tensor_copy(out=page[n][:].indirect(idx2[:, cols]), in_=yw[half, n][:])
 
-        J0 = ["vvvv","vvvv","vvvv","vvvv"]
-        J1 = ["gggg","gggg","gggg","gggg"]
         quantise_weight("w1", 0, [("v", 0, P)])
-        for q in range(CHUNKS):
-            first_product(0, q, J0[0][q])
         w4 = regions.tile([P, PASSES, N], U32, name="w4", align_bytes=64, offset=0)
         nc.sync.dma_start(out=w4[:].bitcast(I32), in_=w4_words.rearrange("a p e i -> p a (e i)").bitcast(I32))
-        quantise_weight("w3", 0, [("g", 0, 64), ("s", 64, P)])
+        quantise_weight("w3", 0, [("v", 0, 48), ("s", 48, 128)])
         gain = regions.tile([P, S], F32, name="gain", align_bytes=64, offset=REGION)
         nc.sync.dma_start(out=gain[:], in_=wgo)
-        quantise_weight("w1", 1, [("g", 0, 64), ("s", 64, P)])
-        quantise_weight("w3", 1, [("g", 0, 64), ("s", 64, P)])
-        for q in range(CHUNKS):
-            second_product(0, q, J0[1][q])
-        for q in range(CHUNKS):
-            first_product(1, q, J0[2][q])
+        quantise_weight("w1", 1, [("v", 0, 48), ("s", 48, 128)])
+        quantise_weight("w3", 1, [("v", 0, 64), ("s", 64, 128)])
+        project_b(0, 0)
+        project_b(0, 1)
+        project_b(0, 2)
+        project_b(0, 3)
+        first_product(0, 0, "v")
+        first_product(0, 1, "v")
+        first_product(0, 2, "v")
+        first_product(0, 3, "v")
+        second_product(0, 3, "g")
+        second_product(0, 0, "v")
+        second_product(0, 1, "v")
+        second_product(0, 2, "v")
+        project_b(1, 0)
+        project_b(1, 1)
+        project_b(1, 2)
+        project_b(1, 3)
+        first_product(1, 3, "g")
+        first_product(1, 0, "v")
+        first_product(1, 1, "v")
+        first_product(1, 2, "v")
         quantise_h(0, 0)
-        for q in range(CHUNKS):
-            second_product(1, q, J0[3][q])
+        second_product(1, 3, "g")
+        second_product(1, 0, "v")
+        second_product(1, 1, "v")
+        second_product(1, 2, "v")
+        project_b(0, 4)
+        first_product(0, 4, "g")
+        project_b(0, 5)
+        first_product(0, 5, "g")
+        second_product(0, 4, "g")
+        project_b(0, 6)
+        first_product(0, 6, "g")
         quantise_h(0, 1)
-
         x = {}
         for n in range(NT):
-            x[n] = regions.tile([P, S], F32, name="x_%d" % n, align_bytes=64, offset=(3 + n) * PAGE_BYTES)
+            x[n] = regions.tile([P, S], F32, name="x_%d" % n, align_bytes=64, offset=(3, 4, 5, 9, 10, 8)[n] * PAGE_BYTES)
             nc.sync.dma_start(out=x[n][:], in_=x0[n * P : (n + 1) * P, :])
-
+        scores(0, 0, "v")
+        scores(0, 1, "v")
+        scores(0, 2, "v")
+        scores(0, 3, "v")
+        scores(0, 4, "v")
+        scores(0, 5, "v")
+        second_product(0, 5, "g")
+        project_b(0, 7)
+        first_product(0, 7, "g")
+        second_product(0, 6, "g")
+        project_b(1, 4)
+        first_product(1, 4, "g")
+        second_product(0, 7, "g")
+        quantise_h(1, 0)
+        project_b(1, 5)
+        first_product(1, 5, "g")
+        second_product(1, 4, "g")
+        project_b(1, 6)
+        first_product(1, 6, "g")
+        second_product(1, 5, "g")
+        project_b(1, 7)
+        first_product(1, 7, "g")
+        second_product(1, 6, "g")
+        second_product(1, 7, "g")
+        quantise_h(1, 1)
+        place(0, 0)
+        place(0, 1)
+        place(0, 2)
+        place(0, 3)
+        place(0, 4)
+        place(0, 5)
+        scores(1, 0, "v")
+        scores(1, 1, "g")
+        scores(1, 2, "g")
+        scores(1, 3, "g")
+        scores(1, 4, "g")
+        scores(1, 5, "g")
+        place(1, 0)
+        place(1, 1)
+        place(1, 2)
+        place(1, 3)
+        place(1, 4)
+        place(1, 5)
         for n in range(NT):
-            scores(0, n, "vvvvvv"[n])
-        for a in range(PASSES):
-            for q in range(CHUNKS, 2 * CHUNKS):
-                first_product(a, q, J1[2 * a][q - CHUNKS])
-                second_product(a, q, J1[2 * a + 1][q - CHUNKS])
-            quantise_h(1, a)
-        for n in range(NT):
-            place(0, n)
-        for n in range(NT):
-            scores(1, n, "gggggg"[n])
-        for n in range(NT):
-            place(1, n)
-        for n in range(NT):
-            res = work.tile([P, S], F32, name="res", tag="res", bufs=3)
-            xn = x[n][:]
             rows = slice(n * P, (n + 1) * P)
             if "gggggv"[n] == "v":
+                res = late.tile([P, S], F32, name="factor", tag="factor", bufs=2, offset=HALF * 4)
                 for u in range(2):
                     cols = slice(u * HALF, (u + 1) * HALF)
-                    nc.vector.scalar_tensor_tensor(res[:, cols], page[n][:, cols], 1.0, xn[:, cols], ADD, MULT)
+                    nc.vector.scalar_tensor_tensor(res[:, cols], page[n][:, cols], 1.0, x[n][:, cols], ADD, MULT)
                     nc.sync.dma_start(out=out[rows, cols], in_=res[:, cols])
             else:
-                nc.scalar.activation(res[:], page[n][:], COPY, bias=1.0, scale=1.0)
-                nc.gpsimd.tensor_tensor(res[:], res[:], xn, MULT)
-                nc.sync.dma_start(out=out[rows, :], in_=res[:])
+                factor = late.tile([P, S], F32, name="factor", tag="factor", bufs=2, offset=HALF * 4)
+                nc.scalar.activation(factor[:], page[n][:], COPY, bias=1.0, scale=1.0)
+                for u in range(1):
+                    cols = slice(u * S // 1, (u + 1) * S // 1)
+                    nc.gpsimd.tensor_tensor(x[n][:, cols], factor[:, cols], x[n][:, cols], MULT)
+                nc.sync.dma_start(out=out[rows, :], in_=x[n][:])

@@ -52,7 +52,7 @@ def tile_list_marker_triple_interaction_kernel(
         REGION = PACK * PASS * 4
         regions = ctx.enter_context(tc.tile_pool(name="regions", bufs=1))
 
-        tab_plane = shared.tile([P, 1, T], U8, name="tab_plane", tag="plane", align_bytes=64, offset=6 * S * 4)
+        tab_plane = shared.tile([P, 1, T], U8, name="tab_plane", tag="plane", align_bytes=64, offset=7 * S * 4)
         w2_plane_raw = held.tile([P, 1, H], U8, name="w2_plane_raw", align_bytes=64)
         nc.vector.memset(tab_plane[:].bitcast(I32), 0)
         nc.gpsimd.memset(w2_plane_raw[:].bitcast(I32), 0)
@@ -95,9 +95,12 @@ def tile_list_marker_triple_interaction_kernel(
         v = held.tile([P, S], U32, name="v", align_bytes=64)
         v_plane = held.tile([P, S], U8, name="v_plane", align_bytes=64)
         nc.vector.tensor_copy(out=v_plane[:], in_=tab_plane[:, 0, :].indirect(idx[:]))
-        nc.vector.tensor_copy(out=v[:], in_=tab[:].indirect(idx[:]))
+        for half in range(2):
+            nc.vector.tensor_copy(
+                out=v[:, half * HALF : (half + 1) * HALF], in_=tab[:].indirect(idx[:, half * HALF // 16 : (half + 1) * HALF // 16])
+            )
 
-        w4_plane = shared.tile([P, PASSES, N], U8, name="w4_plane", align_bytes=64, offset=6 * S * 4)
+        w4_plane = shared.tile([P, PASSES, N], U8, name="w4_plane", align_bytes=64, offset=7 * S * 4)
         nc.gpsimd.memset(w4_plane[:].bitcast(I32), 0)
         load_scale_rows(nc.sync, w4_plane, w4_scales)
         codes, planes = {}, {}
@@ -147,10 +150,11 @@ def tile_list_marker_triple_interaction_kernel(
 
         hb, ab = {}, {}
         PAGE_BYTES = S * 4
+        hb_second = shared.tile([P, PASSES, HALF, PACK], BF16, name="hb_second", offset=5 * PAGE_BYTES, align_bytes=64)
         for half in range(2):
             for a in range(PASSES):
-                if (half, a) == (1, 1):
-                    hb[half, a] = shared.tile([P, HALF, PACK], BF16, name="hb_last", offset=5 * PAGE_BYTES, align_bytes=64)
+                if half == 1:
+                    hb[half, a] = hb_second[:, a]
                 elif (half, a) == (0, 0):
                     hb[half, a] = regions.tile([P, HALF, PACK], BF16, name="hb_first", offset=4 * REGION, align_bytes=64)
                 else:
@@ -201,6 +205,16 @@ def tile_list_marker_triple_interaction_kernel(
                 in_=hb[half, a][:].rearrange("p j t -> p (j t)"),
             )
 
+        def quantise_second_half():
+            words = held.tile([P, PASSES, HALF], U32, name="hq_second", align_bytes=64)
+            plane = held.tile([P, PASSES, HALF], U8, name="hs_second", align_bytes=64)
+            nc.vector.quantize_mx(
+                out=words[:].rearrange("p a j -> p (a j)").bitcast(FP8X4), scales=plane[:].rearrange("p a j -> p (a j)"),
+                in_=hb_second[:].rearrange("p a j t -> p (a j t)"),
+            )
+            for a in range(PASSES):
+                hq[1, a], hs[1, a] = words[:, a], plane[:, a]
+
         yw = {}
 
         def scores(half, n, engine):
@@ -215,7 +229,10 @@ def tile_list_marker_triple_interaction_kernel(
                 )
             yw[half, n] = work.tile([P, HALF], F32, name="yw", tag="yw", bufs=8)
             g = gain[:, half * HALF : (half + 1) * HALF]
-            if engine == "v":
+            if engine == "f":
+                nc.scalar.copy(out=yw[half, n][:], in_=bank[:])
+                fused.add((half, n))
+            elif engine == "v":
                 nc.vector.tensor_tensor(yw[half, n][:], bank[:], g, MULT)
             else:
                 y_sb = late.tile([P, HALF], F32, name="y_sb_%d_%d" % (half, n), offset=(n - 1) * HALF * 4)
@@ -223,20 +240,24 @@ def tile_list_marker_triple_interaction_kernel(
                 nc.gpsimd.tensor_tensor(yw[half, n][:], y_sb[:], g, MULT)
 
         page = {}
+        fused = set()
 
         def place(half, n):
             if half == 0:
                 page[n] = shared.tile([P, S], F32, name="page_%d" % n, offset=n * PAGE_BYTES, align_bytes=64)
             cols = slice(half * HALF // 16, (half + 1) * HALF // 16)
-            nc.vector.tensor_copy(out=page[n][:].indirect(idx2[:, cols]), in_=yw[half, n][:])
+            if (half, n) in fused:
+                nc.vector.tensor_tensor(page[n][:].indirect(idx2[:, cols]), yw[half, n][:], gain[:, half * HALF : (half + 1) * HALF], MULT)
+            else:
+                nc.vector.tensor_copy(out=page[n][:].indirect(idx2[:, cols]), in_=yw[half, n][:])
 
         quantise_weight("w1", 0, [("v", 0, P)])
         w4 = regions.tile([P, PASSES, N], U32, name="w4", align_bytes=64, offset=0)
         nc.sync.dma_start(out=w4[:].bitcast(I32), in_=w4_words.rearrange("a p e i -> p a (e i)").bitcast(I32))
-        quantise_weight("w3", 0, [("v", 0, 48), ("s", 48, 128)])
+        quantise_weight("w3", 0, [("v", 0, P)])
         gain = regions.tile([P, S], F32, name="gain", align_bytes=64, offset=REGION)
         nc.sync.dma_start(out=gain[:], in_=wgo)
-        quantise_weight("w1", 1, [("v", 0, 48), ("s", 48, 128)])
+        quantise_weight("w1", 1, [("s", 0, P)])
         quantise_weight("w3", 1, [("v", 0, 64), ("s", 64, 128)])
         project_b(0, 0)
         project_b(0, 1)
@@ -254,10 +275,10 @@ def tile_list_marker_triple_interaction_kernel(
         project_b(1, 1)
         project_b(1, 2)
         project_b(1, 3)
-        first_product(1, 3, "g")
         first_product(1, 0, "v")
         first_product(1, 1, "v")
         first_product(1, 2, "v")
+        first_product(1, 3, "v")
         quantise_h(0, 0)
         second_product(1, 3, "g")
         second_product(1, 0, "v")
@@ -276,19 +297,18 @@ def tile_list_marker_triple_interaction_kernel(
             x[n] = regions.tile([P, S], F32, name="x_%d" % n, align_bytes=64, offset=(3, 4, 5, 9, 10, 8)[n] * PAGE_BYTES)
             nc.sync.dma_start(out=x[n][:], in_=x0[n * P : (n + 1) * P, :])
         scores(0, 0, "v")
-        scores(0, 1, "v")
-        scores(0, 2, "v")
-        scores(0, 3, "v")
-        scores(0, 4, "v")
-        scores(0, 5, "v")
         second_product(0, 5, "g")
+        scores(0, 1, "v")
         project_b(0, 7)
         first_product(0, 7, "g")
+        scores(0, 2, "v")
         second_product(0, 6, "g")
+        scores(0, 3, "v")
         project_b(1, 4)
         first_product(1, 4, "g")
+        scores(0, 4, "g")
         second_product(0, 7, "g")
-        quantise_h(1, 0)
+        scores(0, 5, "f")
         project_b(1, 5)
         first_product(1, 5, "g")
         second_product(1, 4, "g")
@@ -299,7 +319,7 @@ def tile_list_marker_triple_interaction_kernel(
         first_product(1, 7, "g")
         second_product(1, 6, "g")
         second_product(1, 7, "g")
-        quantise_h(1, 1)
+        quantise_second_half()
         place(0, 0)
         place(0, 1)
         place(0, 2)
@@ -329,7 +349,8 @@ def tile_list_marker_triple_interaction_kernel(
             else:
                 factor = late.tile([P, S], F32, name="factor", tag="factor", bufs=2, offset=HALF * 4)
                 nc.scalar.activation(factor[:], page[n][:], COPY, bias=1.0, scale=1.0)
-                for u in range(1):
-                    cols = slice(u * S // 1, (u + 1) * S // 1)
+                pieces = 2 if n == NT - 2 else 1
+                for u in range(pieces):
+                    cols = slice(u * S // pieces, (u + 1) * S // pieces)
                     nc.gpsimd.tensor_tensor(x[n][:, cols], factor[:, cols], x[n][:, cols], MULT)
-                nc.sync.dma_start(out=out[rows, :], in_=x[n][:])
+                    nc.sync.dma_start(out=out[rows, cols], in_=x[n][:, cols])

@@ -21,10 +21,13 @@ P = 128
 PACK = 4
 PASS = P * PACK
 PASSES = H // PASS
+GROUP = 128
+PAIR = 2 * GROUP
 HALF = S // 2
-CHUNK = 128
-CHUNKS = HALF // CHUNK
 NT = N // P
+KB = 1024
+YW = 8
+RING = 4
 
 
 def tile_list_marker_triple_interaction_kernel(
@@ -33,52 +36,58 @@ def tile_list_marker_triple_interaction_kernel(
     nc = tc.nc
     with ExitStack() as ctx:
         held = ctx.enter_context(tc.tile_pool(name="held", bufs=1))
-        work = ctx.enter_context(tc.tile_pool(name="work", bufs=1))
-        shared = ctx.enter_context(tc.tile_pool(name="shared", bufs=1))
-        late = ctx.enter_context(tc.tile_pool(name="late", bufs=1))
+        early = ctx.enter_context(tc.tile_pool(name="early", bufs=1))
+        slots = ctx.enter_context(tc.tile_pool(name="slots", bufs=1))
         psum = ctx.enter_context(tc.psum_pool(name="psum", bufs=1))
 
         def load_scale_rows(queue, plane, rows):
-            for q in range(4):
+            for quad in range(4):
                 queue.dma_start(
-                    out=plane[32 * q : 32 * q + 4].bitcast(I32),
-                    in_=rows[:, 4 * q : 4 * q + 4, :].rearrange("a r c -> r a c").bitcast(I32),
+                    out=plane[32 * quad : 32 * quad + 4].bitcast(I32),
+                    in_=rows[:, 4 * quad : 4 * quad + 4, :].rearrange("a r c -> r a c").bitcast(I32),
                 )
+
+        def bank_tile(bank, shape):
+            return psum.tile(shape, F32, name="bank_%d" % bank, tag="bank_%d" % bank)
+
+        def slot_tile(name, slot, shape, dtype):
+            return slots.tile(shape, dtype, name=name, align_bytes=64, offset=slot * 2 * KB)
 
         idx = held.tile([P, S // 16], U16, name="idx")
         idx2 = held.tile([P, S // 16], U16, name="idx2")
-        nc.sync.dma_start(idx[:], offs)
-        nc.sync.dma_start(idx2[:], offs2)
-        REGION = PACK * PASS * 4
-        regions = ctx.enter_context(tc.tile_pool(name="regions", bufs=1))
-
-        tab_plane = shared.tile([P, 1, T], U8, name="tab_plane", tag="plane", align_bytes=64, offset=7 * S * 4)
+        tab_plane = early.tile([P, 1, T], U8, name="tab_plane", align_bytes=64, offset=48 * KB)
         w2_plane_raw = held.tile([P, 1, H], U8, name="w2_plane_raw", align_bytes=64)
+        w4_plane = held.tile([P, PASSES, N], U8, name="w4_plane", align_bytes=64)
         nc.vector.memset(tab_plane[:].bitcast(I32), 0)
         nc.gpsimd.memset(w2_plane_raw[:].bitcast(I32), 0)
+        nc.gpsimd.memset(w4_plane[:].bitcast(I32), 0)
 
-        w2_raw = regions.tile([P, H], U16, name="w2_raw", align_bytes=64, offset=3 * REGION)
-        nc.sync.dma_start(out=w2_raw[:].bitcast(I32), in_=w2_words[0].bitcast(I32))
-        load_scale_rows(nc.sync, w2_plane_raw, w2_scales)
-        tab = held.tile([P, T], U32, name="tab", align_bytes=64)
+        w2_raw = held.tile([P, H], U16, name="w2_raw", align_bytes=64)
+        tab = early.tile([P, T], U32, name="tab", align_bytes=64, offset=32 * KB)
         tab_rows = tab_words[0].rearrange("p t i -> p (t i)").bitcast(I32)
-        for u in range(2):
-            cols = slice(u * T // 2, (u + 1) * T // 2)
-            nc.sync.dma_start(out=tab[:, cols].bitcast(I32), in_=tab_rows[:, cols])
-            if u == 0:
-                load_scale_rows(nc.sync, tab_plane, tab_scales)
-
         raw = {}
 
-        def load_weight(name, w, a, region):
-            raw[name, a] = regions.tile([P, PACK, PASS], F32, name="raw_%d" % region, align_bytes=64, offset=region * REGION)
-            nc.sync.dma_start(
-                out=raw[name, a][:], in_=w[:, a * PASS : (a + 1) * PASS].rearrange("(p i) c -> p i c", i=PACK)
-            )
+        def load_weight(name, w, a, slot):
+            raw[name, a] = early.tile([P, PACK, PASS], F32, name="raw_%s_%d" % (name, a), align_bytes=64, offset=slot * 8 * KB)
+            nc.sync.dma_start(out=raw[name, a][:], in_=w[:, a * PASS : (a + 1) * PASS].rearrange("(p i) c -> p i c", i=PACK))
 
+        nc.sync.dma_start(idx[:], offs)
+        nc.sync.dma_start(idx2[:], offs2)
         load_weight("w1", w1, 0, 0)
+        nc.sync.dma_start(out=w2_raw[:].bitcast(I32), in_=w2_words[0].bitcast(I32))
+        load_scale_rows(nc.sync, tab_plane, tab_scales)
+        nc.sync.dma_start(out=tab[:, : T // 2].bitcast(I32), in_=tab_rows[:, : T // 2])
+        load_scale_rows(nc.sync, w2_plane_raw, w2_scales)
+        nc.sync.dma_start(out=tab[:, T // 2 :].bitcast(I32), in_=tab_rows[:, T // 2 :])
         load_weight("w3", w3, 0, 1)
         load_weight("w1", w1, 1, 2)
+        load_weight("w3", w3, 1, 3)
+        load_scale_rows(nc.sync, w4_plane, w4_scales)
+
+        w4 = held.tile([P, PASSES, N], U32, name="w4", align_bytes=64)
+        nc.sync.dma_start(out=w4[:].bitcast(I32), in_=w4_words.rearrange("a p e i -> p a (e i)").bitcast(I32))
+        gain = held.tile([P, S], F32, name="gain", align_bytes=64)
+        nc.sync.dma_start(out=gain[:], in_=wgo)
 
         w2 = held.tile([P, H], U16, name="w2", align_bytes=64)
         w2_plane = held.tile([P, H], U8, name="w2_plane", align_bytes=64)
@@ -86,27 +95,21 @@ def tile_list_marker_triple_interaction_kernel(
             out=w2[:].rearrange("p (a t m) -> p a t m", a=PASSES, t=PACK),
             in_=w2_raw[:].rearrange("p (a m t) -> p a t m", a=PASSES, t=PACK),
         )
+        v = held.tile([P, S], U32, name="v", align_bytes=64)
+        v_plane = held.tile([P, S], U8, name="v_plane", align_bytes=64)
+        nc.vector.tensor_copy(out=v_plane[:], in_=tab_plane[:, 0, :].indirect(idx[:]))
         nc.vector.tensor_copy(
             out=w2_plane[:].rearrange("p (a t m) -> p a t m", a=PASSES, t=PACK),
             in_=w2_plane_raw[:, 0, :].rearrange("p (a m t) -> p a t m", a=PASSES, t=PACK),
         )
-
-        load_weight("w3", w3, 1, 3)
-        v = held.tile([P, S], U32, name="v", align_bytes=64)
-        v_plane = held.tile([P, S], U8, name="v_plane", align_bytes=64)
-        nc.vector.tensor_copy(out=v_plane[:], in_=tab_plane[:, 0, :].indirect(idx[:]))
         for half in range(2):
-            nc.vector.tensor_copy(
-                out=v[:, half * HALF : (half + 1) * HALF], in_=tab[:].indirect(idx[:, half * HALF // 16 : (half + 1) * HALF // 16])
-            )
+            cols = slice(half * S // 2, (half + 1) * S // 2)
+            nc.vector.tensor_copy(out=v[:, cols], in_=tab[:].indirect(idx[:, cols.start // 16 : cols.stop // 16]))
 
-        w4_plane = shared.tile([P, PASSES, N], U8, name="w4_plane", align_bytes=64, offset=7 * S * 4)
-        nc.gpsimd.memset(w4_plane[:].bitcast(I32), 0)
-        load_scale_rows(nc.sync, w4_plane, w4_scales)
         codes, planes = {}, {}
 
-        def quantise_weight(name, a, shares):
-            grouped = regions.tile([P, PACK, P, PACK], BF16, name="grouped", tag="grouped", bufs=2, align_bytes=64, offset=9 * S * 4)
+        def quantise_weight(name, a, shares, slot):
+            grouped = slot_tile("grouped_%s_%d" % (name, a), slot, [P, PACK, P, PACK], BF16)
             src = raw[name, a][:].rearrange("p i (m t) -> p m t i", t=PACK)
             dst = grouped[:].rearrange("p t m i -> p m t i")
             for engine, m0, m1 in shares:
@@ -124,8 +127,9 @@ def tile_list_marker_triple_interaction_kernel(
                 in_=grouped[:].rearrange("p t m i -> p (t m i)"),
             )
 
-        def project(name, a, j0, tag, bufs):
-            bank = psum.tile([P, PACK, CHUNK], F32, name="bank_" + tag, tag=tag, bufs=bufs)
+        def project(name, a, q, bank):
+            acc = bank_tile(bank, [P, PACK, GROUP])
+            cols = slice(q * GROUP, (q + 1) * GROUP)
             for t in range(PACK):
                 if name == "w2":
                     c0 = a * PASS + t * P
@@ -134,223 +138,204 @@ def tile_list_marker_triple_interaction_kernel(
                     lhsT = codes[name, a][:, t * P : (t + 1) * P].bitcast(FP8X4)
                     lhsT_scale = planes[name, a][:, t * P : (t + 1) * P]
                 nc.tensor.matmul_mx(
-                    out=bank[:, t, :], lhsT=lhsT, lhsT_scale=lhsT_scale,
-                    rhs=v[:, j0 : j0 + CHUNK].bitcast(FP8X4), rhs_scale=v_plane[:, j0 : j0 + CHUNK],
-                    start=True, stop=True,
+                    out=acc[:, t, :], lhsT=lhsT, lhsT_scale=lhsT_scale,
+                    rhs=v[:, cols].bitcast(FP8X4), rhs_scale=v_plane[:, cols], start=True, stop=True,
                 )
-            return bank[:].rearrange("p t j -> p j t")
+            return acc[:].rearrange("p t j -> p j t")
 
-        def evacuate(bank, tag, bufs, offset=None):
-            if offset is None:
-                sb = work.tile([P, CHUNK, PACK], F32, name=tag, tag=tag, bufs=bufs)
+        turn = {"v": 0, "s": 0}
+
+        def next_bank(engine):
+            bank = {"v": 0, "s": 4}[engine] + turn[engine] % 4
+            turn[engine] = turn[engine] + 1
+            return bank
+
+        staged, ab = {}, {}
+
+        def stage_steps(name, a, q0, q1, slot=None):
+            shape = [P, (q1 - q0) * GROUP, PACK]
+            if slot is None:
+                sb = held.tile(shape, F32, name="ring", tag="ring", bufs=RING, align_bytes=64)
             else:
-                sb = regions.tile([P, CHUNK, PACK], F32, name=tag, tag=tag, bufs=bufs, align_bytes=64, offset=offset)
-            nc.scalar.copy(out=sb[:], in_=bank)
-            return sb
+                sb = slot_tile("%s_%d_%d" % (name, a, q0), slot, shape, F32)
+            staged[name, a, q0] = sb[:]
 
-        hb, ab = {}, {}
-        PAGE_BYTES = S * 4
-        hb_second = shared.tile([P, PASSES, HALF, PACK], BF16, name="hb_second", offset=5 * PAGE_BYTES, align_bytes=64)
-        for half in range(2):
-            for a in range(PASSES):
-                if half == 1:
-                    hb[half, a] = hb_second[:, a]
-                elif (half, a) == (0, 0):
-                    hb[half, a] = regions.tile([P, HALF, PACK], BF16, name="hb_first", offset=4 * REGION, align_bytes=64)
-                else:
-                    hb[half, a] = held.tile([P, HALF, PACK], BF16, name="hb_%d_%d" % (half, a), align_bytes=64)
+            def step(q):
+                return lambda: nc.scalar.copy(out=sb[:, (q - q0) * GROUP : (q - q0 + 1) * GROUP, :], in_=project(name, a, q, next_bank("s")))
 
-        b_sb = {}
+            return [step(q) for q in range(q0, q1)]
 
-        def project_b(a, q):
-            if q < CHUNKS:
-                b_sb[a, q] = evacuate(project("w2", a, q * CHUNK, "ay", 3), "b0", 8)
-            else:
-                b_sb[a, q] = evacuate(project("w2", a, q * CHUNK, "g", 2), "bg", 2, 3 * REGION)
+        def stage(name, a, q0, q1, slot=None):
+            for step in stage_steps(name, a, q0, q1, slot):
+                step()
 
-        def first_product(a, q, engine):
-            j0 = q * CHUNK
-            if q < CHUNKS:
-                ab[a, q] = work.tile([P, CHUNK, PACK], F32, name="abv", tag="abv", bufs=8)
-            else:
-                ab[a, q] = work.tile([P, CHUNK, PACK], F32, name="abg", tag="abg", bufs=3)
+        hb = {}
+        for half, offset in ((0, 56), (1, 44)):
+            hb[half] = early.tile([P, PASSES, HALF, PACK], BF16, name="hb_%d" % half, align_bytes=64, offset=offset * KB)
+
+        def h_slice(a, q0, q1):
+            half, first = divmod(q0, 4)
+            return hb[half][:, a, first * GROUP : (first + q1 - q0) * GROUP, :]
+
+        def first_product(engine, a, q0, q1, dst=None):
+            b = staged["w2", a, q0]
+            dst = b if dst is None else dst
             if engine == "v":
-                nc.vector.tensor_tensor(ab[a, q][:], project("w1", a, j0, "bc", 3), b_sb[a, q][:], MULT)
+                nc.vector.tensor_tensor(dst, project("w1", a, q0, next_bank("v")), b, MULT)
             else:
-                if q < CHUNKS:
-                    a_sb = evacuate(project("w1", a, j0, "bc", 3), "jg", 2)
-                else:
-                    a_sb = evacuate(project("w1", a, j0, "g", 2), "ag", 2, 3 * REGION + REGION // 2)
-                nc.gpsimd.tensor_tensor(ab[a, q][:], a_sb[:], b_sb[a, q][:], MULT)
+                nc.gpsimd.tensor_tensor(dst, staged["w1", a, q0], b, MULT)
+            for q in range(q0, q1):
+                ab[a, q] = (dst, q0)
 
-        def second_product(a, q, engine):
-            j0 = q * CHUNK
-            dst = hb[q // CHUNKS, a][:, (q % CHUNKS) * CHUNK : (q % CHUNKS + 1) * CHUNK, :]
+        def second_product(engine, a, q0, q1, operand=None):
+            src, first = ab[a, q0]
+            src = src[:, (q0 - first) * GROUP : (q1 - first) * GROUP, :] if operand is None else operand
             if engine == "v":
-                nc.vector.tensor_tensor(dst, project("w3", a, j0, "bc", 3), ab[a, q][:], MULT)
+                nc.vector.tensor_tensor(h_slice(a, q0, q1), project("w3", a, q0, next_bank("v")), src, MULT)
             else:
-                if q < CHUNKS:
-                    c_sb = evacuate(project("w3", a, j0, "bc", 3), "jg", 2)
-                else:
-                    c_sb = evacuate(project("w3", a, j0, "g", 2), "cg", 2)
-                nc.gpsimd.tensor_tensor(dst, c_sb[:], ab[a, q][:], MULT)
+                nc.gpsimd.tensor_tensor(h_slice(a, q0, q1), staged["w3", a, q0], src, MULT)
 
         hq, hs = {}, {}
 
-        def quantise_h(half, a):
-            hq[half, a] = held.tile([P, HALF], U32, name="hq_%d_%d" % (half, a), align_bytes=64)
-            hs[half, a] = held.tile([P, HALF], U8, name="hs_%d_%d" % (half, a), align_bytes=64)
+        def quantise_h(half):
+            hq[half] = held.tile([P, PASSES, HALF], U32, name="hq_%d" % half, align_bytes=64)
+            hs[half] = held.tile([P, PASSES, HALF], U8, name="hs_%d" % half, align_bytes=64)
             nc.vector.quantize_mx(
-                out=hq[half, a][:].bitcast(FP8X4), scales=hs[half, a][:],
-                in_=hb[half, a][:].rearrange("p j t -> p (j t)"),
+                out=hq[half][:].rearrange("p a j -> p (a j)").bitcast(FP8X4), scales=hs[half][:].rearrange("p a j -> p (a j)"),
+                in_=hb[half][:].rearrange("p a j t -> p (a j t)"),
             )
 
-        def quantise_second_half():
-            words = held.tile([P, PASSES, HALF], U32, name="hq_second", align_bytes=64)
-            plane = held.tile([P, PASSES, HALF], U8, name="hs_second", align_bytes=64)
-            nc.vector.quantize_mx(
-                out=words[:].rearrange("p a j -> p (a j)").bitcast(FP8X4), scales=plane[:].rearrange("p a j -> p (a j)"),
-                in_=hb_second[:].rearrange("p a j t -> p (a j t)"),
-            )
+        def scores(half, n, bank):
+            acc = bank_tile(bank, [P, HALF])
+            rows = slice(n * P, (n + 1) * P)
             for a in range(PASSES):
-                hq[1, a], hs[1, a] = words[:, a], plane[:, a]
-
-        yw = {}
-
-        def scores(half, n, engine):
-            tag = "ay" if n < NT // 2 else "bc"
-            bank = psum.tile([P, HALF], F32, name="bank_" + tag, tag=tag, bufs=3)
-            cols = slice(n * P, (n + 1) * P)
-            for a in reversed(range(PASSES)):
                 nc.tensor.matmul_mx(
-                    out=bank[:], lhsT=w4[:, a, cols].bitcast(FP8X4), lhsT_scale=w4_plane[:, a, cols],
-                    rhs=hq[half, a][:].bitcast(FP8X4), rhs_scale=hs[half, a][:],
-                    start=(a == PASSES - 1), stop=(a == 0),
+                    out=acc[:], lhsT=w4[:, a, rows].bitcast(FP8X4), lhsT_scale=w4_plane[:, a, rows],
+                    rhs=hq[half][:, a, :].bitcast(FP8X4), rhs_scale=hs[half][:, a, :],
+                    start=(a == 0), stop=(a == PASSES - 1),
                 )
-            yw[half, n] = work.tile([P, HALF], F32, name="yw", tag="yw", bufs=8)
-            g = gain[:, half * HALF : (half + 1) * HALF]
-            if engine == "f":
-                nc.scalar.copy(out=yw[half, n][:], in_=bank[:])
-                fused.add((half, n))
-            elif engine == "v":
-                nc.vector.tensor_tensor(yw[half, n][:], bank[:], g, MULT)
-            else:
-                y_sb = late.tile([P, HALF], F32, name="y_sb_%d_%d" % (half, n), offset=(n - 1) * HALF * 4)
-                nc.scalar.copy(out=y_sb[:], in_=bank[:])
-                nc.gpsimd.tensor_tensor(yw[half, n][:], y_sb[:], g, MULT)
+            return acc
+
+        def half_gain(half):
+            return gain[:, half * HALF : (half + 1) * HALF]
+
+        weighted = {}
+
+        def weigh_on_vector(half, n):
+            weighted[half, n] = held.tile([P, HALF], F32, name="yw", tag="yw", bufs=YW)
+            nc.vector.tensor_tensor(weighted[half, n][:], scores(half, n, next_bank("v"))[:], half_gain(half), MULT)
+
+        def stage_scores(half, n, slot):
+            staged["y", half, n] = slot_tile("y_%d_%d" % (half, n), slot, [P, HALF], F32)
+            nc.scalar.copy(out=staged["y", half, n][:], in_=scores(half, n, next_bank("s"))[:])
+
+        def weigh_on_gpsimd(half, n):
+            weighted[half, n] = held.tile([P, HALF], F32, name="yw", tag="yw", bufs=YW)
+            nc.gpsimd.tensor_tensor(weighted[half, n][:], staged["y", half, n][:], half_gain(half), MULT)
 
         page = {}
-        fused = set()
 
         def place(half, n):
             if half == 0:
-                page[n] = shared.tile([P, S], F32, name="page_%d" % n, offset=n * PAGE_BYTES, align_bytes=64)
-            cols = slice(half * HALF // 16, (half + 1) * HALF // 16)
-            if (half, n) in fused:
-                nc.vector.tensor_tensor(page[n][:].indirect(idx2[:, cols]), yw[half, n][:], gain[:, half * HALF : (half + 1) * HALF], MULT)
+                page[n] = early.tile([P, S], F32, name="page_%d" % n, align_bytes=64, offset=(24 + 4 * n) * KB)
+            window = page[n][:].indirect(idx2[:, half * HALF // 16 : (half + 1) * HALF // 16])
+            if (half, n) in weighted:
+                nc.vector.tensor_copy(out=window, in_=weighted[half, n][:])
             else:
-                nc.vector.tensor_copy(out=page[n][:].indirect(idx2[:, cols]), in_=yw[half, n][:])
+                nc.vector.tensor_tensor(window, staged["y", half, n][:], half_gain(half), MULT)
 
-        quantise_weight("w1", 0, [("v", 0, P)])
-        w4 = regions.tile([P, PASSES, N], U32, name="w4", align_bytes=64, offset=0)
-        nc.sync.dma_start(out=w4[:].bitcast(I32), in_=w4_words.rearrange("a p e i -> p a (e i)").bitcast(I32))
-        quantise_weight("w3", 0, [("v", 0, P)])
-        gain = regions.tile([P, S], F32, name="gain", align_bytes=64, offset=REGION)
-        nc.sync.dma_start(out=gain[:], in_=wgo)
-        quantise_weight("w1", 1, [("s", 0, P)])
-        quantise_weight("w3", 1, [("v", 0, 64), ("s", 64, 128)])
-        project_b(0, 0)
-        project_b(0, 1)
-        project_b(0, 2)
-        project_b(0, 3)
-        first_product(0, 0, "v")
-        first_product(0, 1, "v")
-        first_product(0, 2, "v")
-        first_product(0, 3, "v")
-        second_product(0, 3, "g")
-        second_product(0, 0, "v")
-        second_product(0, 1, "v")
-        second_product(0, 2, "v")
-        project_b(1, 0)
-        project_b(1, 1)
-        project_b(1, 2)
-        project_b(1, 3)
-        first_product(1, 0, "v")
-        first_product(1, 1, "v")
-        first_product(1, 2, "v")
-        first_product(1, 3, "v")
-        quantise_h(0, 0)
-        second_product(1, 3, "g")
-        second_product(1, 0, "v")
-        second_product(1, 1, "v")
-        second_product(1, 2, "v")
-        project_b(0, 4)
-        first_product(0, 4, "g")
-        project_b(0, 5)
-        first_product(0, 5, "g")
-        second_product(0, 4, "g")
-        project_b(0, 6)
-        first_product(0, 6, "g")
-        quantise_h(0, 1)
+        V_WEIGH = 3
+
+        def after_first_half(name, offset):
+            return early.tile([P, PAIR, PACK], F32, name=name, align_bytes=64, offset=offset * KB)[:]
+
+        shares = [("s", 0, 64), ("g", 64, P)]
+        quantise_weight("w1", 0, [("s", 0, P)], 27)
+        quantise_weight("w3", 0, shares, 29)
+        quantise_weight("w1", 1, shares, 27)
+        for q, slot in enumerate((0, 2, 3)):
+            stage("w2", 0, q, q + 1, slot)
+            first_product("v", 0, q, q + 1)
+        stage("w2", 0, 3, 4, 4)
+        stage("w2", 1, 0, 1, 5)
+        second_product("v", 0, 0, 1)
+        quantise_weight("w3", 1, shares, 0)
+        second_product("v", 0, 1, 2)
+        second_product("v", 0, 2, 3)
+        first_product("v", 0, 3, 4)
+        scalar_steps = stage_steps("w3", 0, 3, 4)
+        for q in range(1, 4):
+            scalar_steps = scalar_steps + stage_steps("w2", 1, q, q + 1, 5 + q)
+        scalar_steps = scalar_steps + stage_steps("w3", 1, 0, 1)
+        for q in (4, 5):
+            scalar_steps = scalar_steps + stage_steps("w2", 0, q, q + 1, 5 + q)
+        scalar_steps = scalar_steps + stage_steps("w2", 1, 4, 6, 11) + stage_steps("w1", 1, 4, 6)
+        fill = after_first_half("ab_0_4", 53)
+        vector_steps = [lambda q=q: first_product("v", 1, q, q + 1) for q in range(4)]
+        vector_steps = vector_steps + [lambda q=q: second_product("v", 1, q, q + 1) for q in range(1, 4)]
+        scalar_steps[0]()
+        second_product("g", 0, 3, 4)
+        for k, step in enumerate(vector_steps):
+            scalar_steps[k + 1]()
+            if k == 3:
+                second_product("g", 1, 0, 1)
+            step()
+        quantise_h(0)
+        for g in range(2):
+            scalar_steps[8 + g]()
+            first_product("v", 0, 4 + g, 5 + g, fill[:, g * GROUP : (g + 1) * GROUP, :])
+        ab[0, 4] = (fill, 4)
+        scalar_steps[10]()
+        first_product("g", 1, 4, 6, after_first_half("ab_1_4", 57))
         x = {}
         for n in range(NT):
-            x[n] = regions.tile([P, S], F32, name="x_%d" % n, align_bytes=64, offset=(3, 4, 5, 9, 10, 8)[n] * PAGE_BYTES)
+            x[n] = early.tile([P, S], F32, name="x_%d" % n, align_bytes=64, offset=4 * n * KB)
             nc.sync.dma_start(out=x[n][:], in_=x0[n * P : (n + 1) * P, :])
-        scores(0, 0, "v")
-        second_product(0, 5, "g")
-        scores(0, 1, "v")
-        project_b(0, 7)
-        first_product(0, 7, "g")
-        scores(0, 2, "v")
-        second_product(0, 6, "g")
-        scores(0, 3, "v")
-        project_b(1, 4)
-        first_product(1, 4, "g")
-        scores(0, 4, "g")
-        second_product(0, 7, "g")
-        scores(0, 5, "f")
-        project_b(1, 5)
-        first_product(1, 5, "g")
-        second_product(1, 4, "g")
-        project_b(1, 6)
-        first_product(1, 6, "g")
-        second_product(1, 5, "g")
-        project_b(1, 7)
-        first_product(1, 7, "g")
-        second_product(1, 6, "g")
-        second_product(1, 7, "g")
-        quantise_second_half()
-        place(0, 0)
-        place(0, 1)
-        place(0, 2)
-        place(0, 3)
-        place(0, 4)
+        steps = [("w3", 1, 4), ("w3", 0, 4), ("w1", 0, 6), ("w3", 0, 6), ("w1", 1, 6), ("w3", 1, 6)]
+        for n in range(V_WEIGH):
+            weigh_on_vector(0, n)
+            if n == 0:
+                stage("w3", 1, 4, 6)
+            place(0, n)
+        for k, (name, a, q) in enumerate(steps):
+            n = V_WEIGH + k
+            if n < NT - 1:
+                stage_scores(0, n, 12 + n)
+            if name == "w1":
+                stage("w2", a, q, q + 2, 17 + 3 * a)
+            if k > 0:
+                stage(name, a, q, q + 2)
+            if name == "w3":
+                second_product("g", a, q, q + 2)
+            elif a == 0:
+                first_product("g", a, q, q + 2, after_first_half("ab_0_6", 61))
+            else:
+                first_product("g", a, q, q + 2)
+            if n < NT - 1:
+                weigh_on_gpsimd(0, n)
+                place(0, n)
+        stage_scores(0, 5, 19)
+        quantise_h(1)
         place(0, 5)
-        scores(1, 0, "v")
-        scores(1, 1, "g")
-        scores(1, 2, "g")
-        scores(1, 3, "g")
-        scores(1, 4, "g")
-        scores(1, 5, "g")
+        weigh_on_vector(1, 0)
         place(1, 0)
-        place(1, 1)
-        place(1, 2)
-        place(1, 3)
-        place(1, 4)
-        place(1, 5)
+        for n in range(1, NT):
+            stage_scores(1, n, (22, 23, 27, 28, 25)[n - 1])
+            weigh_on_gpsimd(1, n)
+            place(1, n)
         for n in range(NT):
             rows = slice(n * P, (n + 1) * P)
-            if "gggggv"[n] == "v":
-                res = late.tile([P, S], F32, name="factor", tag="factor", bufs=2, offset=HALF * 4)
+            if n == NT - 1:
+                res = slots.tile([P, S], F32, name="res", align_bytes=64, offset=47 * KB)
                 for u in range(2):
                     cols = slice(u * HALF, (u + 1) * HALF)
                     nc.vector.scalar_tensor_tensor(res[:, cols], page[n][:, cols], 1.0, x[n][:, cols], ADD, MULT)
                     nc.sync.dma_start(out=out[rows, cols], in_=res[:, cols])
             else:
-                factor = late.tile([P, S], F32, name="factor", tag="factor", bufs=2, offset=HALF * 4)
-                nc.scalar.activation(factor[:], page[n][:], COPY, bias=1.0, scale=1.0)
+                factor = slots.tile([P, S], F32, name="factor", tag="factor", bufs=2, align_bytes=64, offset=47 * KB)
                 pieces = 2 if n == NT - 2 else 1
                 for u in range(pieces):
                     cols = slice(u * S // pieces, (u + 1) * S // pieces)
+                    nc.scalar.activation(factor[:, cols], page[n][:, cols], COPY, bias=1.0, scale=1.0)
                     nc.gpsimd.tensor_tensor(x[n][:, cols], factor[:, cols], x[n][:, cols], MULT)
                     nc.sync.dma_start(out=out[rows, cols], in_=x[n][:, cols])

@@ -67,18 +67,24 @@ def tile_list_marker_triple_interaction_kernel(
         tab_rows = tab_words[0].rearrange("p t i -> p (t i)").bitcast(I32)
         raw = {}
 
-        def load_weight(name, w, a, slot):
-            raw[name, a] = early.tile([P, PACK, PASS], F32, name="raw_%s_%d" % (name, a), align_bytes=64, offset=slot * 8 * KB)
-            nc.sync.dma_start(out=raw[name, a][:], in_=w[:, a * PASS : (a + 1) * PASS].rearrange("(p i) c -> p i c", i=PACK))
+        def load_weight(name, w, a, slot, pieces=1):
+            width = PASS // pieces
+            for u in range(pieces):
+                tile = early.tile(
+                    [P, PACK, width], F32, name="raw_%s_%d_%d" % (name, a, u), align_bytes=64, offset=slot * 8 * KB + u * 16 * width
+                )
+                cols = slice(a * PASS + u * width, a * PASS + (u + 1) * width)
+                nc.sync.dma_start(out=tile[:], in_=w[:, cols].rearrange("(p i) c -> p i c", i=PACK))
+                raw[name, a, u] = tile
 
         nc.sync.dma_start(idx[:], offs)
         nc.sync.dma_start(idx2[:], offs2)
-        load_weight("w1", w1, 0, 0)
         nc.sync.dma_start(out=w2_raw[:].bitcast(I32), in_=w2_words[0].bitcast(I32))
-        load_scale_rows(nc.sync, tab_plane, tab_scales)
-        nc.sync.dma_start(out=tab[:, : T // 2].bitcast(I32), in_=tab_rows[:, : T // 2])
         load_scale_rows(nc.sync, w2_plane_raw, w2_scales)
+        nc.sync.dma_start(out=tab[:, : T // 2].bitcast(I32), in_=tab_rows[:, : T // 2])
+        load_scale_rows(nc.sync, tab_plane, tab_scales)
         nc.sync.dma_start(out=tab[:, T // 2 :].bitcast(I32), in_=tab_rows[:, T // 2 :])
+        load_weight("w1", w1, 0, 0, 2)
         load_weight("w3", w3, 0, 1)
         load_weight("w1", w1, 1, 2)
         load_weight("w3", w3, 1, 3)
@@ -110,15 +116,16 @@ def tile_list_marker_triple_interaction_kernel(
 
         def quantise_weight(name, a, shares, slot):
             grouped = slot_tile("grouped_%s_%d" % (name, a), slot, [P, PACK, P, PACK], BF16)
-            src = raw[name, a][:].rearrange("p i (m t) -> p m t i", t=PACK)
-            dst = grouped[:].rearrange("p t m i -> p m t i")
             for engine, m0, m1 in shares:
+                u = 1 if (name, a, 1) in raw and m0 >= P // 2 else 0
+                src = raw[name, a, u][:].rearrange("p i (m t) -> p m t i", t=PACK)[:, m0 - u * P // 2 : m1 - u * P // 2]
+                dst = grouped[:].rearrange("p t m i -> p m t i")[:, m0:m1]
                 if engine == "v":
-                    nc.vector.tensor_copy(out=dst[:, m0:m1], in_=src[:, m0:m1])
+                    nc.vector.tensor_copy(out=dst, in_=src)
                 elif engine == "s":
-                    nc.scalar.copy(out=dst[:, m0:m1], in_=src[:, m0:m1])
+                    nc.scalar.copy(out=dst, in_=src)
                 else:
-                    nc.gpsimd.tensor_scalar(dst[:, m0:m1], src[:, m0:m1], 1.0, 0.0, MULT, ADD)
+                    nc.gpsimd.tensor_scalar(dst, src, 1.0, 0.0, MULT, ADD)
             codes[name, a] = held.tile([P, PASS], U32, name="codes_%s_%d" % (name, a), align_bytes=64)
             planes[name, a] = held.tile([P, PASS], U8, name="plane_%s_%d" % (name, a), align_bytes=64)
             nc.vector.quantize_mx(
@@ -250,13 +257,13 @@ def tile_list_marker_triple_interaction_kernel(
             return early.tile([P, PAIR, PACK], F32, name=name, align_bytes=64, offset=offset * KB)[:]
 
         shares = [("s", 0, 64), ("g", 64, P)]
-        quantise_weight("w1", 0, [("s", 0, P)], 27)
+        quantise_weight("w1", 0, [("s", 0, P // 2), ("v", P // 2, P)], 27)
         quantise_weight("w3", 0, shares, 29)
-        quantise_weight("w1", 1, shares, 27)
-        for q, slot in enumerate((0, 2, 3)):
+        quantise_weight("w1", 1, shares, 31)
+        for q, slot in enumerate((0, 2, 3, 4)):
             stage("w2", 0, q, q + 1, slot)
+        for q in range(3):
             first_product("v", 0, q, q + 1)
-        stage("w2", 0, 3, 4, 4)
         stage("w2", 1, 0, 1, 5)
         second_product("v", 0, 0, 1)
         quantise_weight("w3", 1, shares, 0)
@@ -291,15 +298,15 @@ def tile_list_marker_triple_interaction_kernel(
         for n in range(NT):
             x[n] = early.tile([P, S], F32, name="x_%d" % n, align_bytes=64, offset=4 * n * KB)
             nc.sync.dma_start(out=x[n][:], in_=x0[n * P : (n + 1) * P, :])
-        steps = [("w3", 1, 4), ("w3", 0, 4), ("w1", 0, 6), ("w3", 0, 6), ("w1", 1, 6), ("w3", 1, 6)]
+        steps = [("w3", 0, 4), ("w3", 1, 4), ("w1", 0, 6), ("w1", 1, 6), ("w3", 0, 6), ("w3", 1, 6)]
         for n in range(V_WEIGH):
             weigh_on_vector(0, n)
             if n == 0:
-                stage("w3", 1, 4, 6)
+                stage("w3", 0, 4, 6)
             place(0, n)
         for k, (name, a, q) in enumerate(steps):
-            n = V_WEIGH + k
-            if n < NT - 1:
+            n = V_WEIGH + k - 1
+            if V_WEIGH <= n < NT - 1:
                 stage_scores(0, n, 12 + n)
             if name == "w1":
                 stage("w2", a, q, q + 2, 17 + 3 * a)
@@ -311,7 +318,7 @@ def tile_list_marker_triple_interaction_kernel(
                 first_product("g", a, q, q + 2, after_first_half("ab_0_6", 61))
             else:
                 first_product("g", a, q, q + 2)
-            if n < NT - 1:
+            if V_WEIGH <= n < NT - 1:
                 weigh_on_gpsimd(0, n)
                 place(0, n)
         stage_scores(0, 5, 19)

@@ -256,17 +256,16 @@ def tile_list_marker_triple_interaction_kernel(
         def after_first_half(name, offset):
             return early.tile([P, PAIR, PACK], F32, name=name, align_bytes=64, offset=offset * KB)[:]
 
-        shares = [("s", 0, 64), ("g", 64, P)]
         quantise_weight("w1", 0, [("s", 0, P // 2), ("v", P // 2, P)], 27)
-        quantise_weight("w3", 0, shares, 29)
-        quantise_weight("w1", 1, shares, 31)
+        quantise_weight("w3", 0, [("s", 0, 48), ("v", 48, 128)], 29)
+        quantise_weight("w1", 1, [("s", 0, 48), ("v", 48, 128)], 31)
         for q, slot in enumerate((0, 2, 3, 4)):
             stage("w2", 0, q, q + 1, slot)
         for q in range(3):
             first_product("v", 0, q, q + 1)
         stage("w2", 1, 0, 1, 5)
         second_product("v", 0, 0, 1)
-        quantise_weight("w3", 1, shares, 0)
+        quantise_weight("w3", 1, [("s", 0, 48), ("v", 48, 128)], 0)
         second_product("v", 0, 1, 2)
         second_product("v", 0, 2, 3)
         first_product("v", 0, 3, 4)

@@ -22,12 +22,12 @@ PACK = 4
 PASS = P * PACK
 PASSES = H // PASS
 GROUP = 128
-PAIR = 2 * GROUP
 HALF = S // 2
 NT = N // P
 KB = 1024
-YW = 8
-RING = 4
+SCALAR_SHARE = 64
+VECTOR_WEIGHS = 2
+GPSIMD_CLOSES = 768
 
 
 def tile_list_marker_triple_interaction_kernel(
@@ -40,22 +40,22 @@ def tile_list_marker_triple_interaction_kernel(
         slots = ctx.enter_context(tc.tile_pool(name="slots", bufs=1))
         psum = ctx.enter_context(tc.psum_pool(name="psum", bufs=1))
 
-        def load_scale_rows(queue, plane, rows):
+        def early_tile(name, kb, shape, dtype):
+            return early.tile(shape, dtype, name=name, align_bytes=64, offset=kb * KB)
+
+        def slot_tile(name, kb, shape, dtype):
+            return slots.tile(shape, dtype, name=name, align_bytes=64, offset=kb * KB)
+
+        def load_scale_rows(plane, rows):
             for quad in range(4):
-                queue.dma_start(
+                nc.sync.dma_start(
                     out=plane[32 * quad : 32 * quad + 4].bitcast(I32),
                     in_=rows[:, 4 * quad : 4 * quad + 4, :].rearrange("a r c -> r a c").bitcast(I32),
                 )
 
-        def bank_tile(bank, shape):
-            return psum.tile(shape, F32, name="bank_%d" % bank, tag="bank_%d" % bank)
-
-        def slot_tile(name, slot, shape, dtype):
-            return slots.tile(shape, dtype, name=name, align_bytes=64, offset=slot * 2 * KB)
-
         idx = held.tile([P, S // 16], U16, name="idx")
         idx2 = held.tile([P, S // 16], U16, name="idx2")
-        tab_plane = early.tile([P, 1, T], U8, name="tab_plane", align_bytes=64, offset=48 * KB)
+        tab_plane = early_tile("tab_plane", 48, [P, 1, T], U8)
         w2_plane_raw = held.tile([P, 1, H], U8, name="w2_plane_raw", align_bytes=64)
         w4_plane = held.tile([P, PASSES, N], U8, name="w4_plane", align_bytes=64)
         nc.vector.memset(tab_plane[:].bitcast(I32), 0)
@@ -63,33 +63,26 @@ def tile_list_marker_triple_interaction_kernel(
         nc.gpsimd.memset(w4_plane[:].bitcast(I32), 0)
 
         w2_raw = held.tile([P, H], U16, name="w2_raw", align_bytes=64)
-        tab = early.tile([P, T], U32, name="tab", align_bytes=64, offset=32 * KB)
+        tab = early_tile("tab", 32, [P, T], U32)
         tab_rows = tab_words[0].rearrange("p t i -> p (t i)").bitcast(I32)
-        raw = {}
 
-        def load_weight(name, w, a, slot, pieces=1):
-            width = PASS // pieces
-            for u in range(pieces):
-                tile = early.tile(
-                    [P, PACK, width], F32, name="raw_%s_%d_%d" % (name, a, u), align_bytes=64, offset=slot * 8 * KB + u * 16 * width
-                )
-                cols = slice(a * PASS + u * width, a * PASS + (u + 1) * width)
-                nc.sync.dma_start(out=tile[:], in_=w[:, cols].rearrange("(p i) c -> p i c", i=PACK))
-                raw[name, a, u] = tile
+        def load_weight(name, w, first, width, kb):
+            tile = early_tile("raw_%s_%d" % (name, first), kb, [P, PACK, width], F32)
+            nc.sync.dma_start(out=tile[:], in_=w[:, first : first + width].rearrange("(p i) c -> p i c", i=PACK))
+            return tile[:].rearrange("p i (m t) -> p m t i", t=PACK)
 
         nc.sync.dma_start(idx[:], offs)
         nc.sync.dma_start(idx2[:], offs2)
         nc.sync.dma_start(out=w2_raw[:].bitcast(I32), in_=w2_words[0].bitcast(I32))
-        load_scale_rows(nc.sync, w2_plane_raw, w2_scales)
+        load_scale_rows(w2_plane_raw, w2_scales)
         nc.sync.dma_start(out=tab[:, : T // 2].bitcast(I32), in_=tab_rows[:, : T // 2])
-        load_scale_rows(nc.sync, tab_plane, tab_scales)
+        load_scale_rows(tab_plane, tab_scales)
         nc.sync.dma_start(out=tab[:, T // 2 :].bitcast(I32), in_=tab_rows[:, T // 2 :])
-        load_weight("w1", w1, 0, 0, 2)
-        load_weight("w3", w3, 0, 1)
-        load_weight("w1", w1, 1, 2)
-        load_weight("w3", w3, 1, 3)
-        load_scale_rows(nc.sync, w4_plane, w4_scales)
-
+        first_halves = [load_weight("w1", w1, u * PASS // 2, PASS // 2, 4 * u) for u in range(2)]
+        raw = {}
+        for slot, (name, w, a) in enumerate((("w3", w3, 0), ("w1", w1, 1), ("w3", w3, 1))):
+            raw[name, a] = load_weight(name, w, a * PASS, PASS, 8 + 8 * slot)
+        load_scale_rows(w4_plane, w4_scales)
         w4 = held.tile([P, PASSES, N], U32, name="w4", align_bytes=64)
         nc.sync.dma_start(out=w4[:].bitcast(I32), in_=w4_words.rearrange("a p e i -> p a (e i)").bitcast(I32))
         gain = held.tile([P, S], F32, name="gain", align_bytes=64)
@@ -101,31 +94,30 @@ def tile_list_marker_triple_interaction_kernel(
             out=w2[:].rearrange("p (a t m) -> p a t m", a=PASSES, t=PACK),
             in_=w2_raw[:].rearrange("p (a m t) -> p a t m", a=PASSES, t=PACK),
         )
-        v = held.tile([P, S], U32, name="v", align_bytes=64)
-        v_plane = held.tile([P, S], U8, name="v_plane", align_bytes=64)
-        nc.vector.tensor_copy(out=v_plane[:], in_=tab_plane[:, 0, :].indirect(idx[:]))
         nc.vector.tensor_copy(
             out=w2_plane[:].rearrange("p (a t m) -> p a t m", a=PASSES, t=PACK),
             in_=w2_plane_raw[:, 0, :].rearrange("p (a m t) -> p a t m", a=PASSES, t=PACK),
         )
-        for half in range(2):
-            cols = slice(half * S // 2, (half + 1) * S // 2)
-            nc.vector.tensor_copy(out=v[:, cols], in_=tab[:].indirect(idx[:, cols.start // 16 : cols.stop // 16]))
+        v_plane = held.tile([P, S], U8, name="v_plane", align_bytes=64)
+        nc.vector.tensor_copy(out=v_plane[:], in_=tab_plane[:, 0, :].indirect(idx[:]))
+        v = {}
+
+        def gather_words(half, tile):
+            v[half] = tile
+            nc.vector.tensor_copy(out=tile[:], in_=tab[:].indirect(idx[:, half * HALF // 16 : (half + 1) * HALF // 16]))
+
+        gather_words(0, held.tile([P, HALF], U32, name="v_0", align_bytes=64))
 
         codes, planes = {}, {}
 
-        def quantise_weight(name, a, shares, slot):
-            grouped = slot_tile("grouped_%s_%d" % (name, a), slot, [P, PACK, P, PACK], BF16)
-            for engine, m0, m1 in shares:
-                u = 1 if (name, a, 1) in raw and m0 >= P // 2 else 0
-                src = raw[name, a, u][:].rearrange("p i (m t) -> p m t i", t=PACK)[:, m0 - u * P // 2 : m1 - u * P // 2]
+        def quantise_weight(name, a, kb, shares):
+            grouped = slot_tile("grouped_%s_%d" % (name, a), kb, [P, PACK, P, PACK], BF16)
+            for engine, src, m0, m1 in shares:
                 dst = grouped[:].rearrange("p t m i -> p m t i")[:, m0:m1]
-                if engine == "v":
+                if engine == "vector":
                     nc.vector.tensor_copy(out=dst, in_=src)
-                elif engine == "s":
-                    nc.scalar.copy(out=dst, in_=src)
                 else:
-                    nc.gpsimd.tensor_scalar(dst, src, 1.0, 0.0, MULT, ADD)
+                    nc.scalar.copy(out=dst, in_=src)
             codes[name, a] = held.tile([P, PASS], U32, name="codes_%s_%d" % (name, a), align_bytes=64)
             planes[name, a] = held.tile([P, PASS], U8, name="plane_%s_%d" % (name, a), align_bytes=64)
             nc.vector.quantize_mx(
@@ -134,9 +126,23 @@ def tile_list_marker_triple_interaction_kernel(
                 in_=grouped[:].rearrange("p t m i -> p (t m i)"),
             )
 
-        def project(name, a, q, bank):
-            acc = bank_tile(bank, [P, PACK, GROUP])
-            cols = slice(q * GROUP, (q + 1) * GROUP)
+        quantise_weight("w1", 0, 0, [("scalar", first_halves[0], 0, P // 2), ("vector", first_halves[1], P // 2, P)])
+        gather_words(1, held.tile([P, HALF], U32, name="v_1", align_bytes=64))
+        for slot, (name, a) in enumerate(raw):
+            src = raw[name, a]
+            shares = [("scalar", src[:, :SCALAR_SHARE], 0, SCALAR_SHARE), ("vector", src[:, SCALAR_SHARE:], SCALAR_SHARE, P)]
+            quantise_weight(name, a, 4 + 4 * slot, shares)
+
+        turn = {"vector": 0, "scalar": 0}
+
+        def next_bank(reader, shape):
+            bank = {"vector": 0, "scalar": 4}[reader] + turn[reader] % 4
+            turn[reader] = turn[reader] + 1
+            return psum.tile(shape, F32, name="bank_%d" % bank, tag="bank_%d" % bank)
+
+        def project(name, a, q, reader):
+            acc = next_bank(reader, [P, PACK, GROUP])
+            half, first = divmod(q * GROUP, HALF)
             for t in range(PACK):
                 if name == "w2":
                     c0 = a * PASS + t * P
@@ -146,61 +152,53 @@ def tile_list_marker_triple_interaction_kernel(
                     lhsT_scale = planes[name, a][:, t * P : (t + 1) * P]
                 nc.tensor.matmul_mx(
                     out=acc[:, t, :], lhsT=lhsT, lhsT_scale=lhsT_scale,
-                    rhs=v[:, cols].bitcast(FP8X4), rhs_scale=v_plane[:, cols], start=True, stop=True,
+                    rhs=v[half][:, first : first + GROUP].bitcast(FP8X4), rhs_scale=v_plane[:, q * GROUP : (q + 1) * GROUP],
+                    start=True, stop=True,
                 )
             return acc[:].rearrange("p t j -> p j t")
 
-        turn = {"v": 0, "s": 0}
-
-        def next_bank(engine):
-            bank = {"v": 0, "s": 4}[engine] + turn[engine] % 4
-            turn[engine] = turn[engine] + 1
-            return bank
-
         staged, ab = {}, {}
 
-        def stage_steps(name, a, q0, q1, slot=None):
-            shape = [P, (q1 - q0) * GROUP, PACK]
-            if slot is None:
-                sb = held.tile(shape, F32, name="ring", tag="ring", bufs=RING, align_bytes=64)
+        def staging_tile(name, a, q0, groups):
+            shape = [P, groups * GROUP, PACK]
+            if name == "w2":
+                tile = slot_tile("b_%d_%d" % (a, q0), 16 + 16 * a + 2 * q0, shape, F32)
             else:
-                sb = slot_tile("%s_%d_%d" % (name, a, q0), slot, shape, F32)
-            staged[name, a, q0] = sb[:]
+                tile = held.tile(shape, F32, name="ring", tag="ring", bufs=5, align_bytes=64)
+            for g in range(groups):
+                staged[name, a, q0 + g] = tile[:, g * GROUP : (g + 1) * GROUP, :]
+            staged[name, a, q0, groups] = tile[:]
 
-            def step(q):
-                return lambda: nc.scalar.copy(out=sb[:, (q - q0) * GROUP : (q - q0 + 1) * GROUP, :], in_=project(name, a, q, next_bank("s")))
+        def stage(name, a, q, groups=1):
+            if (name, a, q) not in staged:
+                staging_tile(name, a, q, groups)
+            nc.scalar.copy(out=staged[name, a, q], in_=project(name, a, q, "scalar"))
 
-            return [step(q) for q in range(q0, q1)]
+        def stage_pair(name, a, q):
+            stage(name, a, q, 2)
+            stage(name, a, q + 1)
 
-        def stage(name, a, q0, q1, slot=None):
-            for step in stage_steps(name, a, q0, q1, slot):
-                step()
+        hb = {0: early_tile("hb_0", 56, [P, PASSES, HALF, PACK], BF16), 1: early_tile("hb_1", 44, [P, PASSES, HALF, PACK], BF16)}
 
-        hb = {}
-        for half, offset in ((0, 56), (1, 44)):
-            hb[half] = early.tile([P, PASSES, HALF, PACK], BF16, name="hb_%d" % half, align_bytes=64, offset=offset * KB)
+        def h_rows(a, q, groups):
+            half, first = divmod(q * GROUP, HALF)
+            return hb[half][:, a, first : first + groups * GROUP, :]
 
-        def h_slice(a, q0, q1):
-            half, first = divmod(q0, 4)
-            return hb[half][:, a, first * GROUP : (first + q1 - q0) * GROUP, :]
+        def vector_ab(a, q, dst=None):
+            b = staged["w2", a, q]
+            ab[a, q] = b if dst is None else dst
+            nc.vector.tensor_tensor(ab[a, q], project("w1", a, q, "vector"), b, MULT)
 
-        def first_product(engine, a, q0, q1, dst=None):
-            b = staged["w2", a, q0]
-            dst = b if dst is None else dst
-            if engine == "v":
-                nc.vector.tensor_tensor(dst, project("w1", a, q0, next_bank("v")), b, MULT)
-            else:
-                nc.gpsimd.tensor_tensor(dst, staged["w1", a, q0], b, MULT)
-            for q in range(q0, q1):
-                ab[a, q] = (dst, q0)
+        def vector_h(a, q):
+            nc.vector.tensor_tensor(h_rows(a, q, 1), project("w3", a, q, "vector"), ab[a, q], MULT)
 
-        def second_product(engine, a, q0, q1, operand=None):
-            src, first = ab[a, q0]
-            src = src[:, (q0 - first) * GROUP : (q1 - first) * GROUP, :] if operand is None else operand
-            if engine == "v":
-                nc.vector.tensor_tensor(h_slice(a, q0, q1), project("w3", a, q0, next_bank("v")), src, MULT)
-            else:
-                nc.gpsimd.tensor_tensor(h_slice(a, q0, q1), staged["w3", a, q0], src, MULT)
+        def gpsimd_ab(a, q, groups, dst=None):
+            b = staged["w2", a, q, groups]
+            ab[a, q] = b if dst is None else dst
+            nc.gpsimd.tensor_tensor(ab[a, q], staged["w1", a, q, groups], b, MULT)
+
+        def gpsimd_h(a, q, groups):
+            nc.gpsimd.tensor_tensor(h_rows(a, q, groups), staged["w3", a, q, groups], ab[a, q], MULT)
 
         hq, hs = {}, {}
 
@@ -212,8 +210,8 @@ def tile_list_marker_triple_interaction_kernel(
                 in_=hb[half][:].rearrange("p a j t -> p (a j t)"),
             )
 
-        def scores(half, n, bank):
-            acc = bank_tile(bank, [P, HALF])
+        def scores(half, n, reader):
+            acc = next_bank(reader, [P, HALF])
             rows = slice(n * P, (n + 1) * P)
             for a in range(PASSES):
                 nc.tensor.matmul_mx(
@@ -221,127 +219,115 @@ def tile_list_marker_triple_interaction_kernel(
                     rhs=hq[half][:, a, :].bitcast(FP8X4), rhs_scale=hs[half][:, a, :],
                     start=(a == 0), stop=(a == PASSES - 1),
                 )
-            return acc
+            return acc[:]
 
         def half_gain(half):
             return gain[:, half * HALF : (half + 1) * HALF]
 
-        weighted = {}
+        y, weighted = {}, {}
 
         def weigh_on_vector(half, n):
-            weighted[half, n] = held.tile([P, HALF], F32, name="yw", tag="yw", bufs=YW)
-            nc.vector.tensor_tensor(weighted[half, n][:], scores(half, n, next_bank("v"))[:], half_gain(half), MULT)
+            weighted[half, n] = held.tile([P, HALF], F32, name="weighted", tag="weighted", bufs=8)
+            nc.vector.tensor_tensor(weighted[half, n][:], scores(half, n, "vector"), half_gain(half), MULT)
 
-        def stage_scores(half, n, slot):
-            staged["y", half, n] = slot_tile("y_%d_%d" % (half, n), slot, [P, HALF], F32)
-            nc.scalar.copy(out=staged["y", half, n][:], in_=scores(half, n, next_bank("s"))[:])
+        def stage_scores(half, n, kb):
+            y[half, n] = slot_tile("y_%d_%d" % (half, n), kb, [P, HALF], F32)
+            nc.scalar.copy(out=y[half, n][:], in_=scores(half, n, "scalar"))
 
         def weigh_on_gpsimd(half, n):
-            weighted[half, n] = held.tile([P, HALF], F32, name="yw", tag="yw", bufs=YW)
-            nc.gpsimd.tensor_tensor(weighted[half, n][:], staged["y", half, n][:], half_gain(half), MULT)
+            weighted[half, n] = held.tile([P, HALF], F32, name="weighted", tag="weighted", bufs=8)
+            nc.gpsimd.tensor_tensor(weighted[half, n][:], y[half, n][:], half_gain(half), MULT)
 
         page = {}
 
         def place(half, n):
             if half == 0:
-                page[n] = early.tile([P, S], F32, name="page_%d" % n, align_bytes=64, offset=(24 + 4 * n) * KB)
+                page[n] = early_tile("page_%d" % n, 52 if n == 0 else 24 + 4 * n, [P, S], F32)
             window = page[n][:].indirect(idx2[:, half * HALF // 16 : (half + 1) * HALF // 16])
             if (half, n) in weighted:
                 nc.vector.tensor_copy(out=window, in_=weighted[half, n][:])
             else:
-                nc.vector.tensor_tensor(window, staged["y", half, n][:], half_gain(half), MULT)
+                nc.vector.tensor_tensor(window, y[half, n][:], half_gain(half), MULT)
 
-        V_WEIGH = 3
-
-        def after_first_half(name, offset):
-            return early.tile([P, PAIR, PACK], F32, name=name, align_bytes=64, offset=offset * KB)[:]
-
-        quantise_weight("w1", 0, [("s", 0, P // 2), ("v", P // 2, P)], 27)
-        quantise_weight("w3", 0, [("s", 0, 48), ("v", 48, 128)], 29)
-        quantise_weight("w1", 1, [("s", 0, 48), ("v", 48, 128)], 31)
-        for q, slot in enumerate((0, 2, 3, 4)):
-            stage("w2", 0, q, q + 1, slot)
-        for q in range(3):
-            first_product("v", 0, q, q + 1)
-        stage("w2", 1, 0, 1, 5)
-        second_product("v", 0, 0, 1)
-        quantise_weight("w3", 1, [("s", 0, 48), ("v", 48, 128)], 0)
-        second_product("v", 0, 1, 2)
-        second_product("v", 0, 2, 3)
-        first_product("v", 0, 3, 4)
-        scalar_steps = stage_steps("w3", 0, 3, 4)
-        for q in range(1, 4):
-            scalar_steps = scalar_steps + stage_steps("w2", 1, q, q + 1, 5 + q)
-        scalar_steps = scalar_steps + stage_steps("w3", 1, 0, 1)
-        for q in (4, 5):
-            scalar_steps = scalar_steps + stage_steps("w2", 0, q, q + 1, 5 + q)
-        scalar_steps = scalar_steps + stage_steps("w2", 1, 4, 6, 11) + stage_steps("w1", 1, 4, 6)
-        fill = after_first_half("ab_0_4", 53)
-        vector_steps = [lambda q=q: first_product("v", 1, q, q + 1) for q in range(4)]
-        vector_steps = vector_steps + [lambda q=q: second_product("v", 1, q, q + 1) for q in range(1, 4)]
-        scalar_steps[0]()
-        second_product("g", 0, 3, 4)
-        for k, step in enumerate(vector_steps):
-            scalar_steps[k + 1]()
-            if k == 3:
-                second_product("g", 1, 0, 1)
-            step()
+        for q in range(4):
+            stage("w2", 0, q)
+        for q in range(2):
+            stage("w2", 1, q)
+        for q in range(4):
+            vector_ab(0, q)
+        for q in range(2, 4):
+            stage("w2", 1, q)
+        fill = early_tile("ab_0_4", 53, [P, 2 * GROUP, PACK], F32)
+        to_stage = [("w3", 0, q, 1) for q in range(2, 4)] + [("w2", 0, 4, 1), ("w2", 0, 5, 1), ("w3", 1, 0, 1)]
+        for name, a, q in (("w2", 1, 4), ("w1", 1, 4), ("w3", 1, 4), ("w2", 0, 6), ("w1", 0, 6)):
+            to_stage = to_stage + [(name, a, q, 2), (name, a, q + 1, 2)]
+        on_vector = [(vector_h, 0, q) for q in range(2)] + [(vector_ab, 1, q) for q in range(4)] + [(vector_h, 1, q) for q in range(1, 4)]
+        for step in to_stage[:0]:
+            stage(*step)
+        for k, (product, a, q) in enumerate(on_vector):
+            product(a, q)
+            stage(*to_stage[0 + k])
+        to_stage = to_stage[0 + len(on_vector) :]
+        for q in range(2, 4):
+            gpsimd_h(0, q, 1)
+        gpsimd_h(1, 0, 1)
         quantise_h(0)
-        for g in range(2):
-            scalar_steps[8 + g]()
-            first_product("v", 0, 4 + g, 5 + g, fill[:, g * GROUP : (g + 1) * GROUP, :])
-        ab[0, 4] = (fill, 4)
-        scalar_steps[10]()
-        first_product("g", 1, 4, 6, after_first_half("ab_1_4", 57))
         x = {}
         for n in range(NT):
-            x[n] = early.tile([P, S], F32, name="x_%d" % n, align_bytes=64, offset=4 * n * KB)
+            x[n] = early_tile("x_%d" % n, 4 * n, [P, S], F32)
             nc.sync.dma_start(out=x[n][:], in_=x0[n * P : (n + 1) * P, :])
-        steps = [("w3", 0, 4), ("w3", 1, 4), ("w1", 0, 6), ("w1", 1, 6), ("w3", 0, 6), ("w3", 1, 6)]
-        for n in range(V_WEIGH):
+
+        for g in range(2):
+            vector_ab(0, 4 + g, fill[:, g * GROUP : (g + 1) * GROUP, :])
+            stage(*to_stage[g])
+        for g in range(2):
+            weigh_on_vector(0, g)
+            vector_h(0, 4 + g)
+            for step in to_stage[2 + 2 * g : 4 + 2 * g]:
+                stage(*step)
+        gpsimd_ab(1, 4, 2, early_tile("ab_1_4", 57, [P, 2 * GROUP, PACK], F32)[:])
+        gpsimd_h(1, 4, 2)
+        for n in range(2, VECTOR_WEIGHS):
             weigh_on_vector(0, n)
-            if n == 0:
-                stage("w3", 0, 4, 6)
+        for n in range(VECTOR_WEIGHS):
             place(0, n)
+        steps = [("w1", 0, 6), ("w1", 1, 6), ("w3", 0, 6), ("w3", 1, 6)]
         for k, (name, a, q) in enumerate(steps):
-            n = V_WEIGH + k - 1
-            if V_WEIGH <= n < NT - 1:
-                stage_scores(0, n, 12 + n)
-            if name == "w1":
-                stage("w2", a, q, q + 2, 17 + 3 * a)
-            if k > 0:
-                stage(name, a, q, q + 2)
-            if name == "w3":
-                second_product("g", a, q, q + 2)
-            elif a == 0:
-                first_product("g", a, q, q + 2, after_first_half("ab_0_6", 61))
-            else:
-                first_product("g", a, q, q + 2)
-            if V_WEIGH <= n < NT - 1:
+            n = VECTOR_WEIGHS + k
+            if n < NT - 1:
+                stage_scores(0, n, 48 + 2 * k)
                 weigh_on_gpsimd(0, n)
                 place(0, n)
-        stage_scores(0, 5, 19)
+            if k == 0:
+                gpsimd_ab(a, q, 2, early_tile("ab_0_6", 61, [P, 2 * GROUP, PACK], F32)[:])
+            elif name == "w1":
+                stage_pair("w2", a, q)
+                stage_pair(name, a, q)
+                gpsimd_ab(a, q, 2)
+            else:
+                stage_pair(name, a, q)
+                gpsimd_h(a, q, 2)
+        stage_scores(0, NT - 1, 54)
         quantise_h(1)
-        place(0, 5)
+        place(0, NT - 1)
         weigh_on_vector(1, 0)
         place(1, 0)
         for n in range(1, NT):
-            stage_scores(1, n, (22, 23, 27, 28, 25)[n - 1])
+            stage_scores(1, n, (16, 18, 20, 27, 22)[n - 1])
             weigh_on_gpsimd(1, n)
             place(1, n)
-        for n in range(NT):
+        for n in range(NT - 1):
             rows = slice(n * P, (n + 1) * P)
-            if n == NT - 1:
-                res = slots.tile([P, S], F32, name="res", align_bytes=64, offset=47 * KB)
-                for u in range(2):
-                    cols = slice(u * HALF, (u + 1) * HALF)
-                    nc.vector.scalar_tensor_tensor(res[:, cols], page[n][:, cols], 1.0, x[n][:, cols], ADD, MULT)
-                    nc.sync.dma_start(out=out[rows, cols], in_=res[:, cols])
-            else:
-                factor = slots.tile([P, S], F32, name="factor", tag="factor", bufs=2, align_bytes=64, offset=47 * KB)
-                pieces = 2 if n == NT - 2 else 1
-                for u in range(pieces):
-                    cols = slice(u * S // pieces, (u + 1) * S // pieces)
-                    nc.scalar.activation(factor[:, cols], page[n][:, cols], COPY, bias=1.0, scale=1.0)
-                    nc.gpsimd.tensor_tensor(x[n][:, cols], factor[:, cols], x[n][:, cols], MULT)
-                    nc.sync.dma_start(out=out[rows, cols], in_=x[n][:, cols])
+            factor = slots.tile([P, S], F32, name="factor", tag="factor", bufs=2, align_bytes=64, offset=24 * KB)
+            cuts = (0, S) if n < NT - 2 else (0, HALF, GPSIMD_CLOSES)
+            for c0, c1 in zip(cuts, cuts[1:]):
+                nc.scalar.activation(factor[:, c0:c1], page[n][:, c0:c1], COPY, bias=1.0, scale=1.0)
+                nc.gpsimd.tensor_tensor(x[n][:, c0:c1], factor[:, c0:c1], x[n][:, c0:c1], MULT)
+                nc.sync.dma_start(out=out[rows, c0:c1], in_=x[n][:, c0:c1])
+        closing = slots.tile([P, 2 * S - GPSIMD_CLOSES], F32, name="closing", align_bytes=64, offset=24 * KB)
+        done = 0
+        for n, c0, c1 in ((NT - 2, GPSIMD_CLOSES, S), (NT - 1, 0, HALF), (NT - 1, HALF, S - GROUP), (NT - 1, S - GROUP, S)):
+            res = closing[:, done : done + c1 - c0]
+            done = done + c1 - c0
+            nc.vector.scalar_tensor_tensor(res, page[n][:, c0:c1], 1.0, x[n][:, c0:c1], ADD, MULT)
+            nc.sync.dma_start(out=out[n * P : (n + 1) * P, c0:c1], in_=res)

@@ -116,6 +116,8 @@ def tile_list_marker_triple_interaction_kernel(
                 dst = grouped[:].rearrange("p t m i -> p m t i")[:, m0:m1]
                 if engine == "vector":
                     nc.vector.tensor_copy(out=dst, in_=src)
+                elif engine == "gpsimd":
+                    nc.gpsimd.tensor_scalar(dst, src, 1.0, 0.0, MULT, ADD)
                 else:
                     nc.scalar.copy(out=dst, in_=src)
             codes[name, a] = held.tile([P, PASS], U32, name="codes_%s_%d" % (name, a), align_bytes=64)
@@ -126,12 +128,13 @@ def tile_list_marker_triple_interaction_kernel(
                 in_=grouped[:].rearrange("p t m i -> p (t m i)"),
             )
 
-        quantise_weight("w1", 0, 0, [("scalar", first_halves[0], 0, P // 2), ("vector", first_halves[1], P // 2, P)])
-        gather_words(1, held.tile([P, HALF], U32, name="v_1", align_bytes=64))
+        quantise_weight("w1", 0, 0, [("vector", first_halves[0], 0, P // 2), ("vector", first_halves[1], P // 2, P)])
+        gather_words(1, slot_tile("v_1", 0, [P, HALF], U32))
         for slot, (name, a) in enumerate(raw):
             src = raw[name, a]
-            shares = [("scalar", src[:, :SCALAR_SHARE], 0, SCALAR_SHARE), ("vector", src[:, SCALAR_SHARE:], SCALAR_SHARE, P)]
-            quantise_weight(name, a, 4 + 4 * slot, shares)
+            other, cut = (("gpsimd", 72), ("gpsimd", 72), ("gpsimd", 72))[slot]
+            shares = [("scalar", src[:, :cut], 0, cut), (other, src[:, cut:], cut, P)]
+            quantise_weight(name, a, 4, shares)
 
         turn = {"vector": 0, "scalar": 0}
 
@@ -178,7 +181,7 @@ def tile_list_marker_triple_interaction_kernel(
             stage(name, a, q, 2)
             stage(name, a, q + 1)
 
-        hb = {0: early_tile("hb_0", 56, [P, PASSES, HALF, PACK], BF16), 1: early_tile("hb_1", 44, [P, PASSES, HALF, PACK], BF16)}
+        hb = {0: early_tile("hb_0", 37, [P, PASSES, HALF, PACK], BF16), 1: early_tile("hb_1", 44, [P, PASSES, HALF, PACK], BF16)}
 
         def h_rows(a, q, groups):
             half, first = divmod(q * GROUP, HALF)
@@ -242,7 +245,7 @@ def tile_list_marker_triple_interaction_kernel(
 
         def place(half, n):
             if half == 0:
-                page[n] = early_tile("page_%d" % n, 52 if n == 0 else 24 + 4 * n, [P, S], F32)
+                page[n] = early_tile("page_%d" % n, (52, 24, 28, 56, 60, 48)[n], [P, S], F32)
             window = page[n][:].indirect(idx2[:, half * HALF // 16 : (half + 1) * HALF // 16])
             if (half, n) in weighted:
                 nc.vector.tensor_copy(out=window, in_=weighted[half, n][:])
@@ -255,22 +258,26 @@ def tile_list_marker_triple_interaction_kernel(
             stage("w2", 1, q)
         for q in range(4):
             vector_ab(0, q)
+        fill = early_tile("ab_0_4", 52, [P, 2 * GROUP, PACK], F32)
+        for g in range(2):
+            stage("w2", 0, 4 + g)
+            vector_ab(0, 4 + g, fill[:, g * GROUP : (g + 1) * GROUP, :])
+        for q in range(4):
+            vector_h(0, q)
         for q in range(2, 4):
             stage("w2", 1, q)
-        fill = early_tile("ab_0_4", 53, [P, 2 * GROUP, PACK], F32)
-        to_stage = [("w3", 0, q, 1) for q in range(2, 4)] + [("w2", 0, 4, 1), ("w2", 0, 5, 1), ("w3", 1, 0, 1)]
-        for name, a, q in (("w2", 1, 4), ("w1", 1, 4), ("w3", 1, 4), ("w2", 0, 6), ("w1", 0, 6)):
+        for q in range(2):
+            vector_ab(1, q)
+        to_stage = [("w3", 1, q, 1) for q in range(1)] + [("w2", 1, 4, 2), ("w2", 1, 5, 2)]
+        for name, a, q in (("w1", 1, 4), ("w3", 1, 4), ("w2", 0, 6), ("w1", 0, 6)):
             to_stage = to_stage + [(name, a, q, 2), (name, a, q + 1, 2)]
-        on_vector = [(vector_h, 0, q) for q in range(2)] + [(vector_ab, 1, q) for q in range(4)] + [(vector_h, 1, q) for q in range(1, 4)]
-        for step in to_stage[:0]:
-            stage(*step)
+        on_vector = [(vector_ab, 1, q) for q in range(2, 4)] + [(vector_h, 1, q) for q in range(1, 4)]
         for k, (product, a, q) in enumerate(on_vector):
             product(a, q)
-            stage(*to_stage[0 + k])
-        to_stage = to_stage[0 + len(on_vector) :]
-        for q in range(2, 4):
-            gpsimd_h(0, q, 1)
-        gpsimd_h(1, 0, 1)
+            stage(*to_stage[k])
+        to_stage = to_stage[len(on_vector) :]
+        for q in range(1):
+            gpsimd_h(1, q, 1)
         quantise_h(0)
         x = {}
         for n in range(NT):
@@ -278,14 +285,15 @@ def tile_list_marker_triple_interaction_kernel(
             nc.sync.dma_start(out=x[n][:], in_=x0[n * P : (n + 1) * P, :])
 
         for g in range(2):
-            vector_ab(0, 4 + g, fill[:, g * GROUP : (g + 1) * GROUP, :])
+            vector_h(0, 4 + g)
             stage(*to_stage[g])
         for g in range(2):
             weigh_on_vector(0, g)
-            vector_h(0, 4 + g)
             for step in to_stage[2 + 2 * g : 4 + 2 * g]:
                 stage(*step)
-        gpsimd_ab(1, 4, 2, early_tile("ab_1_4", 57, [P, 2 * GROUP, PACK], F32)[:])
+        for step in to_stage[6:]:
+            stage(*step)
+        gpsimd_ab(1, 4, 2, early_tile("ab_1_4", 34, [P, 2 * GROUP, PACK], F32)[:])
         gpsimd_h(1, 4, 2)
         for n in range(2, VECTOR_WEIGHS):
             weigh_on_vector(0, n)
@@ -299,7 +307,7 @@ def tile_list_marker_triple_interaction_kernel(
                 weigh_on_gpsimd(0, n)
                 place(0, n)
             if k == 0:
-                gpsimd_ab(a, q, 2, early_tile("ab_0_6", 61, [P, 2 * GROUP, PACK], F32)[:])
+                gpsimd_ab(a, q, 2, early_tile("ab_0_6", 39, [P, 2 * GROUP, PACK], F32)[:])
             elif name == "w1":
                 stage_pair("w2", a, q)
                 stage_pair(name, a, q)

@@ -69,7 +69,7 @@ def tile_list_marker_triple_interaction_kernel(
         def load_weight(name, w, first, width, kb):
             tile = early_tile("raw_%s_%d" % (name, first), kb, [P, PACK, width], F32)
             nc.sync.dma_start(out=tile[:], in_=w[:, first : first + width].rearrange("(p i) c -> p i c", i=PACK))
-            return tile[:].rearrange("p i (m t) -> p m t i", t=PACK)
+            return tile[:].rearrange("p i (m t) -> p m i t", t=PACK)
 
         nc.sync.dma_start(idx[:], offs)
         nc.sync.dma_start(idx2[:], offs2)
@@ -113,7 +113,7 @@ def tile_list_marker_triple_interaction_kernel(
         def quantise_weight(name, a, kb, shares):
             grouped = slot_tile("grouped_%s_%d" % (name, a), kb, [P, PACK, P, PACK], BF16)
             for engine, src, m0, m1 in shares:
-                dst = grouped[:].rearrange("p t m i -> p m t i")[:, m0:m1]
+                dst = grouped[:].rearrange("p t m i -> p m i t")[:, m0:m1]
                 if engine == "vector":
                     nc.vector.tensor_copy(out=dst, in_=src)
                 elif engine == "gpsimd":

@@ -47,10 +47,9 @@ def tile_list_marker_triple_interaction_kernel(
             return slots.tile(shape, dtype, name=name, align_bytes=64, offset=kb * KB)
 
         def load_scale_rows(plane, rows):
-            for quad in range(4):
+            for r in range(4):
                 nc.sync.dma_start(
-                    out=plane[32 * quad : 32 * quad + 4].bitcast(I32),
-                    in_=rows[:, 4 * quad : 4 * quad + 4, :].rearrange("a r c -> r a c").bitcast(I32),
+                    out=plane[r:P:32].bitcast(I32), in_=rows[:, r:16:4, :].rearrange("a q c -> q a c").bitcast(I32)
                 )
 
         idx = held.tile([P, S // 16], U16, name="idx")

@@ -41,7 +41,7 @@ def tile_list_marker_triple_interaction_kernel(
         psum = ctx.enter_context(tc.psum_pool(name="psum", bufs=1))
 
         def early_tile(name, kb, shape, dtype):
-            return early.tile(shape, dtype, name=name, align_bytes=64, offset=kb * KB)
+            return early.tile(shape, dtype, name=name, align_bytes=64, offset=int(kb * KB))
 
         def slot_tile(name, kb, shape, dtype):
             return slots.tile(shape, dtype, name=name, align_bytes=64, offset=kb * KB)
@@ -54,15 +54,13 @@ def tile_list_marker_triple_interaction_kernel(
 
         idx = held.tile([P, S // 16], U16, name="idx")
         idx2 = held.tile([P, S // 16], U16, name="idx2")
-        tab_plane = early_tile("tab_plane", 48, [P, 1, T], U8)
-        w2_plane_raw = held.tile([P, 1, H], U8, name="w2_plane_raw", align_bytes=64)
-        w4_plane = held.tile([P, PASSES, N], U8, name="w4_plane", align_bytes=64)
-        nc.vector.memset(tab_plane[:].bitcast(I32), 0)
+        tab_plane = early_tile("tab_plane", 64, [P, T], U8)
+        w2_plane_raw = held.tile([P, H], U8, name="w2_plane_raw", align_bytes=64)
         nc.gpsimd.memset(w2_plane_raw[:].bitcast(I32), 0)
-        nc.gpsimd.memset(w4_plane[:].bitcast(I32), 0)
+        nc.vector.memset(tab_plane[:].bitcast(I32), 0)
 
         w2_raw = held.tile([P, H], U16, name="w2_raw", align_bytes=64)
-        tab = early_tile("tab", 32, [P, T], U32)
+        tab = early_tile("tab", 22, [P, T], U32)
         tab_rows = tab_words[0].rearrange("p t i -> p (t i)").bitcast(I32)
 
         def load_weight(name, w, first, width, kb):
@@ -73,39 +71,42 @@ def tile_list_marker_triple_interaction_kernel(
         nc.sync.dma_start(idx[:], offs)
         nc.sync.dma_start(idx2[:], offs2)
         nc.sync.dma_start(out=w2_raw[:].bitcast(I32), in_=w2_words[0].bitcast(I32))
-        load_scale_rows(w2_plane_raw, w2_scales)
+        nc.sync.dma_start(out=w2_plane_raw[0:P:8].bitcast(I32), in_=w2_scales[0].bitcast(I32))
+        nc.sync.dma_start(out=tab_plane[0:P:8].bitcast(I32), in_=tab_scales[0].bitcast(I32))
         nc.sync.dma_start(out=tab[:, : T // 2].bitcast(I32), in_=tab_rows[:, : T // 2])
-        load_scale_rows(tab_plane, tab_scales)
         nc.sync.dma_start(out=tab[:, T // 2 :].bitcast(I32), in_=tab_rows[:, T // 2 :])
-        first_halves = [load_weight("w1", w1, u * PASS // 2, PASS // 2, 4 * u) for u in range(2)]
-        raw = {}
-        for slot, (name, w, a) in enumerate((("w3", w3, 0), ("w1", w1, 1), ("w3", w3, 1))):
-            raw[name, a] = load_weight(name, w, a * PASS, PASS, 8 + 8 * slot)
-        load_scale_rows(w4_plane, w4_scales)
-        w4 = held.tile([P, PASSES, N], U32, name="w4", align_bytes=64)
-        nc.sync.dma_start(out=w4[:].bitcast(I32), in_=w4_words.rearrange("a p e i -> p a (e i)").bitcast(I32))
-        gain = held.tile([P, S], F32, name="gain", align_bytes=64)
-        nc.sync.dma_start(out=gain[:], in_=wgo)
+        first_halves = [load_weight("w1", w1, 0, PASS // 2, 0)]
 
         w2 = held.tile([P, H], U16, name="w2", align_bytes=64)
-        w2_plane = held.tile([P, H], U8, name="w2_plane", align_bytes=64)
+        both_planes = held.tile([P, S + H], U8, name="both_planes", align_bytes=64)
+        v_plane, w2_plane = both_planes[:, :S], both_planes[:, S:]
+        picked_plane = early_tile("picked_plane", 7.5, [P, S], U8)
+        nc.vector.tensor_copy(out=picked_plane[:], in_=tab_plane[:].indirect(idx[:]))
+        nc.vector.tensor_copy(
+            out=w2_plane.rearrange("p (a t m) -> p a t m", a=PASSES, t=PACK),
+            in_=w2_plane_raw[:].rearrange("p (a m t) -> p a t m", a=PASSES, t=PACK),
+        )
+        nc.vector.tensor_copy(out=v_plane.bitcast(I32), in_=picked_plane[:].bitcast(I32))
+        for r in range(1, 4):
+            nc.sync.dma_start(out=both_planes[r:P:32].bitcast(I32), in_=both_planes[8 * r : P : 32].bitcast(I32))
         nc.vector.tensor_copy(
             out=w2[:].rearrange("p (a t m) -> p a t m", a=PASSES, t=PACK),
             in_=w2_raw[:].rearrange("p (a m t) -> p a t m", a=PASSES, t=PACK),
         )
-        nc.vector.tensor_copy(
-            out=w2_plane[:].rearrange("p (a t m) -> p a t m", a=PASSES, t=PACK),
-            in_=w2_plane_raw[:, 0, :].rearrange("p (a m t) -> p a t m", a=PASSES, t=PACK),
-        )
-        v_plane = held.tile([P, S], U8, name="v_plane", align_bytes=64)
-        nc.vector.tensor_copy(out=v_plane[:], in_=tab_plane[:, 0, :].indirect(idx[:]))
-        v = {}
-
-        def gather_words(half, tile):
-            v[half] = tile
-            nc.vector.tensor_copy(out=tile[:], in_=tab[:].indirect(idx[:, half * HALF // 16 : (half + 1) * HALF // 16]))
-
-        gather_words(0, held.tile([P, HALF], U32, name="v_0", align_bytes=64))
+        first_halves.append(load_weight("w1", w1, PASS // 2, PASS // 2, 4))
+        v = held.tile([P, S], U32, name="v", align_bytes=64)
+        for c0, c1 in ((0, 256), (256, 512), (512, 1024)):
+            nc.vector.tensor_copy(out=v[:, c0:c1], in_=tab[:].indirect(idx[:, c0 // 16 : c1 // 16]))
+        raw = {}
+        for kb, name, w, a in ((8, "w3", w3, 0), (16, "w1", w1, 1), (36, "w3", w3, 1)):
+            raw[name, a] = load_weight(name, w, a * PASS, PASS, kb)
+        w4 = early_tile("w4", 24, [P, PASSES, N], U32)
+        nc.sync.dma_start(out=w4[:].bitcast(I32), in_=w4_words.rearrange("a p e i -> p a (e i)").bitcast(I32))
+        w4_plane = early_tile("w4_plane", 34, [P, PASSES, N], U8)
+        nc.gpsimd.memset(w4_plane[:].bitcast(I32), 0)
+        load_scale_rows(w4_plane, w4_scales)
+        gain = early_tile("gain", 30, [P, S], F32)
+        nc.sync.dma_start(out=gain[:], in_=wgo)
 
         codes, planes = {}, {}
 
@@ -128,7 +129,6 @@ def tile_list_marker_triple_interaction_kernel(
             )
 
         quantise_weight("w1", 0, 0, [("vector", first_halves[0], 0, P // 2), ("vector", first_halves[1], P // 2, P)])
-        gather_words(1, slot_tile("v_1", 0, [P, HALF], U32))
         for slot, (name, a) in enumerate(raw):
             src = raw[name, a]
             other, cut = (("gpsimd", 72), ("gpsimd", 72), ("gpsimd", 72))[slot]
@@ -144,7 +144,6 @@ def tile_list_marker_triple_interaction_kernel(
 
         def project(name, a, q, reader):
             acc = next_bank(reader, [P, PACK, GROUP])
-            half, first = divmod(q * GROUP, HALF)
             for t in range(PACK):
                 if name == "w2":
                     c0 = a * PASS + t * P
@@ -154,7 +153,7 @@ def tile_list_marker_triple_interaction_kernel(
                     lhsT_scale = planes[name, a][:, t * P : (t + 1) * P]
                 nc.tensor.matmul_mx(
                     out=acc[:, t, :], lhsT=lhsT, lhsT_scale=lhsT_scale,
-                    rhs=v[half][:, first : first + GROUP].bitcast(FP8X4), rhs_scale=v_plane[:, q * GROUP : (q + 1) * GROUP],
+                    rhs=v[:, q * GROUP : (q + 1) * GROUP].bitcast(FP8X4), rhs_scale=v_plane[:, q * GROUP : (q + 1) * GROUP],
                     start=True, stop=True,
                 )
             return acc[:].rearrange("p t j -> p j t")
@@ -180,7 +179,7 @@ def tile_list_marker_triple_interaction_kernel(
             stage(name, a, q, 2)
             stage(name, a, q + 1)
 
-        hb = {0: early_tile("hb_0", 37, [P, PASSES, HALF, PACK], BF16), 1: early_tile("hb_1", 44, [P, PASSES, HALF, PACK], BF16)}
+        hb = {0: early_tile("hb_0", 53, [P, PASSES, HALF, PACK], BF16), 1: early_tile("hb_1", 60, [P, PASSES, HALF, PACK], BF16)}
 
         def h_rows(a, q, groups):
             half, first = divmod(q * GROUP, HALF)
@@ -244,7 +243,7 @@ def tile_list_marker_triple_interaction_kernel(
 
         def place(half, n):
             if half == 0:
-                page[n] = early_tile("page_%d" % n, (52, 24, 28, 56, 60, 48)[n], [P, S], F32)
+                page[n] = early_tile("page_%d" % n, (68, 36, 40, 72, 76, 64)[n], [P, S], F32)
             window = page[n][:].indirect(idx2[:, half * HALF // 16 : (half + 1) * HALF // 16])
             if (half, n) in weighted:
                 nc.vector.tensor_copy(out=window, in_=weighted[half, n][:])
@@ -257,7 +256,7 @@ def tile_list_marker_triple_interaction_kernel(
             stage("w2", 1, q)
         for q in range(4):
             vector_ab(0, q)
-        fill = early_tile("ab_0_4", 52, [P, 2 * GROUP, PACK], F32)
+        fill = early_tile("ab_0_4", 68, [P, 2 * GROUP, PACK], F32)
         for g in range(2):
             stage("w2", 0, 4 + g)
             vector_ab(0, 4 + g, fill[:, g * GROUP : (g + 1) * GROUP, :])
@@ -292,7 +291,7 @@ def tile_list_marker_triple_interaction_kernel(
                 stage(*step)
         for step in to_stage[6:]:
             stage(*step)
-        gpsimd_ab(1, 4, 2, early_tile("ab_1_4", 34, [P, 2 * GROUP, PACK], F32)[:])
+        gpsimd_ab(1, 4, 2, early_tile("ab_1_4", 50, [P, 2 * GROUP, PACK], F32)[:])
         gpsimd_h(1, 4, 2)
         for n in range(2, VECTOR_WEIGHS):
             weigh_on_vector(0, n)
@@ -306,7 +305,7 @@ def tile_list_marker_triple_interaction_kernel(
                 weigh_on_gpsimd(0, n)
                 place(0, n)
             if k == 0:
-                gpsimd_ab(a, q, 2, early_tile("ab_0_6", 39, [P, 2 * GROUP, PACK], F32)[:])
+                gpsimd_ab(a, q, 2, early_tile("ab_0_6", 55, [P, 2 * GROUP, PACK], F32)[:])
             elif name == "w1":
                 stage_pair("w2", a, q)
                 stage_pair(name, a, q)

@@ -25,9 +25,11 @@ GROUP = 128
 HALF = S // 2
 NT = N // P
 KB = 1024
-SCALAR_SHARE = 64
+SHARE_0 = 40
+SHARE_1 = 96
+SHARE_2 = 32
 VECTOR_WEIGHS = 2
-GPSIMD_CLOSES = 768
+GPSIMD_CLOSES = 896
 
 
 def tile_list_marker_triple_interaction_kernel(
@@ -59,8 +61,8 @@ def tile_list_marker_triple_interaction_kernel(
         nc.gpsimd.memset(w2_plane_raw[:].bitcast(I32), 0)
         nc.vector.memset(tab_plane[:].bitcast(I32), 0)
 
-        w2_raw = held.tile([P, H], U16, name="w2_raw", align_bytes=64)
-        tab = early_tile("tab", 22, [P, T], U32)
+        w2_raw = early_tile("w2_raw", 16, [P, H], U16)
+        tab = early_tile("tab", 24, [P, T], U32)
         tab_rows = tab_words[0].rearrange("p t i -> p (t i)").bitcast(I32)
 
         def load_weight(name, w, first, width, kb):
@@ -77,18 +79,18 @@ def tile_list_marker_triple_interaction_kernel(
         nc.sync.dma_start(out=tab[:, T // 2 :].bitcast(I32), in_=tab_rows[:, T // 2 :])
         first_halves = [load_weight("w1", w1, 0, PASS // 2, 0)]
 
-        w2 = held.tile([P, H], U16, name="w2", align_bytes=64)
         both_planes = held.tile([P, S + H], U8, name="both_planes", align_bytes=64)
         v_plane, w2_plane = both_planes[:, :S], both_planes[:, S:]
         picked_plane = early_tile("picked_plane", 7.5, [P, S], U8)
-        nc.vector.tensor_copy(out=picked_plane[:], in_=tab_plane[:].indirect(idx[:]))
         nc.vector.tensor_copy(
             out=w2_plane.rearrange("p (a t m) -> p a t m", a=PASSES, t=PACK),
             in_=w2_plane_raw[:].rearrange("p (a m t) -> p a t m", a=PASSES, t=PACK),
         )
+        nc.vector.tensor_copy(out=picked_plane[:], in_=tab_plane[:].indirect(idx[:]))
         nc.vector.tensor_copy(out=v_plane.bitcast(I32), in_=picked_plane[:].bitcast(I32))
         for r in range(1, 4):
             nc.sync.dma_start(out=both_planes[r:P:32].bitcast(I32), in_=both_planes[8 * r : P : 32].bitcast(I32))
+        w2 = early_tile("w2", 65, [P, H], U16)
         nc.vector.tensor_copy(
             out=w2[:].rearrange("p (a t m) -> p a t m", a=PASSES, t=PACK),
             in_=w2_raw[:].rearrange("p (a m t) -> p a t m", a=PASSES, t=PACK),
@@ -103,37 +105,44 @@ def tile_list_marker_triple_interaction_kernel(
         w4 = early_tile("w4", 24, [P, PASSES, N], U32)
         nc.sync.dma_start(out=w4[:].bitcast(I32), in_=w4_words.rearrange("a p e i -> p a (e i)").bitcast(I32))
         w4_plane = early_tile("w4_plane", 34, [P, PASSES, N], U8)
-        nc.gpsimd.memset(w4_plane[:].bitcast(I32), 0)
+        nc.vector.memset(w4_plane[:].bitcast(I32), 0)
         load_scale_rows(w4_plane, w4_scales)
         gain = early_tile("gain", 30, [P, S], F32)
         nc.sync.dma_start(out=gain[:], in_=wgo)
 
         codes, planes = {}, {}
 
-        def quantise_weight(name, a, kb, shares):
-            grouped = slot_tile("grouped_%s_%d" % (name, a), kb, [P, PACK, P, PACK], BF16)
+        grouped = {}
+
+        def round_weight(name, a, tile, shares):
+            grouped[name, a] = tile.rearrange("p (t m i) -> p t m i", t=PACK, i=PACK)
             for engine, src, m0, m1 in shares:
-                dst = grouped[:].rearrange("p t m i -> p m i t")[:, m0:m1]
+                dst = grouped[name, a].rearrange("p t m i -> p m i t")[:, m0:m1]
                 if engine == "vector":
                     nc.vector.tensor_copy(out=dst, in_=src)
                 elif engine == "gpsimd":
                     nc.gpsimd.tensor_scalar(dst, src, 1.0, 0.0, MULT, ADD)
                 else:
                     nc.scalar.copy(out=dst, in_=src)
-            codes[name, a] = held.tile([P, PASS], U32, name="codes_%s_%d" % (name, a), align_bytes=64)
+
+        def quantise_weight(name, a, kb=None):
+            if kb is None:
+                codes[name, a] = held.tile([P, PASS], U32, name="codes_%s_%d" % (name, a), align_bytes=64)
+            else:
+                codes[name, a] = slot_tile("codes_%s_%d" % (name, a), kb, [P, PASS], U32)
             planes[name, a] = held.tile([P, PASS], U8, name="plane_%s_%d" % (name, a), align_bytes=64)
             nc.vector.quantize_mx(
                 out=codes[name, a][:].bitcast(FP8X4),
                 scales=planes[name, a][:],
-                in_=grouped[:].rearrange("p t m i -> p (t m i)"),
+                in_=grouped[name, a].rearrange("p t m i -> p (t m i)"),
             )
 
-        quantise_weight("w1", 0, 0, [("vector", first_halves[0], 0, P // 2), ("vector", first_halves[1], P // 2, P)])
-        for slot, (name, a) in enumerate(raw):
-            src = raw[name, a]
-            other, cut = (("gpsimd", 72), ("gpsimd", 72), ("gpsimd", 72))[slot]
-            shares = [("scalar", src[:, :cut], 0, cut), (other, src[:, cut:], cut, P)]
-            quantise_weight(name, a, 4, shares)
+        round_weight(
+            "w1", 0, slot_tile("grouped_w1_0", 0, [P, PACK * PASS], BF16)[:],
+            [("scalar", first_halves[0][:, :SHARE_0], 0, SHARE_0), ("gpsimd", first_halves[0][:, SHARE_0:], SHARE_0, P // 2), ("vector", first_halves[1], P // 2, P)],
+        )
+        quantise_weight("w1", 0)
+        round_weight("w3", 0, slot_tile("grouped_w3_0", 2, [P, PACK * PASS], BF16)[:], [("gpsimd", raw["w3", 0], 0, P)])
 
         turn = {"vector": 0, "scalar": 0}
 
@@ -160,65 +169,73 @@ def tile_list_marker_triple_interaction_kernel(
 
         staged, ab = {}, {}
 
-        def staging_tile(name, a, q0, groups):
-            shape = [P, groups * GROUP, PACK]
-            if name == "w2":
-                tile = slot_tile("b_%d_%d" % (a, q0), 16 + 16 * a + 2 * q0, shape, F32)
-            else:
-                tile = held.tile(shape, F32, name="ring", tag="ring", bufs=5, align_bytes=64)
-            for g in range(groups):
-                staged[name, a, q0 + g] = tile[:, g * GROUP : (g + 1) * GROUP, :]
+        def stage(name, a, q0, groups, kb):
+            tile = slot_tile("staged_%s_%d_%d" % (name, a, q0), kb, [P, groups * GROUP, PACK], F32)
             staged[name, a, q0, groups] = tile[:]
+            for g in range(groups):
+                staged[name, a, q0 + g, 1] = tile[:, g * GROUP : (g + 1) * GROUP, :]
+                nc.scalar.copy(out=staged[name, a, q0 + g, 1], in_=project(name, a, q0 + g, "scalar"))
 
-        def stage(name, a, q, groups=1):
-            if (name, a, q) not in staged:
-                staging_tile(name, a, q, groups)
-            nc.scalar.copy(out=staged[name, a, q], in_=project(name, a, q, "scalar"))
+        def stage_b_pair(a, q, kb):
+            tile = slot_tile("b_%d_%d" % (a, q), kb, [P, 2, 2 * GROUP, 2], F32)
+            cols = slice(q * GROUP, (q + 2) * GROUP)
+            for u in range(2):
+                acc = next_bank("scalar", [P, 2, 2 * GROUP])
+                for r in range(2):
+                    c0 = a * PASS + (2 * u + r) * P
+                    nc.tensor.matmul_mx(
+                        out=acc[:, r, :], lhsT=w2[:, c0 : c0 + P].bitcast(FP4X4), lhsT_scale=w2_plane[:, c0 : c0 + P],
+                        rhs=v[:, cols].bitcast(FP8X4), rhs_scale=v_plane[:, cols], start=True, stop=True,
+                    )
+                nc.scalar.copy(out=tile[:, u], in_=acc[:].rearrange("p r j -> p j r"))
+            for g in range(2):
+                staged["w2", a, q + g, 1] = tile[:].rearrange("p u j r -> p j u r")[:, g * GROUP : (g + 1) * GROUP]
 
-        def stage_pair(name, a, q):
-            stage(name, a, q, 2)
-            stage(name, a, q + 1)
+        pieces = {}
 
-        hb = {0: early_tile("hb_0", 53, [P, PASSES, HALF, PACK], BF16), 1: early_tile("hb_1", 60, [P, PASSES, HALF, PACK], BF16)}
+        def h_piece(name, kb, a, q, groups):
+            tile = early_tile(name, kb, [P, groups * GROUP, PACK], BF16)
+            for g in range(groups):
+                pieces[a, q + g] = (tile, g)
 
         def h_rows(a, q, groups):
-            half, first = divmod(q * GROUP, HALF)
-            return hb[half][:, a, first : first + groups * GROUP, :]
+            tile, g = pieces[a, q]
+            return tile[:, g * GROUP : (g + groups) * GROUP, :]
 
-        def vector_ab(a, q, dst=None):
-            b = staged["w2", a, q]
-            ab[a, q] = b if dst is None else dst
-            nc.vector.tensor_tensor(ab[a, q], project("w1", a, q, "vector"), b, MULT)
+        def in_pairs(rows):
+            return rows.rearrange("p j (u r) -> p j u r", u=2)
+
+        def vector_ab(a, q, dst):
+            ab[a, q] = dst
+            nc.vector.tensor_tensor(in_pairs(dst), in_pairs(project("w1", a, q, "vector")), staged["w2", a, q, 1], MULT)
 
         def vector_h(a, q):
             nc.vector.tensor_tensor(h_rows(a, q, 1), project("w3", a, q, "vector"), ab[a, q], MULT)
 
-        def gpsimd_ab(a, q, groups, dst=None):
-            b = staged["w2", a, q, groups]
-            ab[a, q] = b if dst is None else dst
-            nc.gpsimd.tensor_tensor(ab[a, q], staged["w1", a, q, groups], b, MULT)
-
-        def gpsimd_h(a, q, groups):
-            nc.gpsimd.tensor_tensor(h_rows(a, q, groups), staged["w3", a, q, groups], ab[a, q], MULT)
+        def gpsimd_h(a, q, groups, both):
+            nc.gpsimd.tensor_tensor(h_rows(a, q, groups), staged["w3", a, q, groups], both, MULT)
 
         hq, hs = {}, {}
 
-        def quantise_h(half):
-            hq[half] = held.tile([P, PASSES, HALF], U32, name="hq_%d" % half, align_bytes=64)
-            hs[half] = held.tile([P, PASSES, HALF], U8, name="hs_%d" % half, align_bytes=64)
-            nc.vector.quantize_mx(
-                out=hq[half][:].rearrange("p a j -> p (a j)").bitcast(FP8X4), scales=hs[half][:].rearrange("p a j -> p (a j)"),
-                in_=hb[half][:].rearrange("p a j t -> p (a j t)"),
-            )
+        def quantise_h(half, a, kb, calls):
+            hq[half, a] = slot_tile("hq_%d_%d" % (half, a), kb, [P, HALF], U32)
+            hs[half, a] = held.tile([P, HALF], U8, name="hs_%d_%d" % (half, a), align_bytes=64)
+            for q, groups in calls:
+                cols = slice(q % 4 * GROUP, (q % 4 + groups) * GROUP)
+                nc.vector.quantize_mx(
+                    out=hq[half, a][:, cols].bitcast(FP8X4), scales=hs[half, a][:, cols],
+                    in_=h_rows(a, q, groups).rearrange("p j t -> p (j t)"),
+                )
 
-        def scores(half, n, reader):
-            acc = next_bank(reader, [P, HALF])
+        def scores(half, n, reader, cols=slice(0, HALF)):
+            acc = next_bank(reader, [P, cols.stop - cols.start])
             rows = slice(n * P, (n + 1) * P)
-            for a in range(PASSES):
+            order = (0, 1) if n == 0 else (1, 0)
+            for a in order:
                 nc.tensor.matmul_mx(
                     out=acc[:], lhsT=w4[:, a, rows].bitcast(FP8X4), lhsT_scale=w4_plane[:, a, rows],
-                    rhs=hq[half][:, a, :].bitcast(FP8X4), rhs_scale=hs[half][:, a, :],
-                    start=(a == 0), stop=(a == PASSES - 1),
+                    rhs=hq[half, a][:, cols].bitcast(FP8X4), rhs_scale=hs[half, a][:, cols],
+                    start=(a == order[0]), stop=(a == order[1]),
                 )
             return acc[:]
 
@@ -227,100 +244,105 @@ def tile_list_marker_triple_interaction_kernel(
 
         y, weighted = {}, {}
 
-        def weigh_on_vector(half, n):
-            weighted[half, n] = held.tile([P, HALF], F32, name="weighted", tag="weighted", bufs=8)
-            nc.vector.tensor_tensor(weighted[half, n][:], scores(half, n, "vector"), half_gain(half), MULT)
-
         def stage_scores(half, n, kb):
             y[half, n] = slot_tile("y_%d_%d" % (half, n), kb, [P, HALF], F32)
             nc.scalar.copy(out=y[half, n][:], in_=scores(half, n, "scalar"))
 
         def weigh_on_gpsimd(half, n):
-            weighted[half, n] = held.tile([P, HALF], F32, name="weighted", tag="weighted", bufs=8)
+            weighted[half, n] = held.tile([P, HALF], F32, name="weighted", tag="weighted", bufs=4)
             nc.gpsimd.tensor_tensor(weighted[half, n][:], y[half, n][:], half_gain(half), MULT)
+
+        def weigh_pair_on_gpsimd(half, n, kb):
+            both = slot_tile("y_%d_%d" % (half, n), kb, [P, 2, HALF], F32)
+            for g in range(2):
+                nc.scalar.copy(out=both[:, g, :], in_=scores(half, n + g, "scalar"))
+            pair = held.tile([P, 2, HALF], F32, name="weighted_pair", tag="weighted_pair", bufs=3)
+            nc.gpsimd.tensor_tensor(pair[:], both[:], half_gain(half).unsqueeze(1).to_broadcast([P, 2, HALF]), MULT)
+            weighted[half, n], weighted[half, n + 1] = pair[:, 0, :], pair[:, 1, :]
 
         page = {}
 
         def place(half, n):
             if half == 0:
-                page[n] = early_tile("page_%d" % n, (68, 36, 40, 72, 76, 64)[n], [P, S], F32)
+                page[n] = early_tile("page_%d" % n, (70, 0, 4, 74, 78, 60)[n], [P, S], F32)
             window = page[n][:].indirect(idx2[:, half * HALF // 16 : (half + 1) * HALF // 16])
             if (half, n) in weighted:
                 nc.vector.tensor_copy(out=window, in_=weighted[half, n][:])
             else:
                 nc.vector.tensor_tensor(window, y[half, n][:], half_gain(half), MULT)
 
-        for q in range(4):
-            stage("w2", 0, q)
+        def shared(src, cut):
+            return [("scalar", src[:, :cut], 0, cut), ("gpsimd", src[:, cut:], cut, P)]
+
+        ab_0 = slot_tile("ab_0", 76, [P, S, PACK], F32)
+        for q in (0, 2):
+            stage_b_pair(0, q, 16 + 2 * q)
+        for q in range(8):
+            if q in (1, 3):
+                stage_b_pair(0, q + 3, 22 + 2 * q)
+            vector_ab(0, q, ab_0[:, q * GROUP : (q + 1) * GROUP, :])
+        round_weight("w1", 1, early_tile("grouped_w1_1", 53, [P, PACK * PASS], BF16)[:], shared(raw["w1", 1], SHARE_1))
+        quantise_weight("w3", 0, 28)
+        quantise_weight("w1", 1, 30)
+        for q in (0, 2):
+            stage_b_pair(1, q, 32 + 2 * q)
+        round_weight("w3", 1, early_tile("grouped_w3_1", 53, [P, PACK * PASS], BF16)[:], shared(raw["w3", 1], SHARE_2))
+        h_piece("h_0_0", 61, 0, 0, 2)
+        h_piece("h_1_0", 57, 1, 0, 4)
         for q in range(2):
-            stage("w2", 1, q)
-        for q in range(4):
-            vector_ab(0, q)
-        fill = early_tile("ab_0_4", 68, [P, 2 * GROUP, PACK], F32)
-        for g in range(2):
-            stage("w2", 0, 4 + g)
-            vector_ab(0, 4 + g, fill[:, g * GROUP : (g + 1) * GROUP, :])
-        for q in range(4):
             vector_h(0, q)
-        for q in range(2, 4):
-            stage("w2", 1, q)
-        for q in range(2):
-            vector_ab(1, q)
-        to_stage = [("w3", 1, q, 1) for q in range(1)] + [("w2", 1, 4, 2), ("w2", 1, 5, 2)]
-        for name, a, q in (("w1", 1, 4), ("w3", 1, 4), ("w2", 0, 6), ("w1", 0, 6)):
-            to_stage = to_stage + [(name, a, q, 2), (name, a, q + 1, 2)]
-        on_vector = [(vector_ab, 1, q) for q in range(2, 4)] + [(vector_h, 1, q) for q in range(1, 4)]
-        for k, (product, a, q) in enumerate(on_vector):
-            product(a, q)
-            stage(*to_stage[k])
-        to_stage = to_stage[len(on_vector) :]
-        for q in range(1):
-            gpsimd_h(1, q, 1)
-        quantise_h(0)
+        for q in range(4):
+            vector_ab(1, q, slot_tile("ab_1_%d" % q, 8 + 2 * q, [P, GROUP, PACK], F32)[:])
+        stage("w2", 1, 4, 1, 40)
+        staged["w2", 1, 4, 1] = in_pairs(staged["w2", 1, 4, 1])
+        stage("w3", 0, 2, 2, 42)
+        quantise_weight("w3", 1, 38)
+        h_piece("h_0_2", 55, 0, 2, 2)
+        gpsimd_h(0, 2, 2, ab_0[:, 2 * GROUP : 4 * GROUP, :])
+        ab_1_4 = early_tile("ab_1_4", 46, [P, 4 * GROUP, PACK], F32)
+        vector_ab(1, 4, ab_1_4[:, :GROUP, :])
+        for q in range(4):
+            vector_h(1, q)
+        stage("w3", 0, 5, 3, 46)
+        quantise_h(0, 0, 12, [(0, 2), (2, 2)])
+        quantise_h(0, 1, 14, [(0, 2), (2, 2)])
+        h_piece("h_second", 56, 0, 4, 8)
+        for g in range(4):
+            pieces[1, 4 + g] = pieces[0, 8 + g]
         x = {}
         for n in range(NT):
-            x[n] = early_tile("x_%d" % n, 4 * n, [P, S], F32)
+            x[n] = early_tile("x_%d" % n, (8, 12, 16, 20, 36, 40)[n], [P, S], F32)
             nc.sync.dma_start(out=x[n][:], in_=x0[n * P : (n + 1) * P, :])
 
+        weighted[0, 0] = held.tile([P, HALF], F32, name="weighted", tag="weighted", bufs=4)
         for g in range(2):
-            vector_h(0, 4 + g)
-            stage(*to_stage[g])
-        for g in range(2):
-            weigh_on_vector(0, g)
-            for step in to_stage[2 + 2 * g : 4 + 2 * g]:
-                stage(*step)
-        for step in to_stage[6:]:
-            stage(*step)
-        gpsimd_ab(1, 4, 2, early_tile("ab_1_4", 50, [P, 2 * GROUP, PACK], F32)[:])
-        gpsimd_h(1, 4, 2)
-        for n in range(2, VECTOR_WEIGHS):
-            weigh_on_vector(0, n)
-        for n in range(VECTOR_WEIGHS):
+            cols = slice(g * HALF // 2, (g + 1) * HALF // 2)
+            nc.vector.tensor_tensor(weighted[0, 0][:, cols], scores(0, 0, "vector", cols), gain[:, cols], MULT)
+            if g == 0:
+                vector_h(0, 4)
+        place(0, 0)
+        gpsimd_h(0, 5, 3, ab_0[:, 5 * GROUP :, :])
+        stage_scores(0, 1, 72)
+        weigh_on_gpsimd(0, 1)
+        weigh_pair_on_gpsimd(0, 2, 52)
+        stage("w2", 1, 5, 3, 66)
+        stage("w1", 1, 5, 3, 46)
+        nc.gpsimd.tensor_tensor(ab_1_4[:, GROUP:, :], staged["w1", 1, 5, 3], staged["w2", 1, 5, 3], MULT)
+        weigh_pair_on_gpsimd(0, 4, 62)
+        for n in range(1, NT - 1):
             place(0, n)
-        steps = [("w1", 0, 6), ("w1", 1, 6), ("w3", 0, 6), ("w3", 1, 6)]
-        for k, (name, a, q) in enumerate(steps):
-            n = VECTOR_WEIGHS + k
-            if n < NT - 1:
-                stage_scores(0, n, 48 + 2 * k)
-                weigh_on_gpsimd(0, n)
-                place(0, n)
-            if k == 0:
-                gpsimd_ab(a, q, 2, early_tile("ab_0_6", 55, [P, 2 * GROUP, PACK], F32)[:])
-            elif name == "w1":
-                stage_pair("w2", a, q)
-                stage_pair(name, a, q)
-                gpsimd_ab(a, q, 2)
-            else:
-                stage_pair(name, a, q)
-                gpsimd_h(a, q, 2)
-        stage_scores(0, NT - 1, 54)
-        quantise_h(1)
+        stage("w3", 1, 4, 4, 54)
+        gpsimd_h(1, 4, 4, ab_1_4[:])
+        quantise_h(1, 0, 55, [(4, 4)])
+        quantise_h(1, 1, 57, [(4, 4)])
         place(0, NT - 1)
-        weigh_on_vector(1, 0)
-        place(1, 0)
-        for n in range(1, NT):
-            stage_scores(1, n, (16, 18, 20, 27, 22)[n - 1])
-            weigh_on_gpsimd(1, n)
+        stage_scores(1, 0, 42)
+        weigh_on_gpsimd(1, 0)
+        weigh_pair_on_gpsimd(1, 1, 18)
+        weigh_pair_on_gpsimd(1, 3, 26)
+        stage_scores(1, 5, 22)
+        weigh_on_gpsimd(1, 5)
+        for n in range(NT):
             place(1, n)
         for n in range(NT - 1):
             rows = slice(n * P, (n + 1) * P)

@@ -25,10 +25,9 @@ GROUP = 128
 HALF = S // 2
 NT = N // P
 KB = 1024
-SHARE_0 = 40
-SHARE_1 = 96
-SHARE_2 = 32
-VECTOR_WEIGHS = 2
+GPSIMD_ROUNDS_W3_0 = 24
+GPSIMD_ROUNDS_W1_1 = 44
+VECTOR_ROUNDS_W3_1 = 72
 GPSIMD_CLOSES = 896
 
 
@@ -38,37 +37,27 @@ def tile_list_marker_triple_interaction_kernel(
     nc = tc.nc
     with ExitStack() as ctx:
         held = ctx.enter_context(tc.tile_pool(name="held", bufs=1))
-        early = ctx.enter_context(tc.tile_pool(name="early", bufs=1))
-        slots = ctx.enter_context(tc.tile_pool(name="slots", bufs=1))
+        space = ctx.enter_context(tc.tile_pool(name="space", bufs=1))
         psum = ctx.enter_context(tc.psum_pool(name="psum", bufs=1))
 
-        def early_tile(name, kb, shape, dtype):
-            return early.tile(shape, dtype, name=name, align_bytes=64, offset=int(kb * KB))
+        def kept(name, shape, dtype):
+            return held.tile(shape, dtype, name=name, align_bytes=64)
 
-        def slot_tile(name, kb, shape, dtype):
-            return slots.tile(shape, dtype, name=name, align_bytes=64, offset=kb * KB)
+        def placed(name, kb, shape, dtype):
+            return space.tile(shape, dtype, name=name, align_bytes=64, offset=int(kb * KB))
 
-        def load_scale_rows(plane, rows):
-            for r in range(4):
-                nc.sync.dma_start(
-                    out=plane[r:P:32].bitcast(I32), in_=rows[:, r:16:4, :].rearrange("a q c -> q a c").bitcast(I32)
-                )
+        def cols(q, groups=1):
+            return slice(q * GROUP, (q + groups) * GROUP)
 
         idx = held.tile([P, S // 16], U16, name="idx")
         idx2 = held.tile([P, S // 16], U16, name="idx2")
-        tab_plane = early_tile("tab_plane", 64, [P, T], U8)
-        w2_plane_raw = held.tile([P, H], U8, name="w2_plane_raw", align_bytes=64)
-        nc.gpsimd.memset(w2_plane_raw[:].bitcast(I32), 0)
+        tab_plane = placed("tab_plane", 44, [P, T], U8)
+        w2_plane_raw = kept("w2_plane_raw", [P, H], U8)
+        nc.vector.memset(w2_plane_raw[:].bitcast(I32), 0)
         nc.vector.memset(tab_plane[:].bitcast(I32), 0)
-
-        w2_raw = early_tile("w2_raw", 16, [P, H], U16)
-        tab = early_tile("tab", 24, [P, T], U32)
+        w2_raw = placed("w2_raw", 11, [P, H], U16)
+        tab = placed("tab", 24, [P, T], U32)
         tab_rows = tab_words[0].rearrange("p t i -> p (t i)").bitcast(I32)
-
-        def load_weight(name, w, first, width, kb):
-            tile = early_tile("raw_%s_%d" % (name, first), kb, [P, PACK, width], F32)
-            nc.sync.dma_start(out=tile[:], in_=w[:, first : first + width].rearrange("(p i) c -> p i c", i=PACK))
-            return tile[:].rearrange("p i (m t) -> p m i t", t=PACK)
 
         nc.sync.dma_start(idx[:], offs)
         nc.sync.dma_start(idx2[:], offs2)
@@ -77,11 +66,16 @@ def tile_list_marker_triple_interaction_kernel(
         nc.sync.dma_start(out=tab_plane[0:P:8].bitcast(I32), in_=tab_scales[0].bitcast(I32))
         nc.sync.dma_start(out=tab[:, : T // 2].bitcast(I32), in_=tab_rows[:, : T // 2])
         nc.sync.dma_start(out=tab[:, T // 2 :].bitcast(I32), in_=tab_rows[:, T // 2 :])
-        first_halves = [load_weight("w1", w1, 0, PASS // 2, 0)]
 
-        both_planes = held.tile([P, S + H], U8, name="both_planes", align_bytes=64)
+        def load_weight(name, w, first, width, kb):
+            tile = placed("raw_%s_%d" % (name, first), kb, [P, PACK, width], F32)
+            nc.sync.dma_start(out=tile[:], in_=w[:, first : first + width].rearrange("(p i) c -> p i c", i=PACK))
+            return tile[:].rearrange("p i (m t) -> p m i t", t=PACK)
+
+        w1_0 = [load_weight("w1", w1, 0, PASS // 2, 0)]
+        both_planes = kept("both_planes", [P, S + H], U8)
         v_plane, w2_plane = both_planes[:, :S], both_planes[:, S:]
-        picked_plane = early_tile("picked_plane", 7.5, [P, S], U8)
+        picked_plane = placed("picked_plane", 7.5, [P, S], U8)
         nc.vector.tensor_copy(
             out=w2_plane.rearrange("p (a t m) -> p a t m", a=PASSES, t=PACK),
             in_=w2_plane_raw[:].rearrange("p (a m t) -> p a t m", a=PASSES, t=PACK),
@@ -90,59 +84,47 @@ def tile_list_marker_triple_interaction_kernel(
         nc.vector.tensor_copy(out=v_plane.bitcast(I32), in_=picked_plane[:].bitcast(I32))
         for r in range(1, 4):
             nc.sync.dma_start(out=both_planes[r:P:32].bitcast(I32), in_=both_planes[8 * r : P : 32].bitcast(I32))
-        w2 = early_tile("w2", 65, [P, H], U16)
+        w2 = placed("w2", 45, [P, H], U16)
         nc.vector.tensor_copy(
             out=w2[:].rearrange("p (a t m) -> p a t m", a=PASSES, t=PACK),
             in_=w2_raw[:].rearrange("p (a m t) -> p a t m", a=PASSES, t=PACK),
         )
-        first_halves.append(load_weight("w1", w1, PASS // 2, PASS // 2, 4))
-        v = held.tile([P, S], U32, name="v", align_bytes=64)
+
+        w1_0.append(load_weight("w1", w1, PASS // 2, PASS // 2, 4))
+        w3_0 = [load_weight("w3", w3, u * PASS // 2, PASS // 2, 8 + 4 * u) for u in range(2)]
+        v = kept("v", [P, S], U32)
         for c0, c1 in ((0, 256), (256, 512), (512, 1024)):
             nc.vector.tensor_copy(out=v[:, c0:c1], in_=tab[:].indirect(idx[:, c0 // 16 : c1 // 16]))
-        raw = {}
-        for kb, name, w, a in ((8, "w3", w3, 0), (16, "w1", w1, 1), (36, "w3", w3, 1)):
-            raw[name, a] = load_weight(name, w, a * PASS, PASS, kb)
-        w4 = early_tile("w4", 24, [P, PASSES, N], U32)
+        w1_1 = load_weight("w1", w1, PASS, PASS, 16.5)
+        w3_1 = load_weight("w3", w3, PASS, PASS, 36)
+        w4 = placed("w4", 24.5, [P, PASSES, N], U32)
         nc.sync.dma_start(out=w4[:].bitcast(I32), in_=w4_words.rearrange("a p e i -> p a (e i)").bitcast(I32))
-        w4_plane = early_tile("w4_plane", 34, [P, PASSES, N], U8)
-        nc.vector.memset(w4_plane[:].bitcast(I32), 0)
-        load_scale_rows(w4_plane, w4_scales)
-        gain = early_tile("gain", 30, [P, S], F32)
+        gain = placed("gain", 30.5, [P, S], F32)
         nc.sync.dma_start(out=gain[:], in_=wgo)
 
-        codes, planes = {}, {}
+        grouped, codes, planes = {}, {}, {}
 
-        grouped = {}
-
-        def round_weight(name, a, tile, shares):
-            grouped[name, a] = tile.rearrange("p (t m i) -> p t m i", t=PACK, i=PACK)
-            for engine, src, m0, m1 in shares:
-                dst = grouped[name, a].rearrange("p t m i -> p m i t")[:, m0:m1]
-                if engine == "vector":
-                    nc.vector.tensor_copy(out=dst, in_=src)
-                elif engine == "gpsimd":
-                    nc.gpsimd.tensor_scalar(dst, src, 1.0, 0.0, MULT, ADD)
-                else:
-                    nc.scalar.copy(out=dst, in_=src)
-
-        def quantise_weight(name, a, kb=None):
-            if kb is None:
-                codes[name, a] = held.tile([P, PASS], U32, name="codes_%s_%d" % (name, a), align_bytes=64)
+        def round_rows(engine, name, a, kb, src, m0):
+            if (name, a) not in grouped:
+                tile = placed("grouped_%s_%d" % (name, a), kb, [P, PACK * PASS], BF16)
+                grouped[name, a] = tile[:].rearrange("p (t m i) -> p t m i", t=PACK, i=PACK)
+            dst = grouped[name, a].rearrange("p t m i -> p m i t")[:, m0 : m0 + src.shape[1]]
+            if engine == "vector":
+                nc.vector.tensor_copy(out=dst, in_=src)
+            elif engine == "gpsimd":
+                walk = "p m i t -> p t m i"
+                nc.gpsimd.tensor_scalar(dst.rearrange(walk), src.rearrange(walk), 1.0, 0.0, MULT, ADD)
             else:
-                codes[name, a] = slot_tile("codes_%s_%d" % (name, a), kb, [P, PASS], U32)
-            planes[name, a] = held.tile([P, PASS], U8, name="plane_%s_%d" % (name, a), align_bytes=64)
+                nc.scalar.copy(out=dst, in_=src)
+
+        def quantise_weight(name, a):
+            codes[name, a] = kept("codes_%s_%d" % (name, a), [P, PASS], U32)
+            planes[name, a] = kept("plane_%s_%d" % (name, a), [P, PASS], U8)
             nc.vector.quantize_mx(
                 out=codes[name, a][:].bitcast(FP8X4),
                 scales=planes[name, a][:],
                 in_=grouped[name, a].rearrange("p t m i -> p (t m i)"),
             )
-
-        round_weight(
-            "w1", 0, slot_tile("grouped_w1_0", 0, [P, PACK * PASS], BF16)[:],
-            [("scalar", first_halves[0][:, :SHARE_0], 0, SHARE_0), ("gpsimd", first_halves[0][:, SHARE_0:], SHARE_0, P // 2), ("vector", first_halves[1], P // 2, P)],
-        )
-        quantise_weight("w1", 0)
-        round_weight("w3", 0, slot_tile("grouped_w3_0", 2, [P, PACK * PASS], BF16)[:], [("gpsimd", raw["w3", 0], 0, P)])
 
         turn = {"vector": 0, "scalar": 0}
 
@@ -162,200 +144,179 @@ def tile_list_marker_triple_interaction_kernel(
                     lhsT_scale = planes[name, a][:, t * P : (t + 1) * P]
                 nc.tensor.matmul_mx(
                     out=acc[:, t, :], lhsT=lhsT, lhsT_scale=lhsT_scale,
-                    rhs=v[:, q * GROUP : (q + 1) * GROUP].bitcast(FP8X4), rhs_scale=v_plane[:, q * GROUP : (q + 1) * GROUP],
-                    start=True, stop=True,
+                    rhs=v[:, cols(q)].bitcast(FP8X4), rhs_scale=v_plane[:, cols(q)], start=True, stop=True,
                 )
             return acc[:].rearrange("p t j -> p j t")
 
-        staged, ab = {}, {}
+        spans = {}
 
-        def stage(name, a, q0, groups, kb):
-            tile = slot_tile("staged_%s_%d_%d" % (name, a, q0), kb, [P, groups * GROUP, PACK], F32)
-            staged[name, a, q0, groups] = tile[:]
+        def span(kind, a, q0, groups, kb, dtype):
+            tile = placed("%s_%d_%d" % (kind, a, q0), kb, [P, groups * GROUP, PACK], dtype)
             for g in range(groups):
-                staged[name, a, q0 + g, 1] = tile[:, g * GROUP : (g + 1) * GROUP, :]
-                nc.scalar.copy(out=staged[name, a, q0 + g, 1], in_=project(name, a, q0 + g, "scalar"))
+                spans[kind, a, q0 + g] = (tile, g)
 
-        def stage_b_pair(a, q, kb):
-            tile = slot_tile("b_%d_%d" % (a, q), kb, [P, 2, 2 * GROUP, 2], F32)
-            cols = slice(q * GROUP, (q + 2) * GROUP)
-            for u in range(2):
-                acc = next_bank("scalar", [P, 2, 2 * GROUP])
-                for r in range(2):
-                    c0 = a * PASS + (2 * u + r) * P
-                    nc.tensor.matmul_mx(
-                        out=acc[:, r, :], lhsT=w2[:, c0 : c0 + P].bitcast(FP4X4), lhsT_scale=w2_plane[:, c0 : c0 + P],
-                        rhs=v[:, cols].bitcast(FP8X4), rhs_scale=v_plane[:, cols], start=True, stop=True,
-                    )
-                nc.scalar.copy(out=tile[:, u], in_=acc[:].rearrange("p r j -> p j r"))
-            for g in range(2):
-                staged["w2", a, q + g, 1] = tile[:].rearrange("p u j r -> p j u r")[:, g * GROUP : (g + 1) * GROUP]
+        def rows(kind, a, q, groups=1):
+            tile, g = spans[kind, a, q]
+            return tile[:, cols(g, groups), :]
 
-        pieces = {}
+        def stage(name, a, *qs):
+            for q in qs:
+                nc.scalar.copy(out=rows(name, a, q), in_=project(name, a, q, "scalar"))
 
-        def h_piece(name, kb, a, q, groups):
-            tile = early_tile(name, kb, [P, groups * GROUP, PACK], BF16)
-            for g in range(groups):
-                pieces[a, q + g] = (tile, g)
+        def vector_ab(a, *qs):
+            for q in qs:
+                nc.vector.tensor_tensor(rows("w2", a, q), project("w1", a, q, "vector"), rows("w2", a, q), MULT)
 
-        def h_rows(a, q, groups):
-            tile, g = pieces[a, q]
-            return tile[:, g * GROUP : (g + groups) * GROUP, :]
+        def vector_h(a, *qs):
+            for q in qs:
+                nc.vector.tensor_tensor(rows("h", a, q), project("w3", a, q, "vector"), rows("w2", a, q), MULT)
 
-        def in_pairs(rows):
-            return rows.rearrange("p j (u r) -> p j u r", u=2)
+        def gpsimd_ab(a, q, groups):
+            nc.gpsimd.tensor_tensor(rows("w2", a, q, groups), rows("w1", a, q, groups), rows("w2", a, q, groups), MULT)
 
-        def vector_ab(a, q, dst):
-            ab[a, q] = dst
-            nc.vector.tensor_tensor(in_pairs(dst), in_pairs(project("w1", a, q, "vector")), staged["w2", a, q, 1], MULT)
-
-        def vector_h(a, q):
-            nc.vector.tensor_tensor(h_rows(a, q, 1), project("w3", a, q, "vector"), ab[a, q], MULT)
-
-        def gpsimd_h(a, q, groups, both):
-            nc.gpsimd.tensor_tensor(h_rows(a, q, groups), staged["w3", a, q, groups], both, MULT)
+        def gpsimd_h(a, q, groups):
+            nc.gpsimd.tensor_tensor(rows("h", a, q, groups), rows("w3", a, q, groups), rows("w2", a, q, groups), MULT)
 
         hq, hs = {}, {}
 
         def quantise_h(half, a, kb, calls):
-            hq[half, a] = slot_tile("hq_%d_%d" % (half, a), kb, [P, HALF], U32)
-            hs[half, a] = held.tile([P, HALF], U8, name="hs_%d_%d" % (half, a), align_bytes=64)
+            hq[half, a] = placed("hq_%d_%d" % (half, a), kb, [P, HALF], U32)
+            hs[half, a] = kept("hs_%d_%d" % (half, a), [P, HALF], U8)
             for q, groups in calls:
-                cols = slice(q % 4 * GROUP, (q % 4 + groups) * GROUP)
                 nc.vector.quantize_mx(
-                    out=hq[half, a][:, cols].bitcast(FP8X4), scales=hs[half, a][:, cols],
-                    in_=h_rows(a, q, groups).rearrange("p j t -> p (j t)"),
+                    out=hq[half, a][:, cols(q % 4, groups)].bitcast(FP8X4), scales=hs[half, a][:, cols(q % 4, groups)],
+                    in_=rows("h", a, q, groups).rearrange("p j t -> p (j t)"),
                 )
 
-        def scores(half, n, reader, cols=slice(0, HALF)):
-            acc = next_bank(reader, [P, cols.stop - cols.start])
-            rows = slice(n * P, (n + 1) * P)
+        def scores(half, n, reader, part=slice(0, HALF)):
+            acc = next_bank(reader, [P, part.stop - part.start])
             order = (0, 1) if n == 0 else (1, 0)
             for a in order:
                 nc.tensor.matmul_mx(
-                    out=acc[:], lhsT=w4[:, a, rows].bitcast(FP8X4), lhsT_scale=w4_plane[:, a, rows],
-                    rhs=hq[half, a][:, cols].bitcast(FP8X4), rhs_scale=hs[half, a][:, cols],
+                    out=acc[:], lhsT=w4[:, a, cols(n)].bitcast(FP8X4), lhsT_scale=w4_plane[:, a, cols(n)],
+                    rhs=hq[half, a][:, part].bitcast(FP8X4), rhs_scale=hs[half, a][:, part],
                     start=(a == order[0]), stop=(a == order[1]),
                 )
             return acc[:]
 
-        def half_gain(half):
-            return gain[:, half * HALF : (half + 1) * HALF]
+        weighted = {}
 
-        y, weighted = {}, {}
-
-        def stage_scores(half, n, kb):
-            y[half, n] = slot_tile("y_%d_%d" % (half, n), kb, [P, HALF], F32)
-            nc.scalar.copy(out=y[half, n][:], in_=scores(half, n, "scalar"))
-
-        def weigh_on_gpsimd(half, n):
-            weighted[half, n] = held.tile([P, HALF], F32, name="weighted", tag="weighted", bufs=4)
-            nc.gpsimd.tensor_tensor(weighted[half, n][:], y[half, n][:], half_gain(half), MULT)
-
-        def weigh_pair_on_gpsimd(half, n, kb):
-            both = slot_tile("y_%d_%d" % (half, n), kb, [P, 2, HALF], F32)
-            for g in range(2):
-                nc.scalar.copy(out=both[:, g, :], in_=scores(half, n + g, "scalar"))
-            pair = held.tile([P, 2, HALF], F32, name="weighted_pair", tag="weighted_pair", bufs=3)
-            nc.gpsimd.tensor_tensor(pair[:], both[:], half_gain(half).unsqueeze(1).to_broadcast([P, 2, HALF]), MULT)
-            weighted[half, n], weighted[half, n + 1] = pair[:, 0, :], pair[:, 1, :]
+        def weigh_on_gpsimd(half, n0, tiles, kb):
+            y = placed("y_%d_%d" % (half, n0), kb, [P, tiles, HALF], F32)
+            res = kept("weighted_%d_%d" % (half, n0), [P, tiles, HALF], F32)
+            for g in range(tiles):
+                nc.scalar.copy(out=y[:, g, :], in_=scores(half, n0 + g, "scalar"))
+                weighted[half, n0 + g] = res[:, g, :]
+            half_gain = gain[:, half * HALF : (half + 1) * HALF]
+            nc.gpsimd.tensor_tensor(res[:], y[:], half_gain.unsqueeze(1).to_broadcast([P, tiles, HALF]), MULT)
 
         page = {}
 
         def place(half, n):
             if half == 0:
-                page[n] = early_tile("page_%d" % n, (70, 0, 4, 74, 78, 60)[n], [P, S], F32)
+                page[n] = placed("page_%d" % n, (70, 74, 78, 82, 86, 64)[n], [P, S], F32)
             window = page[n][:].indirect(idx2[:, half * HALF // 16 : (half + 1) * HALF // 16])
-            if (half, n) in weighted:
-                nc.vector.tensor_copy(out=window, in_=weighted[half, n][:])
-            else:
-                nc.vector.tensor_tensor(window, y[half, n][:], half_gain(half), MULT)
+            nc.vector.tensor_copy(out=window, in_=weighted[half, n])
 
-        def shared(src, cut):
-            return [("scalar", src[:, :cut], 0, cut), ("gpsimd", src[:, cut:], cut, P)]
-
-        ab_0 = slot_tile("ab_0", 76, [P, S, PACK], F32)
-        for q in (0, 2):
-            stage_b_pair(0, q, 16 + 2 * q)
-        for q in range(8):
-            if q in (1, 3):
-                stage_b_pair(0, q + 3, 22 + 2 * q)
-            vector_ab(0, q, ab_0[:, q * GROUP : (q + 1) * GROUP, :])
-        round_weight("w1", 1, early_tile("grouped_w1_1", 53, [P, PACK * PASS], BF16)[:], shared(raw["w1", 1], SHARE_1))
-        quantise_weight("w3", 0, 28)
-        quantise_weight("w1", 1, 30)
-        for q in (0, 2):
-            stage_b_pair(1, q, 32 + 2 * q)
-        round_weight("w3", 1, early_tile("grouped_w3_1", 53, [P, PACK * PASS], BF16)[:], shared(raw["w3", 1], SHARE_2))
-        h_piece("h_0_0", 61, 0, 0, 2)
-        h_piece("h_1_0", 57, 1, 0, 4)
-        for q in range(2):
-            vector_h(0, q)
-        for q in range(4):
-            vector_ab(1, q, slot_tile("ab_1_%d" % q, 8 + 2 * q, [P, GROUP, PACK], F32)[:])
-        stage("w2", 1, 4, 1, 40)
-        staged["w2", 1, 4, 1] = in_pairs(staged["w2", 1, 4, 1])
-        stage("w3", 0, 2, 2, 42)
-        quantise_weight("w3", 1, 38)
-        h_piece("h_0_2", 55, 0, 2, 2)
-        gpsimd_h(0, 2, 2, ab_0[:, 2 * GROUP : 4 * GROUP, :])
-        ab_1_4 = early_tile("ab_1_4", 46, [P, 4 * GROUP, PACK], F32)
-        vector_ab(1, 4, ab_1_4[:, :GROUP, :])
-        for q in range(4):
-            vector_h(1, q)
-        stage("w3", 0, 5, 3, 46)
-        quantise_h(0, 0, 12, [(0, 2), (2, 2)])
-        quantise_h(0, 1, 14, [(0, 2), (2, 2)])
-        h_piece("h_second", 56, 0, 4, 8)
-        for g in range(4):
-            pieces[1, 4 + g] = pieces[0, 8 + g]
+        span("w2", 0, 0, 2, 60, F32)
+        span("w2", 0, 2, 6, 90, F32)
+        span("w2", 1, 0, 8, 102, F32)
+        stage("w2", 0, 0, 1, 2, 3)
+        round_rows("vector", "w1", 0, 48, w1_0[0], 0)
+        w4_plane = placed("w4_plane", 34.5, [P, PASSES, N], U8)
+        nc.vector.memset(w4_plane[:].bitcast(I32), 0)
+        for r in range(4):
+            nc.sync.dma_start(
+                out=w4_plane[r:P:32].bitcast(I32), in_=w4_scales[:, r:16:4, :].rearrange("a q c -> q a c").bitcast(I32)
+            )
+        round_rows("vector", "w1", 0, 48, w1_0[1], P // 2)
+        quantise_weight("w1", 0)
+        round_rows("vector", "w3", 0, 50, w3_0[0], 0)
+        vector_ab(0, 0, 1, 2, 3)
+        stage("w2", 1, 0)
+        round_rows("gpsimd", "w3", 0, 50, w3_0[1][:, :GPSIMD_ROUNDS_W3_0], P // 2)
+        round_rows("scalar", "w3", 0, 50, w3_0[1][:, GPSIMD_ROUNDS_W3_0:], P // 2 + GPSIMD_ROUNDS_W3_0)
+        stage("w2", 0, 4, 5, 6)
+        stage("w2", 1, 1)
+        quantise_weight("w3", 0)
+        vector_ab(0, 4, 5)
+        round_rows("gpsimd", "w1", 1, 52, w1_1[:, :GPSIMD_ROUNDS_W1_1], 0)
+        round_rows("scalar", "w1", 1, 52, w1_1[:, GPSIMD_ROUNDS_W1_1:], GPSIMD_ROUNDS_W1_1)
+        span("h", 0, 0, 2, 68, BF16)
+        vector_h(0, 0, 1)
+        span("w3", 0, 2, 2, 118, F32)
+        stage("w3", 0, 2)
+        quantise_weight("w1", 1)
+        round_rows("vector", "w3", 1, 60, w3_1[:, :VECTOR_ROUNDS_W3_1], 0)
+        round_rows("scalar", "w3", 1, 60, w3_1[:, VECTOR_ROUNDS_W3_1:], VECTOR_ROUNDS_W3_1)
+        stage("w3", 0, 3)
+        stage("w2", 1, 2, 3)
+        vector_ab(0, 6)
+        quantise_weight("w3", 1)
+        span("h", 0, 2, 2, 62, BF16)
+        gpsimd_h(0, 2, 2)
+        vector_ab(1, 0, 1, 2, 3)
+        span("w3", 1, 0, 1, 123, F32)
+        span("h", 1, 0, 4, 64, BF16)
+        stage("w3", 1, 0)
+        gpsimd_h(1, 0, 1)
+        vector_h(1, 1, 2, 3)
+        stage("w2", 0, 7)
+        stage("w2", 1, 4, 5)
+        span("w3", 0, 4, 4, 126, F32)
+        stage("w3", 0, 4, 5)
+        quantise_h(0, 0, 122, [(0, 2), (2, 2)])
+        quantise_h(0, 1, 124, [(0, 2), (2, 2)])
+        span("h", 0, 4, 4, 64, BF16)
+        span("h", 1, 4, 4, 172, BF16)
+        gpsimd_h(0, 4, 2)
         x = {}
         for n in range(NT):
-            x[n] = early_tile("x_%d" % n, (8, 12, 16, 20, 36, 40)[n], [P, S], F32)
+            x[n] = placed("x_%d" % n, (0, 4, 8, 12, 16.5, 20.5)[n], [P, S], F32)
             nc.sync.dma_start(out=x[n][:], in_=x0[n * P : (n + 1) * P, :])
 
-        weighted[0, 0] = held.tile([P, HALF], F32, name="weighted", tag="weighted", bufs=4)
+        first = placed("y_0_0", 134, [P, HALF], F32)
+        weighted[0, 0] = first[:]
+        vector_ab(0, 7)
         for g in range(2):
-            cols = slice(g * HALF // 2, (g + 1) * HALF // 2)
-            nc.vector.tensor_tensor(weighted[0, 0][:, cols], scores(0, 0, "vector", cols), gain[:, cols], MULT)
-            if g == 0:
-                vector_h(0, 4)
+            part = slice(g * HALF // 2, (g + 1) * HALF // 2)
+            nc.vector.tensor_tensor(first[:, part], scores(0, 0, "vector", part), gain[:, part], MULT)
+            vector_ab(1, 4 + g)
         place(0, 0)
-        gpsimd_h(0, 5, 3, ab_0[:, 5 * GROUP :, :])
-        stage_scores(0, 1, 72)
-        weigh_on_gpsimd(0, 1)
-        weigh_pair_on_gpsimd(0, 2, 52)
-        stage("w2", 1, 5, 3, 66)
-        stage("w1", 1, 5, 3, 46)
-        nc.gpsimd.tensor_tensor(ab_1_4[:, GROUP:, :], staged["w1", 1, 5, 3], staged["w2", 1, 5, 3], MULT)
-        weigh_pair_on_gpsimd(0, 4, 62)
+        weigh_on_gpsimd(0, 1, 1, 136)
+        weigh_on_gpsimd(0, 2, 2, 138)
+        stage("w3", 0, 6, 7)
+        gpsimd_h(0, 6, 2)
+        span("w1", 1, 6, 2, 142, F32)
+        stage("w2", 1, 6, 7)
+        stage("w1", 1, 6, 7)
+        gpsimd_ab(1, 6, 2)
+        weigh_on_gpsimd(0, 4, 2, 146)
+        span("w3", 1, 4, 4, 150, F32)
+        stage("w3", 1, 4, 5, 6, 7)
+        gpsimd_h(1, 4, 4)
         for n in range(1, NT - 1):
             place(0, n)
-        stage("w3", 1, 4, 4, 54)
-        gpsimd_h(1, 4, 4, ab_1_4[:])
-        quantise_h(1, 0, 55, [(4, 4)])
-        quantise_h(1, 1, 57, [(4, 4)])
+        quantise_h(1, 0, 150, [(4, 4)])
+        quantise_h(1, 1, 152, [(4, 4)])
         place(0, NT - 1)
-        stage_scores(1, 0, 42)
-        weigh_on_gpsimd(1, 0)
-        weigh_pair_on_gpsimd(1, 1, 18)
-        weigh_pair_on_gpsimd(1, 3, 26)
-        stage_scores(1, 5, 22)
-        weigh_on_gpsimd(1, 5)
+        weigh_on_gpsimd(1, 0, 1, 158)
+        weigh_on_gpsimd(1, 1, 2, 160)
+        weigh_on_gpsimd(1, 3, 2, 164)
+        weigh_on_gpsimd(1, 5, 1, 168)
         for n in range(NT):
             place(1, n)
         for n in range(NT - 1):
-            rows = slice(n * P, (n + 1) * P)
-            factor = slots.tile([P, S], F32, name="factor", tag="factor", bufs=2, align_bytes=64, offset=24 * KB)
+            factor = space.tile([P, S], F32, name="factor", tag="factor", bufs=2, align_bytes=64, offset=164 * KB)
             cuts = (0, S) if n < NT - 2 else (0, HALF, GPSIMD_CLOSES)
             for c0, c1 in zip(cuts, cuts[1:]):
                 nc.scalar.activation(factor[:, c0:c1], page[n][:, c0:c1], COPY, bias=1.0, scale=1.0)
                 nc.gpsimd.tensor_tensor(x[n][:, c0:c1], factor[:, c0:c1], x[n][:, c0:c1], MULT)
-                nc.sync.dma_start(out=out[rows, c0:c1], in_=x[n][:, c0:c1])
-        closing = slots.tile([P, 2 * S - GPSIMD_CLOSES], F32, name="closing", align_bytes=64, offset=24 * KB)
+                nc.sync.dma_start(out=out[cols(n), c0:c1], in_=x[n][:, c0:c1])
+        closing = placed("closing", 166, [P, 2 * S - GPSIMD_CLOSES], F32)
         done = 0
         for n, c0, c1 in ((NT - 2, GPSIMD_CLOSES, S), (NT - 1, 0, HALF), (NT - 1, HALF, S - GROUP), (NT - 1, S - GROUP, S)):
             res = closing[:, done : done + c1 - c0]
             done = done + c1 - c0
             nc.vector.scalar_tensor_tensor(res, page[n][:, c0:c1], 1.0, x[n][:, c0:c1], ADD, MULT)
-            nc.sync.dma_start(out=out[n * P : (n + 1) * P, c0:c1], in_=res)
+            nc.sync.dma_start(out=out[cols(n), c0:c1], in_=res)

@@ -25,10 +25,11 @@ GROUP = 128
 HALF = S // 2
 NT = N // P
 KB = 1024
+SCALAR_ROUNDS_W1_0 = 44
 GPSIMD_ROUNDS_W3_0 = 24
 GPSIMD_ROUNDS_W1_1 = 44
 VECTOR_ROUNDS_W3_1 = 72
-GPSIMD_CLOSES = 896
+GPSIMD_CLOSES = 768
 
 
 def tile_list_marker_triple_interaction_kernel(
@@ -221,15 +222,16 @@ def tile_list_marker_triple_interaction_kernel(
         span("w2", 0, 0, 2, 60, F32)
         span("w2", 0, 2, 6, 90, F32)
         span("w2", 1, 0, 8, 102, F32)
+        round_rows("scalar", "w1", 0, 48, w1_0[0][:, :SCALAR_ROUNDS_W1_0], 0)
+        round_rows("gpsimd", "w1", 0, 48, w1_0[0][:, SCALAR_ROUNDS_W1_0:], SCALAR_ROUNDS_W1_0)
         stage("w2", 0, 0, 1, 2, 3)
-        round_rows("vector", "w1", 0, 48, w1_0[0], 0)
+        round_rows("vector", "w1", 0, 48, w1_0[1], P // 2)
         w4_plane = placed("w4_plane", 34.5, [P, PASSES, N], U8)
         nc.vector.memset(w4_plane[:].bitcast(I32), 0)
         for r in range(4):
             nc.sync.dma_start(
                 out=w4_plane[r:P:32].bitcast(I32), in_=w4_scales[:, r:16:4, :].rearrange("a q c -> q a c").bitcast(I32)
             )
-        round_rows("vector", "w1", 0, 48, w1_0[1], P // 2)
         quantise_weight("w1", 0)
         round_rows("vector", "w3", 0, 50, w3_0[0], 0)
         vector_ab(0, 0, 1, 2, 3)
@@ -315,7 +317,7 @@ def tile_list_marker_triple_interaction_kernel(
                 nc.sync.dma_start(out=out[cols(n), c0:c1], in_=x[n][:, c0:c1])
         closing = placed("closing", 166, [P, 2 * S - GPSIMD_CLOSES], F32)
         done = 0
-        for n, c0, c1 in ((NT - 2, GPSIMD_CLOSES, S), (NT - 1, 0, HALF), (NT - 1, HALF, S - GROUP), (NT - 1, S - GROUP, S)):
+        for n, c0, c1 in ((NT - 2, GPSIMD_CLOSES, S), (NT - 1, 0, 256), (NT - 1, 256, 640), (NT - 1, 640, S)):
             res = closing[:, done : done + c1 - c0]
             done = done + c1 - c0
             nc.vector.scalar_tensor_tensor(res, page[n][:, c0:c1], 1.0, x[n][:, c0:c1], ADD, MULT)

@@ -25,6 +25,7 @@ GROUP = 128
 HALF = S // 2
 NT = N // P
 KB = 1024
+TABLE_AHEAD = 768
 SCALAR_ROUNDS_W1_0 = 44
 GPSIMD_ROUNDS_W3_0 = 24
 GPSIMD_ROUNDS_W1_1 = 44
@@ -52,11 +53,11 @@ def tile_list_marker_triple_interaction_kernel(
 
         idx = held.tile([P, S // 16], U16, name="idx")
         idx2 = held.tile([P, S // 16], U16, name="idx2")
-        tab_plane = placed("tab_plane", 44, [P, T], U8)
+        tab_plane = placed("tab_plane", 186, [P, T], U8)
         w2_plane_raw = kept("w2_plane_raw", [P, H], U8)
         nc.vector.memset(w2_plane_raw[:].bitcast(I32), 0)
         nc.vector.memset(tab_plane[:].bitcast(I32), 0)
-        w2_raw = placed("w2_raw", 11, [P, H], U16)
+        w2_raw = placed("w2_raw", 15, [P, H], U16)
         tab = placed("tab", 24, [P, T], U32)
         tab_rows = tab_words[0].rearrange("p t i -> p (t i)").bitcast(I32)
 
@@ -64,9 +65,9 @@ def tile_list_marker_triple_interaction_kernel(
         nc.sync.dma_start(idx2[:], offs2)
         nc.sync.dma_start(out=w2_raw[:].bitcast(I32), in_=w2_words[0].bitcast(I32))
         nc.sync.dma_start(out=w2_plane_raw[0:P:8].bitcast(I32), in_=w2_scales[0].bitcast(I32))
+        nc.sync.dma_start(out=tab[:, :TABLE_AHEAD].bitcast(I32), in_=tab_rows[:, :TABLE_AHEAD])
         nc.sync.dma_start(out=tab_plane[0:P:8].bitcast(I32), in_=tab_scales[0].bitcast(I32))
-        nc.sync.dma_start(out=tab[:, : T // 2].bitcast(I32), in_=tab_rows[:, : T // 2])
-        nc.sync.dma_start(out=tab[:, T // 2 :].bitcast(I32), in_=tab_rows[:, T // 2 :])
+        nc.sync.dma_start(out=tab[:, TABLE_AHEAD:].bitcast(I32), in_=tab_rows[:, TABLE_AHEAD:])
 
         def load_weight(name, w, first, width, kb):
             tile = placed("raw_%s_%d" % (name, first), kb, [P, PACK, width], F32)
@@ -85,7 +86,7 @@ def tile_list_marker_triple_interaction_kernel(
         nc.vector.tensor_copy(out=v_plane.bitcast(I32), in_=picked_plane[:].bitcast(I32))
         for r in range(1, 4):
             nc.sync.dma_start(out=both_planes[r:P:32].bitcast(I32), in_=both_planes[8 * r : P : 32].bitcast(I32))
-        w2 = placed("w2", 45, [P, H], U16)
+        w2 = placed("w2", 187, [P, H], U16)
         nc.vector.tensor_copy(
             out=w2[:].rearrange("p (a t m) -> p a t m", a=PASSES, t=PACK),
             in_=w2_raw[:].rearrange("p (a m t) -> p a t m", a=PASSES, t=PACK),
@@ -96,7 +97,7 @@ def tile_list_marker_triple_interaction_kernel(
         v = kept("v", [P, S], U32)
         for c0, c1 in ((0, 256), (256, 512), (512, 1024)):
             nc.vector.tensor_copy(out=v[:, c0:c1], in_=tab[:].indirect(idx[:, c0 // 16 : c1 // 16]))
-        w1_1 = load_weight("w1", w1, PASS, PASS, 16.5)
+        w1_1 = load_weight("w1", w1, PASS, PASS, 16)
         w3_1 = load_weight("w3", w3, PASS, PASS, 36)
         w4 = placed("w4", 24.5, [P, PASSES, N], U32)
         nc.sync.dma_start(out=w4[:].bitcast(I32), in_=w4_words.rearrange("a p e i -> p a (e i)").bitcast(I32))
@@ -220,8 +221,10 @@ def tile_list_marker_triple_interaction_kernel(
             nc.vector.tensor_copy(out=window, in_=weighted[half, n])
 
         span("w2", 0, 0, 2, 60, F32)
-        span("w2", 0, 2, 6, 90, F32)
-        span("w2", 1, 0, 8, 102, F32)
+        span("w2", 0, 2, 2, 90, F32)
+        span("w2", 0, 4, 4, 8, F32)
+        span("w2", 1, 0, 2, 102, F32)
+        span("w2", 1, 2, 6, 36, F32)
         round_rows("scalar", "w1", 0, 48, w1_0[0][:, :SCALAR_ROUNDS_W1_0], 0)
         round_rows("gpsimd", "w1", 0, 48, w1_0[0][:, SCALAR_ROUNDS_W1_0:], SCALAR_ROUNDS_W1_0)
         stage("w2", 0, 0, 1, 2, 3)
@@ -264,17 +267,17 @@ def tile_list_marker_triple_interaction_kernel(
         gpsimd_h(1, 0, 1)
         vector_h(1, 1, 2, 3)
         stage("w2", 0, 7)
-        stage("w2", 1, 4, 5)
-        span("w3", 0, 4, 4, 126, F32)
-        stage("w3", 0, 4, 5)
+        stage("w2", 1, 4)
+        span("w3", 0, 4, 3, 126, F32)
+        stage("w3", 0, 4, 5, 6)
         quantise_h(0, 0, 122, [(0, 2), (2, 2)])
         quantise_h(0, 1, 124, [(0, 2), (2, 2)])
         span("h", 0, 4, 4, 64, BF16)
         span("h", 1, 4, 4, 172, BF16)
-        gpsimd_h(0, 4, 2)
+        gpsimd_h(0, 4, 3)
         x = {}
         for n in range(NT):
-            x[n] = placed("x_%d" % n, (0, 4, 8, 12, 16.5, 20.5)[n], [P, S], F32)
+            x[n] = placed("x_%d" % n, (0, 4, 16, 20, 48, 52)[n], [P, S], F32)
             nc.sync.dma_start(out=x[n][:], in_=x0[n * P : (n + 1) * P, :])
 
         first = placed("y_0_0", 134, [P, HALF], F32)
@@ -283,16 +286,16 @@ def tile_list_marker_triple_interaction_kernel(
         for g in range(2):
             part = slice(g * HALF // 2, (g + 1) * HALF // 2)
             nc.vector.tensor_tensor(first[:, part], scores(0, 0, "vector", part), gain[:, part], MULT)
-            vector_ab(1, 4 + g)
+            if g == 0:
+                vector_ab(1, 4)
+        vector_h(0, 7)
         place(0, 0)
         weigh_on_gpsimd(0, 1, 1, 136)
         weigh_on_gpsimd(0, 2, 2, 138)
-        stage("w3", 0, 6, 7)
-        gpsimd_h(0, 6, 2)
-        span("w1", 1, 6, 2, 142, F32)
-        stage("w2", 1, 6, 7)
-        stage("w1", 1, 6, 7)
-        gpsimd_ab(1, 6, 2)
+        span("w1", 1, 5, 3, 176, F32)
+        stage("w2", 1, 5, 6, 7)
+        stage("w1", 1, 5, 6, 7)
+        gpsimd_ab(1, 5, 3)
         weigh_on_gpsimd(0, 4, 2, 146)
         span("w3", 1, 4, 4, 150, F32)
         stage("w3", 1, 4, 5, 6, 7)

@@ -174,10 +174,10 @@ def tile_list_marker_triple_interaction_kernel(
                 nc.vector.tensor_tensor(rows("h", a, q), project("w3", a, q, "vector"), rows("w2", a, q), MULT)
 
         def gpsimd_ab(a, q, groups):
-            nc.gpsimd.tensor_tensor(rows("w2", a, q, groups), rows("w1", a, q, groups), rows("w2", a, q, groups), MULT)
+            nc.gpsimd.tensor_tensor(rows("ab", a, q, groups), rows("w1", a, q, groups), rows("w2", a, q, groups), MULT)
 
-        def gpsimd_h(a, q, groups):
-            nc.gpsimd.tensor_tensor(rows("h", a, q, groups), rows("w3", a, q, groups), rows("w2", a, q, groups), MULT)
+        def gpsimd_h(a, q, groups, both="w2"):
+            nc.gpsimd.tensor_tensor(rows("h", a, q, groups), rows("w3", a, q, groups), rows(both, a, q, groups), MULT)
 
         hq, hs = {}, {}
 
@@ -216,7 +216,7 @@ def tile_list_marker_triple_interaction_kernel(
 
         def place(half, n):
             if half == 0:
-                page[n] = placed("page_%d" % n, (70, 74, 78, 82, 86, 64)[n], [P, S], F32)
+                page[n] = placed("page_%d" % n, (70, 74, 78, 82, 86, 126)[n], [P, S], F32)
             window = page[n][:].indirect(idx2[:, half * HALF // 16 : (half + 1) * HALF // 16])
             nc.vector.tensor_copy(out=window, in_=weighted[half, n])
 
@@ -249,6 +249,8 @@ def tile_list_marker_triple_interaction_kernel(
         round_rows("scalar", "w1", 1, 52, w1_1[:, GPSIMD_ROUNDS_W1_1:], GPSIMD_ROUNDS_W1_1)
         span("h", 0, 0, 2, 68, BF16)
         vector_h(0, 0, 1)
+        span("h", 0, 4, 4, 126, BF16)
+        vector_h(0, 4, 5)
         span("w3", 0, 2, 2, 118, F32)
         stage("w3", 0, 2)
         quantise_weight("w1", 1)
@@ -267,14 +269,14 @@ def tile_list_marker_triple_interaction_kernel(
         gpsimd_h(1, 0, 1)
         vector_h(1, 1, 2, 3)
         stage("w2", 0, 7)
-        stage("w2", 1, 4)
-        span("w3", 0, 4, 3, 126, F32)
-        stage("w3", 0, 4, 5, 6)
+        span("w1", 1, 4, 4, 176, F32)
+        stage("w2", 1, 4, 5)
+        stage("w1", 1, 4, 5)
         quantise_h(0, 0, 122, [(0, 2), (2, 2)])
         quantise_h(0, 1, 124, [(0, 2), (2, 2)])
-        span("h", 0, 4, 4, 64, BF16)
         span("h", 1, 4, 4, 172, BF16)
-        gpsimd_h(0, 4, 3)
+        span("ab", 1, 4, 4, 62, F32)
+        gpsimd_ab(1, 4, 2)
         x = {}
         for n in range(NT):
             x[n] = placed("x_%d" % n, (0, 4, 16, 20, 48, 52)[n], [P, S], F32)
@@ -286,20 +288,20 @@ def tile_list_marker_triple_interaction_kernel(
         for g in range(2):
             part = slice(g * HALF // 2, (g + 1) * HALF // 2)
             nc.vector.tensor_tensor(first[:, part], scores(0, 0, "vector", part), gain[:, part], MULT)
-            if g == 0:
-                vector_ab(1, 4)
-        vector_h(0, 7)
+        vector_h(0, 6)
         place(0, 0)
         weigh_on_gpsimd(0, 1, 1, 136)
         weigh_on_gpsimd(0, 2, 2, 138)
-        span("w1", 1, 5, 3, 176, F32)
-        stage("w2", 1, 5, 6, 7)
-        stage("w1", 1, 5, 6, 7)
-        gpsimd_ab(1, 5, 3)
+        stage("w2", 1, 6, 7)
+        stage("w1", 1, 6, 7)
+        gpsimd_ab(1, 6, 2)
+        span("w3", 0, 7, 1, 130, F32)
+        stage("w3", 0, 7)
+        gpsimd_h(0, 7, 1)
         weigh_on_gpsimd(0, 4, 2, 146)
         span("w3", 1, 4, 4, 150, F32)
         stage("w3", 1, 4, 5, 6, 7)
-        gpsimd_h(1, 4, 4)
+        gpsimd_h(1, 4, 4, "ab")
         for n in range(1, NT - 1):
             place(0, n)
         quantise_h(1, 0, 150, [(4, 4)])

@@ -25,10 +25,8 @@ GROUP = 128
 HALF = S // 2
 NT = N // P
 KB = 1024
-TABLE_AHEAD = 768
-SCALAR_ROUNDS_W1_0 = 44
-GPSIMD_ROUNDS_W3_0 = 24
-GPSIMD_ROUNDS_W1_1 = 44
+GPSIMD_ROUNDS_W3_0 = 28
+GPSIMD_ROUNDS_W1_1 = 60
 VECTOR_ROUNDS_W3_1 = 72
 GPSIMD_CLOSES = 768
 
@@ -65,9 +63,9 @@ def tile_list_marker_triple_interaction_kernel(
         nc.sync.dma_start(idx2[:], offs2)
         nc.sync.dma_start(out=w2_raw[:].bitcast(I32), in_=w2_words[0].bitcast(I32))
         nc.sync.dma_start(out=w2_plane_raw[0:P:8].bitcast(I32), in_=w2_scales[0].bitcast(I32))
-        nc.sync.dma_start(out=tab[:, :TABLE_AHEAD].bitcast(I32), in_=tab_rows[:, :TABLE_AHEAD])
         nc.sync.dma_start(out=tab_plane[0:P:8].bitcast(I32), in_=tab_scales[0].bitcast(I32))
-        nc.sync.dma_start(out=tab[:, TABLE_AHEAD:].bitcast(I32), in_=tab_rows[:, TABLE_AHEAD:])
+        nc.sync.dma_start(out=tab[:, : T // 2].bitcast(I32), in_=tab_rows[:, : T // 2])
+        nc.sync.dma_start(out=tab[:, T // 2 :].bitcast(I32), in_=tab_rows[:, T // 2 :])
 
         def load_weight(name, w, first, width, kb):
             tile = placed("raw_%s_%d" % (name, first), kb, [P, PACK, width], F32)
@@ -114,8 +112,7 @@ def tile_list_marker_triple_interaction_kernel(
             if engine == "vector":
                 nc.vector.tensor_copy(out=dst, in_=src)
             elif engine == "gpsimd":
-                walk = "p m i t -> p t m i"
-                nc.gpsimd.tensor_scalar(dst.rearrange(walk), src.rearrange(walk), 1.0, 0.0, MULT, ADD)
+                nc.gpsimd.tensor_scalar(dst, src, 1.0, 0.0, MULT, ADD)
             else:
                 nc.scalar.copy(out=dst, in_=src)
 
@@ -165,6 +162,19 @@ def tile_list_marker_triple_interaction_kernel(
             for q in qs:
                 nc.scalar.copy(out=rows(name, a, q), in_=project(name, a, q, "scalar"))
 
+        def first_products(q0, kb):
+            b = placed("b_pair_%d" % q0, kb, [P, 2, 2 * GROUP, 2], F32)
+            for u in range(2):
+                acc = next_bank("scalar", [P, 2, 2 * GROUP])
+                for r in range(2):
+                    c0 = (2 * u + r) * P
+                    nc.tensor.matmul_mx(
+                        out=acc[:, r, :], lhsT=w2[:, c0 : c0 + P].bitcast(FP4X4), lhsT_scale=w2_plane[:, c0 : c0 + P],
+                        rhs=v[:, cols(q0, 2)].bitcast(FP8X4), rhs_scale=v_plane[:, cols(q0, 2)], start=True, stop=True,
+                    )
+                nc.scalar.copy(out=b[:, u], in_=acc[:].rearrange("p r j -> p j r"))
+            return [b[:, :, cols(g), :].rearrange("p u j r -> p j u r") for g in range(2)]
+
         def vector_ab(a, *qs):
             for q in qs:
                 nc.vector.tensor_tensor(rows("w2", a, q), project("w1", a, q, "vector"), rows("w2", a, q), MULT)
@@ -203,11 +213,13 @@ def tile_list_marker_triple_interaction_kernel(
 
         weighted = {}
 
-        def weigh_on_gpsimd(half, n0, tiles, kb):
+        def weigh_on_gpsimd(half, n0, tiles, kb, parts=1):
             y = placed("y_%d_%d" % (half, n0), kb, [P, tiles, HALF], F32)
             res = kept("weighted_%d_%d" % (half, n0), [P, tiles, HALF], F32)
             for g in range(tiles):
-                nc.scalar.copy(out=y[:, g, :], in_=scores(half, n0 + g, "scalar"))
+                for u in range(parts):
+                    part = slice(u * HALF // parts, (u + 1) * HALF // parts)
+                    nc.scalar.copy(out=y[:, g, part], in_=scores(half, n0 + g, "scalar", part))
                 weighted[half, n0 + g] = res[:, g, :]
             half_gain = gain[:, half * HALF : (half + 1) * HALF]
             nc.gpsimd.tensor_tensor(res[:], y[:], half_gain.unsqueeze(1).to_broadcast([P, tiles, HALF]), MULT)
@@ -216,7 +228,7 @@ def tile_list_marker_triple_interaction_kernel(
 
         def place(half, n):
             if half == 0:
-                page[n] = placed("page_%d" % n, (70, 74, 78, 82, 86, 126)[n], [P, S], F32)
+                page[n] = placed("page_%d" % n, (72, 76, 80, 84, 94, 20)[n], [P, S], F32)
             window = page[n][:].indirect(idx2[:, half * HALF // 16 : (half + 1) * HALF // 16])
             nc.vector.tensor_copy(out=window, in_=weighted[half, n])
 
@@ -225,9 +237,8 @@ def tile_list_marker_triple_interaction_kernel(
         span("w2", 0, 4, 4, 8, F32)
         span("w2", 1, 0, 2, 102, F32)
         span("w2", 1, 2, 6, 36, F32)
-        round_rows("scalar", "w1", 0, 48, w1_0[0][:, :SCALAR_ROUNDS_W1_0], 0)
-        round_rows("gpsimd", "w1", 0, 48, w1_0[0][:, SCALAR_ROUNDS_W1_0:], SCALAR_ROUNDS_W1_0)
-        stage("w2", 0, 0, 1, 2, 3)
+        round_rows("scalar", "w1", 0, 48, w1_0[0], 0)
+        b_first = first_products(0, 106) + first_products(2, 110)
         round_rows("vector", "w1", 0, 48, w1_0[1], P // 2)
         w4_plane = placed("w4_plane", 34.5, [P, PASSES, N], U8)
         nc.vector.memset(w4_plane[:].bitcast(I32), 0)
@@ -237,30 +248,32 @@ def tile_list_marker_triple_interaction_kernel(
             )
         quantise_weight("w1", 0)
         round_rows("vector", "w3", 0, 50, w3_0[0], 0)
-        vector_ab(0, 0, 1, 2, 3)
+        for q in range(4):
+            in_pairs = "p j (u r) -> p j u r"
+            a_q = project("w1", 0, q, "vector").rearrange(in_pairs, u=2)
+            nc.vector.tensor_tensor(rows("w2", 0, q).rearrange(in_pairs, u=2), a_q, b_first[q], MULT)
         stage("w2", 1, 0)
         round_rows("gpsimd", "w3", 0, 50, w3_0[1][:, :GPSIMD_ROUNDS_W3_0], P // 2)
         round_rows("scalar", "w3", 0, 50, w3_0[1][:, GPSIMD_ROUNDS_W3_0:], P // 2 + GPSIMD_ROUNDS_W3_0)
         stage("w2", 0, 4, 5, 6)
         stage("w2", 1, 1)
         quantise_weight("w3", 0)
-        vector_ab(0, 4, 5)
+        vector_ab(0, 4, 5, 6)
         round_rows("gpsimd", "w1", 1, 52, w1_1[:, :GPSIMD_ROUNDS_W1_1], 0)
         round_rows("scalar", "w1", 1, 52, w1_1[:, GPSIMD_ROUNDS_W1_1:], GPSIMD_ROUNDS_W1_1)
         span("h", 0, 0, 2, 68, BF16)
         vector_h(0, 0, 1)
-        span("h", 0, 4, 4, 126, BF16)
-        vector_h(0, 4, 5)
         span("w3", 0, 2, 2, 118, F32)
         stage("w3", 0, 2)
         quantise_weight("w1", 1)
-        round_rows("vector", "w3", 1, 60, w3_1[:, :VECTOR_ROUNDS_W3_1], 0)
-        round_rows("scalar", "w3", 1, 60, w3_1[:, VECTOR_ROUNDS_W3_1:], VECTOR_ROUNDS_W3_1)
+        round_rows("vector", "w3", 1, 16, w3_1[:, :VECTOR_ROUNDS_W3_1], 0)
+        round_rows("scalar", "w3", 1, 16, w3_1[:, VECTOR_ROUNDS_W3_1:], VECTOR_ROUNDS_W3_1)
         stage("w3", 0, 3)
         stage("w2", 1, 2, 3)
-        vector_ab(0, 6)
+        span("h", 0, 4, 4, 20, BF16)
+        vector_h(0, 4)
         quantise_weight("w3", 1)
-        span("h", 0, 2, 2, 62, BF16)
+        span("h", 0, 2, 2, 16, BF16)
         gpsimd_h(0, 2, 2)
         vector_ab(1, 0, 1, 2, 3)
         span("w3", 1, 0, 1, 123, F32)
@@ -272,19 +285,20 @@ def tile_list_marker_triple_interaction_kernel(
         span("w1", 1, 4, 4, 176, F32)
         stage("w2", 1, 4, 5)
         stage("w1", 1, 4, 5)
+        vector_ab(0, 7)
         quantise_h(0, 0, 122, [(0, 2), (2, 2)])
         quantise_h(0, 1, 124, [(0, 2), (2, 2)])
         span("h", 1, 4, 4, 172, BF16)
-        span("ab", 1, 4, 4, 62, F32)
+        span("ab", 1, 4, 4, 64, F32)
         gpsimd_ab(1, 4, 2)
         x = {}
         for n in range(NT):
-            x[n] = placed("x_%d" % n, (0, 4, 16, 20, 48, 52)[n], [P, S], F32)
+            x[n] = placed("x_%d" % n, (0, 4, 48, 52, 60, 118)[n], [P, S], F32)
             nc.sync.dma_start(out=x[n][:], in_=x0[n * P : (n + 1) * P, :])
 
         first = placed("y_0_0", 134, [P, HALF], F32)
         weighted[0, 0] = first[:]
-        vector_ab(0, 7)
+        vector_h(0, 5)
         for g in range(2):
             part = slice(g * HALF // 2, (g + 1) * HALF // 2)
             nc.vector.tensor_tensor(first[:, part], scores(0, 0, "vector", part), gain[:, part], MULT)
@@ -292,12 +306,13 @@ def tile_list_marker_triple_interaction_kernel(
         place(0, 0)
         weigh_on_gpsimd(0, 1, 1, 136)
         weigh_on_gpsimd(0, 2, 2, 138)
-        stage("w2", 1, 6, 7)
-        stage("w1", 1, 6, 7)
-        gpsimd_ab(1, 6, 2)
-        span("w3", 0, 7, 1, 130, F32)
+        span("w3", 0, 7, 1, 126, F32)
+        stage("w2", 1, 6)
         stage("w3", 0, 7)
         gpsimd_h(0, 7, 1)
+        stage("w2", 1, 7)
+        stage("w1", 1, 6, 7)
+        gpsimd_ab(1, 6, 2)
         weigh_on_gpsimd(0, 4, 2, 146)
         span("w3", 1, 4, 4, 150, F32)
         stage("w3", 1, 4, 5, 6, 7)
@@ -305,9 +320,9 @@ def tile_list_marker_triple_interaction_kernel(
         for n in range(1, NT - 1):
             place(0, n)
         quantise_h(1, 0, 150, [(4, 4)])
-        quantise_h(1, 1, 152, [(4, 4)])
+        quantise_h(1, 1, 152, [(4, 2), (6, 2)])
         place(0, NT - 1)
-        weigh_on_gpsimd(1, 0, 1, 158)
+        weigh_on_gpsimd(1, 0, 1, 158, 2)
         weigh_on_gpsimd(1, 1, 2, 160)
         weigh_on_gpsimd(1, 3, 2, 164)
         weigh_on_gpsimd(1, 5, 1, 168)

from contextlib import ExitStack

import concourse.mybir as mybir

K, T, S, H, N = 512, 4096, 1024, 1024, 768
FLOPS = 2 * (3 * K * H * S + H * N * S)

F32 = mybir.dt.float32
BF16 = mybir.dt.bfloat16
U32 = mybir.dt.uint32
I32 = mybir.dt.int32
U16 = mybir.dt.uint16
U8 = mybir.dt.uint8
FP8X4 = mybir.dt.float8_e4m3fn_x4
FP4X4 = mybir.dt.float4_e2m1fn_x4
MULT = mybir.AluOpType.mult
ADD = mybir.AluOpType.add
COPY = mybir.ActivationFunctionType.Copy

P = 128
PACK = 4
PASS = P * PACK
PASSES = H // PASS
GROUP = 128
HALF = S // 2
NT = N // P
KB = 1024
GPSIMD_ROUNDS_W3_0 = 28
GPSIMD_ROUNDS_W1_1 = 60
VECTOR_ROUNDS_W3_1 = 72
GPSIMD_CLOSES = 768


def tile_list_marker_triple_interaction_kernel(
    tc, tab_words, tab_scales, offs, w1, w2_words, w2_scales, w3, w4_words, w4_scales, offs2, wgo, x0, out
):
    nc = tc.nc
    with ExitStack() as ctx:
        held = ctx.enter_context(tc.tile_pool(name="held", bufs=1))
        space = ctx.enter_context(tc.tile_pool(name="space", bufs=1))
        psum = ctx.enter_context(tc.psum_pool(name="psum", bufs=1))

        def kept(name, shape, dtype):
            return held.tile(shape, dtype, name=name, align_bytes=64)

        def placed(name, kb, shape, dtype):
            return space.tile(shape, dtype, name=name, align_bytes=64, offset=int(kb * KB))

        def cols(q, groups=1):
            return slice(q * GROUP, (q + groups) * GROUP)

        idx = held.tile([P, S // 16], U16, name="idx")
        idx2 = held.tile([P, S // 16], U16, name="idx2")
        tab_plane = placed("tab_plane", 186, [P, T], U8)
        w2_plane_raw = kept("w2_plane_raw", [P, H], U8)
        nc.vector.memset(w2_plane_raw[:].bitcast(I32), 0)
        nc.vector.memset(tab_plane[:].bitcast(I32), 0)
        w2_raw = placed("w2_raw", 15, [P, H], U16)
        tab = placed("tab", 24, [P, T], U32)
        tab_rows = tab_words[0].rearrange("p t i -> p (t i)").bitcast(I32)

        nc.sync.dma_start(idx[:], offs)
        nc.sync.dma_start(idx2[:], offs2)
        nc.sync.dma_start(out=w2_raw[:].bitcast(I32), in_=w2_words[0].bitcast(I32))
        nc.sync.dma_start(out=w2_plane_raw[0:P:8].bitcast(I32), in_=w2_scales[0].bitcast(I32))
        nc.sync.dma_start(out=tab_plane[0:P:8].bitcast(I32), in_=tab_scales[0].bitcast(I32))
        nc.sync.dma_start(out=tab[:, : T // 2].bitcast(I32), in_=tab_rows[:, : T // 2])
        nc.sync.dma_start(out=tab[:, T // 2 :].bitcast(I32), in_=tab_rows[:, T // 2 :])

        def load_weight(name, w, first, width, kb):
            tile = placed("raw_%s_%d" % (name, first), kb, [P, PACK, width], F32)
            nc.sync.dma_start(out=tile[:], in_=w[:, first : first + width].rearrange("(p i) c -> p i c", i=PACK))
            return tile[:].rearrange("p i (m t) -> p m i t", t=PACK)

        w1_0 = [load_weight("w1", w1, 0, PASS // 2, 0)]
        both_planes = kept("both_planes", [P, S + H], U8)
        v_plane, w2_plane = both_planes[:, :S], both_planes[:, S:]
        picked_plane = placed("picked_plane", 7.5, [P, S], U8)
        nc.vector.tensor_copy(
            out=w2_plane.rearrange("p (a t m) -> p a t m", a=PASSES, t=PACK),
            in_=w2_plane_raw[:].rearrange("p (a m t) -> p a t m", a=PASSES, t=PACK),
        )
        nc.vector.tensor_copy(out=picked_plane[:], in_=tab_plane[:].indirect(idx[:]))
        nc.vector.tensor_copy(out=v_plane.bitcast(I32), in_=picked_plane[:].bitcast(I32))
        for r in range(1, 4):
            nc.sync.dma_start(out=both_planes[r:P:32].bitcast(I32), in_=both_planes[8 * r : P : 32].bitcast(I32))
        w2 = placed("w2", 187, [P, H], U16)
        nc.vector.tensor_copy(
            out=w2[:].rearrange("p (a t m) -> p a t m", a=PASSES, t=PACK),
            in_=w2_raw[:].rearrange("p (a m t) -> p a t m", a=PASSES, t=PACK),
        )

        w1_0.append(load_weight("w1", w1, PASS // 2, PASS // 2, 4))
        w3_0 = [load_weight("w3", w3, u * PASS // 2, PASS // 2, 8 + 4 * u) for u in range(2)]
        v = kept("v", [P, S], U32)
        for c0, c1 in ((0, 256), (256, 512), (512, 1024)):
            nc.vector.tensor_copy(out=v[:, c0:c1], in_=tab[:].indirect(idx[:, c0 // 16 : c1 // 16]))
        w1_1 = load_weight("w1", w1, PASS, PASS, 16)
        w3_1 = load_weight("w3", w3, PASS, PASS, 36)
        w4 = placed("w4", 24.5, [P, PASSES, N], U32)
        nc.sync.dma_start(out=w4[:].bitcast(I32), in_=w4_words.rearrange("a p e i -> p a (e i)").bitcast(I32))
        gain = placed("gain", 30.5, [P, S], F32)
        nc.sync.dma_start(out=gain[:], in_=wgo)

        grouped, codes, planes = {}, {}, {}

        def round_rows(engine, name, a, kb, src, m0):
            if (name, a) not in grouped:
                tile = placed("grouped_%s_%d" % (name, a), kb, [P, PACK * PASS], BF16)
                grouped[name, a] = tile[:].rearrange("p (t m i) -> p t m i", t=PACK, i=PACK)
            dst = grouped[name, a].rearrange("p t m i -> p m i t")[:, m0 : m0 + src.shape[1]]
            if engine == "vector":
                nc.vector.tensor_copy(out=dst, in_=src)
            elif engine == "gpsimd":
                nc.gpsimd.tensor_scalar(dst, src, 1.0, 0.0, MULT, ADD)
            else:
                nc.scalar.copy(out=dst, in_=src)

        def quantise_weight(name, a):
            codes[name, a] = kept("codes_%s_%d" % (name, a), [P, PASS], U32)
            planes[name, a] = kept("plane_%s_%d" % (name, a), [P, PASS], U8)
            nc.vector.quantize_mx(
                out=codes[name, a][:].bitcast(FP8X4),
                scales=planes[name, a][:],
                in_=grouped[name, a].rearrange("p t m i -> p (t m i)"),
            )

        turn = {"vector": 0, "scalar": 0}

        def next_bank(reader, shape):
            bank = {"vector": 0, "scalar": 4}[reader] + turn[reader] % 4
            turn[reader] = turn[reader] + 1
            return psum.tile(shape, F32, name="bank_%d" % bank, tag="bank_%d" % bank)

        def project(name, a, q, reader):
            acc = next_bank(reader, [P, PACK, GROUP])
            for t in range(PACK):
                if name == "w2":
                    c0 = a * PASS + t * P
                    lhsT, lhsT_scale = w2[:, c0 : c0 + P].bitcast(FP4X4), w2_plane[:, c0 : c0 + P]
                else:
                    lhsT = codes[name, a][:, t * P : (t + 1) * P].bitcast(FP8X4)
                    lhsT_scale = planes[name, a][:, t * P : (t + 1) * P]
                nc.tensor.matmul_mx(
                    out=acc[:, t, :], lhsT=lhsT, lhsT_scale=lhsT_scale,
                    rhs=v[:, cols(q)].bitcast(FP8X4), rhs_scale=v_plane[:, cols(q)], start=True, stop=True,
                )
            return acc[:].rearrange("p t j -> p j t")

        spans = {}

        def span(kind, a, q0, groups, kb, dtype):
            tile = placed("%s_%d_%d" % (kind, a, q0), kb, [P, groups * GROUP, PACK], dtype)
            for g in range(groups):
                spans[kind, a, q0 + g] = (tile, g)

        def rows(kind, a, q, groups=1):
            tile, g = spans[kind, a, q]
            return tile[:, cols(g, groups), :]

        def stage(name, a, *qs):
            for q in qs:
                nc.scalar.copy(out=rows(name, a, q), in_=project(name, a, q, "scalar"))

        def first_products(q0, kb):
            b = placed("b_pair_%d" % q0, kb, [P, 2, 2 * GROUP, 2], F32)
            for u in range(2):
                acc = next_bank("scalar", [P, 2, 2 * GROUP])
                for r in range(2):
                    c0 = (2 * u + r) * P
                    nc.tensor.matmul_mx(
                        out=acc[:, r, :], lhsT=w2[:, c0 : c0 + P].bitcast(FP4X4), lhsT_scale=w2_plane[:, c0 : c0 + P],
                        rhs=v[:, cols(q0, 2)].bitcast(FP8X4), rhs_scale=v_plane[:, cols(q0, 2)], start=True, stop=True,
                    )
                nc.scalar.copy(out=b[:, u], in_=acc[:].rearrange("p r j -> p j r"))
            return [b[:, :, cols(g), :].rearrange("p u j r -> p j u r") for g in range(2)]

        def vector_ab(a, *qs):
            for q in qs:
                nc.vector.tensor_tensor(rows("w2", a, q), project("w1", a, q, "vector"), rows("w2", a, q), MULT)

        def vector_h(a, *qs):
            for q in qs:
                nc.vector.tensor_tensor(rows("h", a, q), project("w3", a, q, "vector"), rows("w2", a, q), MULT)

        def gpsimd_ab(a, q, groups):
            nc.gpsimd.tensor_tensor(rows("ab", a, q, groups), rows("w1", a, q, groups), rows("w2", a, q, groups), MULT)

        def gpsimd_h(a, q, groups, both="w2"):
            nc.gpsimd.tensor_tensor(rows("h", a, q, groups), rows("w3", a, q, groups), rows(both, a, q, groups), MULT)

        hq, hs = {}, {}

        def quantise_h(half, a, kb, calls):
            hq[half, a] = placed("hq_%d_%d" % (half, a), kb, [P, HALF], U32)
            hs[half, a] = kept("hs_%d_%d" % (half, a), [P, HALF], U8)
            for q, groups in calls:
                nc.vector.quantize_mx(
                    out=hq[half, a][:, cols(q % 4, groups)].bitcast(FP8X4), scales=hs[half, a][:, cols(q % 4, groups)],
                    in_=rows("h", a, q, groups).rearrange("p j t -> p (j t)"),
                )

        def scores(half, n, reader, part=slice(0, HALF)):
            acc = next_bank(reader, [P, part.stop - part.start])
            order = (0, 1) if n == 0 else (1, 0)
            for a in order:
                nc.tensor.matmul_mx(
                    out=acc[:], lhsT=w4[:, a, cols(n)].bitcast(FP8X4), lhsT_scale=w4_plane[:, a, cols(n)],
                    rhs=hq[half, a][:, part].bitcast(FP8X4), rhs_scale=hs[half, a][:, part],
                    start=(a == order[0]), stop=(a == order[1]),
                )
            return acc[:]

        weighted = {}

        def weigh_on_gpsimd(half, n0, tiles, kb, parts=1):
            y = placed("y_%d_%d" % (half, n0), kb, [P, tiles, HALF], F32)
            res = kept("weighted_%d_%d" % (half, n0), [P, tiles, HALF], F32)
            for g in range(tiles):
                for u in range(parts):
                    part = slice(u * HALF // parts, (u + 1) * HALF // parts)
                    nc.scalar.copy(out=y[:, g, part], in_=scores(half, n0 + g, "scalar", part))
                weighted[half, n0 + g] = res[:, g, :]
            half_gain = gain[:, half * HALF : (half + 1) * HALF]
            nc.gpsimd.tensor_tensor(res[:], y[:], half_gain.unsqueeze(1).to_broadcast([P, tiles, HALF]), MULT)

        page = {}

        def place(half, n):
            if half == 0:
                page[n] = placed("page_%d" % n, (72, 76, 80, 84, 94, 20)[n], [P, S], F32)
            window = page[n][:].indirect(idx2[:, half * HALF // 16 : (half + 1) * HALF // 16])
            nc.vector.tensor_copy(out=window, in_=weighted[half, n])

        span("w2", 0, 0, 2, 60, F32)
        span("w2", 0, 2, 2, 90, F32)
        span("w2", 0, 4, 4, 8, F32)
        span("w2", 1, 0, 2, 102, F32)
        span("w2", 1, 2, 6, 36, F32)
        round_rows("scalar", "w1", 0, 48, w1_0[0], 0)
        b_first = first_products(0, 106) + first_products(2, 110)
        round_rows("vector", "w1", 0, 48, w1_0[1], P // 2)
        w4_plane = placed("w4_plane", 34.5, [P, PASSES, N], U8)
        nc.vector.memset(w4_plane[:].bitcast(I32), 0)
        for r in range(4):
            nc.sync.dma_start(
                out=w4_plane[r:P:32].bitcast(I32), in_=w4_scales[:, r:16:4, :].rearrange("a q c -> q a c").bitcast(I32)
            )
        quantise_weight("w1", 0)
        round_rows("vector", "w3", 0, 50, w3_0[0], 0)
        for q in range(4):
            in_pairs = "p j (u r) -> p j u r"
            a_q = project("w1", 0, q, "vector").rearrange(in_pairs, u=2)
            nc.vector.tensor_tensor(rows("w2", 0, q).rearrange(in_pairs, u=2), a_q, b_first[q], MULT)
        stage("w2", 1, 0)
        round_rows("gpsimd", "w3", 0, 50, w3_0[1][:, :GPSIMD_ROUNDS_W3_0], P // 2)
        round_rows("scalar", "w3", 0, 50, w3_0[1][:, GPSIMD_ROUNDS_W3_0:], P // 2 + GPSIMD_ROUNDS_W3_0)
        stage("w2", 0, 4, 5, 6)
        stage("w2", 1, 1)
        quantise_weight("w3", 0)
        vector_ab(0, 4, 5, 6)
        round_rows("gpsimd", "w1", 1, 52, w1_1[:, :GPSIMD_ROUNDS_W1_1], 0)
        round_rows("scalar", "w1", 1, 52, w1_1[:, GPSIMD_ROUNDS_W1_1:], GPSIMD_ROUNDS_W1_1)
        span("h", 0, 0, 2, 68, BF16)
        vector_h(0, 0, 1)
        span("w3", 0, 2, 2, 118, F32)
        stage("w3", 0, 2)
        quantise_weight("w1", 1)
        round_rows("vector", "w3", 1, 16, w3_1[:, :VECTOR_ROUNDS_W3_1], 0)
        round_rows("scalar", "w3", 1, 16, w3_1[:, VECTOR_ROUNDS_W3_1:], VECTOR_ROUNDS_W3_1)
        stage("w3", 0, 3)
        stage("w2", 1, 2, 3)
        span("h", 0, 4, 4, 20, BF16)
        vector_h(0, 4)
        quantise_weight("w3", 1)
        span("h", 0, 2, 2, 16, BF16)
        gpsimd_h(0, 2, 2)
        vector_ab(1, 0, 1, 2, 3)
        span("w3", 1, 0, 1, 123, F32)
        span("h", 1, 0, 4, 64, BF16)
        stage("w3", 1, 0)
        gpsimd_h(1, 0, 1)
        vector_h(1, 1, 2, 3)
        stage("w2", 0, 7)
        span("w1", 1, 4, 4, 176, F32)
        stage("w2", 1, 4, 5)
        stage("w1", 1, 4, 5)
        vector_ab(0, 7)
        quantise_h(0, 0, 122, [(0, 2), (2, 2)])
        quantise_h(0, 1, 124, [(0, 2), (2, 2)])
        span("h", 1, 4, 4, 172, BF16)
        span("ab", 1, 4, 4, 64, F32)
        gpsimd_ab(1, 4, 2)
        x = {}
        for n in range(NT):
            x[n] = placed("x_%d" % n, (0, 4, 48, 52, 60, 118)[n], [P, S], F32)
            nc.sync.dma_start(out=x[n][:], in_=x0[n * P : (n + 1) * P, :])

        first = placed("y_0_0", 134, [P, HALF], F32)
        weighted[0, 0] = first[:]
        vector_h(0, 5)
        for g in range(2):
            part = slice(g * HALF // 2, (g + 1) * HALF // 2)
            nc.vector.tensor_tensor(first[:, part], scores(0, 0, "vector", part), gain[:, part], MULT)
        vector_h(0, 6)
        place(0, 0)
        weigh_on_gpsimd(0, 1, 1, 136)
        weigh_on_gpsimd(0, 2, 2, 138)
        span("w3", 0, 7, 1, 126, F32)
        stage("w2", 1, 6)
        stage("w3", 0, 7)
        gpsimd_h(0, 7, 1)
        stage("w2", 1, 7)
        stage("w1", 1, 6, 7)
        gpsimd_ab(1, 6, 2)
        weigh_on_gpsimd(0, 4, 2, 146)
        span("w3", 1, 4, 4, 150, F32)
        stage("w3", 1, 4, 5, 6, 7)
        gpsimd_h(1, 4, 4, "ab")
        for n in range(1, NT - 1):
            place(0, n)
        quantise_h(1, 0, 150, [(4, 4)])
        quantise_h(1, 1, 152, [(4, 2), (6, 2)])
        place(0, NT - 1)
        weigh_on_gpsimd(1, 0, 1, 158, 2)
        weigh_on_gpsimd(1, 1, 2, 160)
        weigh_on_gpsimd(1, 3, 2, 164)
        weigh_on_gpsimd(1, 5, 1, 168)
        for n in range(NT):
            place(1, n)
        for n in range(NT - 1):
            factor = space.tile([P, S], F32, name="factor", tag="factor", bufs=2, align_bytes=64, offset=164 * KB)
            cuts = (0, S) if n < NT - 2 else (0, HALF, GPSIMD_CLOSES)
            for c0, c1 in zip(cuts, cuts[1:]):
                nc.scalar.activation(factor[:, c0:c1], page[n][:, c0:c1], COPY, bias=1.0, scale=1.0)
                nc.gpsimd.tensor_tensor(x[n][:, c0:c1], factor[:, c0:c1], x[n][:, c0:c1], MULT)
                nc.sync.dma_start(out=out[cols(n), c0:c1], in_=x[n][:, c0:c1])
        closing = placed("closing", 166, [P, 2 * S - GPSIMD_CLOSES], F32)
        done = 0
        for n, c0, c1 in ((NT - 2, GPSIMD_CLOSES, S), (NT - 1, 0, 256), (NT - 1, 256, 640), (NT - 1, 640, S)):
            res = closing[:, done : done + c1 - c0]
            done = done + c1 - c0
            nc.vector.scalar_tensor_tensor(res, page[n][:, c0:c1], 1.0, x[n][:, c0:c1], ADD, MULT)
            nc.sync.dma_start(out=out[cols(n), c0:c1], in_=res)
